import numpy as np
import ml_dtypes


def mxq(x, axis, fmt="e4m3"):
    dtype, down = {"e4m3": (ml_dtypes.float8_e4m3fn, 7), "e5m2": (ml_dtypes.float8_e5m2, 14)}[fmt]
    v = np.moveaxis(np.asarray(x, np.float32).astype(ml_dtypes.bfloat16).astype(np.float64), axis, -1)
    blocks = v.reshape(v.shape[:-1] + (-1, 32))
    amax = np.abs(blocks).max(-1, keepdims=True)
    byte = np.maximum(np.where(amax > 0, np.frexp(amax)[1] - 1 + 127, 0) - down, 1)
    scale = np.exp2(byte - 127.0)
    codes = (blocks / scale).astype(np.float32).astype(dtype).astype(np.float64)
    return np.moveaxis((codes * scale).reshape(v.shape), -1, axis)


WIDE = False


def mx_kscale(k):
    if not WIDE:
        return np.ones(k)
    levels = np.array([10, -10, 5, -5, 0])
    if k % 512:
        return np.exp2(np.random.permutation(np.resize(levels, k // 32))).repeat(32)
    a = np.empty((k // 512, 16))
    for p in range(k // 512):
        a[p, :8] = np.random.permutation(np.resize(levels, 8))
        for g in range(8):
            far = levels[np.abs(levels - a[p, g]) >= 10]
            a[p, g + 8] = far[np.random.randint(len(far))]
    return np.exp2(a.ravel()).repeat(32)


def f64(x):
    return np.asarray(x).astype(np.float64)


def striped(idx):
    return np.tile(idx.reshape(-1, 16).T, (8, 1)).astype(np.uint16)


def unstriped(offs):
    return offs[:16].T.reshape(-1).astype(np.int64)


E2M1 = np.array([0.0, 0.5, 1.0, 1.5, 2.0, 3.0, 4.0, 6.0, -0.0, -0.5, -1.0, -1.5, -2.0, -3.0, -4.0, -6.0])


def pack_weight(w, fmt):
    k, n = w.shape
    w = f64(np.asarray(w, np.float32).astype(ml_dtypes.bfloat16)).reshape(k // 32, 32, n)
    amax = np.abs(w).max(1)
    if fmt == "e4m3":
        byte = np.frexp(amax)[1] - 1 + 127 - 7
    else:
        mant, ex = np.frexp(amax / 6.0)
        byte = np.where(mant > 0.5, ex, ex - 1) + 127
    byte = np.clip(np.where(amax > 0, byte, 1), 1, 254)
    scaled = (w * np.exp2(127.0 - byte)[:, None, :]).reshape(k, n).astype(np.float32)
    by_word = np.ascontiguousarray(scaled.reshape(k // 512, 128, 4, n).transpose(0, 1, 3, 2))
    if fmt == "e4m3":
        words = by_word.astype(ml_dtypes.float8_e4m3fn).view(np.uint8)
    else:
        c = by_word.astype(ml_dtypes.float4_e2m1fn).view(np.uint8) & 0xF
        words = (c[..., 0::2] | (c[..., 1::2] << 4)).reshape(k // 512, 128, 2 * n)
    return np.ascontiguousarray(words), np.ascontiguousarray(byte.astype(np.uint8).reshape(k // 512, 16, n))


def unpack_weight(words, scales, fmt):
    g, _, n = scales.shape
    words = np.ascontiguousarray(words).reshape(g, 128, n, -1)
    if fmt == "e4m3":
        vals = words.view(ml_dtypes.float8_e4m3fn).astype(np.float64)
    else:
        nib = np.empty((g, 128, n, 4), np.uint8)
        nib[..., 0::2] = words & 0xF
        nib[..., 1::2] = words >> 4
        vals = E2M1[nib]
    vals = vals * np.repeat(np.exp2(scales.astype(np.float64) - 127.0), 8, axis=1)[..., None]
    return vals.transpose(0, 1, 3, 2).reshape(g * 512, n)


def relu(v):
    return np.maximum(v, 0.0)


K, T, E, C, H, N = 1024, 2048, 8, 256, 512, 128


def by_expert(wq, xq):
    return np.concatenate([wq[e].T @ xq[:, e * C:(e + 1) * C] for e in range(E)], axis=1)


def setup_inputs():
    n = np.random.standard_normal
    s = mx_kscale(K)[:, None]
    u = mx_kscale(H)
    w1 = [pack_weight(m, "e2m1") for m in n((E, K, H)) / np.sqrt(K) / s[None] * u[None, None, :]]
    w2 = [pack_weight(m, "e2m1") for m in n((E, H, N)) / np.sqrt(H) / u[None, :, None]]
    return {
        "xT": (n((K, T)) * s).astype(np.float32),
        "w1_words": np.stack([m[0] for m in w1]),
        "w1_scales": np.stack([m[1] for m in w1]),
        "w2_words": np.stack([m[0] for m in w2]),
        "w2_scales": np.stack([m[1] for m in w2]),
        "gate": np.tile(np.random.uniform(0.2, 1.0, E * C), (N, 1)).astype(np.float32),
        "offs": striped(np.random.permutation(T)[:E * C]),
        "dst": striped(np.random.permutation(T)[:E * C]),
    }


def reference(xT, w1_words, w1_scales, w2_words, w2_scales, gate, offs, dst):
    idx = unstriped(offs)
    w1 = np.stack([unpack_weight(w1_words[e], w1_scales[e], "e2m1") for e in range(E)])
    w2 = np.stack([unpack_weight(w2_words[e], w2_scales[e], "e2m1") for e in range(E)])
    xq = mxq(f64(xT)[:, idx], 0, "e4m3")
    h = relu(by_expert(w1, xq))
    y = by_expert(w2, mxq(h, 0, "e4m3"))
    out = np.zeros((N, T))
    out[:, unstriped(dst)] = f64(gate) * y
    return out

@@ -1,0 +1,197 @@
+from contextlib import ExitStack
+
+import concourse.mybir as mybir
+from concourse.masks import make_identity
+
+K, T, E, C, H, N = 1024, 2048, 8, 256, 512, 128
+FLOPS = 2 * E * C * (K * H + H * N)
+
+F32 = mybir.dt.float32
+BF16 = mybir.dt.bfloat16
+I32 = mybir.dt.int32
+U32 = mybir.dt.uint32
+U16 = mybir.dt.uint16
+U8 = mybir.dt.uint8
+FP8X4 = mybir.dt.float8_e4m3fn_x4
+FP4X4 = mybir.dt.float4_e2m1fn_x4
+RELU = mybir.ActivationFunctionType.Relu
+MULT = mybir.AluOpType.mult
+
+P = 128
+PASSES = K // 512
+CHUNKS = (
+    ((0, 512, 128), (512, 512, 128), (1024, 512, 128), (1536, 256, 96), (1792, 256, 96)),
+    ((0, 512, 0), (512, 512, 0), (1024, 512, 0), (1536, 256, 0), (1792, 256, 64)),
+)
+GROUPS = (((0, 1024), (1024, 1024)), ((0, 256), (256, 256), (512, 512), (1024, 512), (1536, 512)))
+UNITS = ((0, 256), (256, 256), (512, 256), (768, 256), (1024, 256), (1280, 256), (1536, 256), (1792, 256))
+SCATTERS = ((0, 512), (512, 512), (1024, 256), (1280, 256), (1536, 256), (1792, 256))
+TAGS = {"W0_1": "W1_0", "W1_3": "W1_2", "W1_4": "hg3"}
+YBANK = (1, 1, 2, 3, 1, 2, 2, 3)
+W1_AT = 5
+
+
+def tile_moe_two_mlp_relu_kernel(tc, xT, w1_words, w1_scales, w2_words, w2_scales, gate, offs, dst, out):
+    nc = tc.nc
+    with ExitStack() as ctx:
+        lists = ctx.enter_context(tc.tile_pool(name="lists", bufs=1))
+        keep = ctx.enter_context(tc.tile_pool(name="keep", bufs=1))
+        psum_a = ctx.enter_context(tc.psum_pool(name="psum_a", bufs=4))
+        psum_b = ctx.enter_context(tc.psum_pool(name="psum_b", bufs=1))
+
+        offs_t = lists.tile([P, T // 16], U16, name="offs_t")
+        dst_t = lists.tile([P, T // 16], U16, name="dst_t")
+
+        def tile(name, shape, dtype):
+            return keep.tile(shape, dtype, name=name, tag=TAGS.get(name, name), align_bytes=64)
+
+        words = [tile(f"words{s}", [P, T], U32) for s in range(PASSES)]
+        scales = [tile(f"scales{s}", [P, T], U8) for s in range(PASSES)]
+        w1w = tile("w1w", [P, E * PASSES, 2 * H], U8)
+        w1s = tile("w1s", [P, E * PASSES, H], U8)
+        w2w = tile("w2w", [P, E, 2 * N], U8)
+        w2s = tile("w2s", [P, E, N], U8)
+        gate_t = tile("gate_t", [P, T], F32)
+        out_t = tile("out_t", [P, T], F32)
+        ident = tile("ident", [P, P], F32)
+
+        nc.gpsimd.memset(scales[0][:], 0)
+        nc.gpsimd.memset(w1s[:].rearrange("p a b -> p (a b)").bitcast(I32), 0)
+        nc.gpsimd.memset(w2s[:].rearrange("p a b -> p (a b)").bitcast(I32), 0)
+        nc.gpsimd.memset(scales[1][:], 0)
+        make_identity(nc, ident[:])
+
+        raw, grouped = {}, {}
+
+        def load_x(s, c):
+            c0, w, v = CHUNKS[s][c]
+            raw[s, c] = tile(f"raw{s}_{c}", [P, 4, w], F32)
+            grouped[s, c] = tile(f"grouped{s}_{c}", [P, w, 4], BF16)
+            nc.sync.dma_start(out=raw[s, c][:], in_=xT[512 * s : 512 * s + 512, c0 : c0 + w].rearrange("(p j) w -> p j w", j=4))
+
+        def load_w1(e):
+            nc.sync.dma_start(
+                out=w1w[:, 2 * e : 2 * e + 4, :].bitcast(I32),
+                in_=w1_words[e : e + 2].rearrange("e s p b -> p (e s) b").bitcast(I32),
+            )
+
+        def load_scales(plane, source):
+            rows = source.rearrange("e s (q r) i -> r q (e s) i", r=4)
+            for r in range(4):
+                nc.sync.dma_start(out=plane[r:P:32, :, :].bitcast(I32), in_=rows[r].bitcast(I32))
+
+        for c in range(len(CHUNKS[0])):
+            load_x(0, c)
+            if c == 1:
+                nc.sync.dma_start(offs_t[:], offs)
+        for c in range(len(CHUNKS[1]) + 1):
+            if c == W1_AT:
+                load_scales(w1s, w1_scales)
+                load_w1(0)
+            if c < len(CHUNKS[1]):
+                load_x(1, c)
+        load_w1(2)
+        load_scales(w2s, w2_scales)
+        nc.sync.dma_start(out=w2w[:].bitcast(I32), in_=w2_words.rearrange("e s p b -> p (e s) b").bitcast(I32))
+        nc.sync.dma_start(dst_t[:], dst)
+        nc.sync.dma_start(out=gate_t[:, : T // 2], in_=gate[:, : T // 2])
+        load_w1(4)
+        load_w1(6)
+        nc.sync.dma_start(out=gate_t[:, T // 2 :], in_=gate[:, T // 2 :])
+
+        def cast(engine, s, c, lo, hi):
+            if hi > lo:
+                engine(
+                    grouped[s, c][:, lo:hi, :].rearrange("p (b i) j -> p b j i", i=4),
+                    raw[s, c][:, :, lo:hi].rearrange("p j (b i) -> p b j i", i=4),
+                )
+
+        for s in range(PASSES):
+            for c, (c0, w, v) in enumerate(CHUNKS[s]):
+                cast(nc.vector.tensor_copy, s, c, 0, v)
+                cast(nc.scalar.copy, s, c, v, w)
+                nc.vector.quantize_mx(
+                    out=words[s][:, c0 : c0 + w].bitcast(FP8X4),
+                    scales=scales[s][:, c0 : c0 + w],
+                    in_=grouped[s, c][:].rearrange("p w j -> p (w j)"),
+                )
+
+        slot_words, slot_scales, hq, hqs, ys = {}, {}, {}, {}, {}
+
+        def gather(n):
+            for s in range(PASSES):
+                for g, (lo, w) in enumerate(GROUPS[s]):
+                    if lo == UNITS[n][0]:
+                        index = offs_t[:, lo // 16 : (lo + w) // 16]
+                        slot_words[s, g] = tile(f"W{s}_{g}", [P, w], U32)
+                        slot_scales[s, g] = tile(f"B{s}_{g}", [P, w], U8)
+                        nc.vector.tensor_copy(slot_words[s, g][:], words[s][:].indirect(index))
+                        nc.vector.tensor_copy(slot_scales[s, g][:], scales[s][:].indirect(index))
+
+        def of_slots(tiles, s, lo):
+            for g, (g0, w) in enumerate(GROUPS[s]):
+                if g0 <= lo < g0 + w:
+                    return tiles[s, g][:, lo - g0 : lo - g0 + P]
+
+        def first(n):
+            lo, w = UNITS[n]
+            hs = []
+            for b in range(w // P):
+                e = (lo + P * b) // C
+                acc = psum_a.tile([P, H], F32, name="acc")
+                for s in range(PASSES):
+                    nc.tensor.matmul_mx(
+                        out=acc[:],
+                        lhsT=of_slots(slot_words, s, lo + P * b).bitcast(FP8X4),
+                        lhsT_scale=of_slots(slot_scales, s, lo + P * b),
+                        rhs=w1w[:, 2 * e + s, :].bitcast(FP4X4),
+                        rhs_scale=w1s[:, 2 * e + s, :],
+                        start=(s == 0),
+                        stop=(s == PASSES - 1),
+                    )
+                hs.append(tile(f"hs{n}_{b}", [P, 2, P, 2], BF16))
+                nc.scalar.activation(hs[b][:], acc[:].rearrange("c (p u e) -> c u p e", u=2, e=2), RELU)
+            hg = tile(f"hg{n}", [P, w, 4], BF16)
+            hg_words = hg[:].rearrange("p c t -> p (c t)").bitcast(F32).rearrange("p (c u) -> p c u", u=2)
+            for half in range(w // 256):
+                k = (lo + 256 * half) // 256
+                tp = psum_b.tile([P, 2, 256], F32, name=f"tp{k}", tag=f"bank{k % 4}")
+                for b in range(2):
+                    turned = hs[2 * half + b][:].rearrange("c u p e -> c u (p e)").bitcast(F32)
+                    for u in range(2):
+                        nc.tensor.transpose(tp[:, u, P * b : P * b + P], turned[:, u, :], ident[:])
+                nc.scalar.copy(hg_words[:, 256 * half : 256 * half + 256, :], tp[:].rearrange("p u r -> p r u"))
+            hq[n] = tile(f"hq{n}", [P, w], U32)
+            hqs[n] = tile(f"hqs{n}", [P, w], U8)
+            nc.vector.quantize_mx(out=hq[n][:].bitcast(FP8X4), scales=hqs[n][:], in_=hg[:].rearrange("p c t -> p (c t)"))
+
+        def second(n):
+            lo, w = UNITS[n]
+            y = psum_b.tile([P, 512], F32, name=f"y{n}", tag=f"bank{YBANK[n]}")
+            for b in range(w // C):
+                e = lo // C + b
+                cols = slice(C * b, C * b + C)
+                nc.tensor.matmul_mx(
+                    out=y[:, cols],
+                    lhsT=w2w[:, e, :].bitcast(FP4X4),
+                    lhsT_scale=w2s[:, e, :],
+                    rhs=hq[n][:, cols].bitcast(FP8X4),
+                    rhs_scale=hqs[n][:, cols],
+                    start=True,
+                    stop=True,
+                )
+            for g, (g0, gw) in enumerate(SCATTERS):
+                if g0 <= lo < g0 + gw:
+                    if g not in ys:
+                        ys[g] = tile(f"ys{g}", [P, gw], F32)
+                    nc.scalar.copy(ys[g][:, lo - g0 : lo - g0 + w], y[:, :w])
+
+        for n in range(len(UNITS)):
+            gather(n)
+            first(n)
+            if n >= 1:
+                second(n - 1)
+        second(len(UNITS) - 1)
+        for g, (lo, w) in enumerate(SCATTERS):
+            nc.vector.tensor_tensor(out_t[:].indirect(dst_t[:, lo // 16 : (lo + w) // 16]), ys[g][:], gate_t[:, lo : lo + w], MULT)
+        nc.sync.dma_start(out=out, in_=out_t[:])

@@ -20,15 +20,20 @@ MULT = mybir.AluOpType.mult
 P = 128
 PASSES = K // 512
 CHUNKS = (
-    ((0, 512, 128), (512, 512, 128), (1024, 512, 128), (1536, 256, 96), (1792, 256, 96)),
-    ((0, 512, 0), (512, 512, 0), (1024, 512, 0), (1536, 256, 0), (1792, 256, 64)),
+    ((0, 512, 256), (512, 512, 256), (1024, 512, 256), (1536, 256, 128), (1792, 256, 128)),
+    ((0, 256, 0), (256, 512, 0), (768, 512, 0), (1280, 512, 0), (1792, 256, 0)),
 )
-GROUPS = (((0, 1024), (1024, 1024)), ((0, 256), (256, 256), (512, 512), (1024, 512), (1536, 512)))
-UNITS = ((0, 256), (256, 256), (512, 256), (768, 256), (1024, 256), (1280, 256), (1536, 256), (1792, 256))
-SCATTERS = ((0, 512), (512, 512), (1024, 256), (1280, 256), (1536, 256), (1792, 256))
-TAGS = {"W0_1": "W1_0", "W1_3": "W1_2", "W1_4": "hg3"}
-YBANK = (1, 1, 2, 3, 1, 2, 2, 3)
-W1_AT = 5
+WORDS = (
+    ((0, 1536, None), (1536, 512, "grouped1_4")),
+    ((0, 256, None), (256, 256, None), (512, 256, None), (768, 256, None), (1024, 512, None), (1536, 256, None), (1792, 256, None)),
+)
+BYTES_ = (
+    ((0, 1024, None), (1024, 1024, None)),
+    ((0, 256, None), (256, 256, None), (512, 256, None), (768, 256, None), (1024, 512, None), (1536, 256, None), (1792, 256, None)),
+)
+HALF = E // 2
+AFTER = (3, 3, 4, 5, 6, 7, 7, 7)
+SCATTERS = ((0, 1), (1, 1), (2, 1), (3, 1), (4, 1), (5, 1), (6, 2))
 
 
 def tile_moe_two_mlp_relu_kernel(tc, xT, w1_words, w1_scales, w2_words, w2_scales, gate, offs, dst, out):
@@ -42,23 +47,24 @@ def tile_moe_two_mlp_relu_kernel(tc, xT, w1_words, w1_scales, w2_words, w2_scale
         offs_t = lists.tile([P, T // 16], U16, name="offs_t")
         dst_t = lists.tile([P, T // 16], U16, name="dst_t")
 
-        def tile(name, shape, dtype):
-            return keep.tile(shape, dtype, name=name, tag=TAGS.get(name, name), align_bytes=64)
+        def tile(name, shape, dtype, tag=None):
+            return keep.tile(shape, dtype, name=name, tag=tag or name, align_bytes=64)
 
         words = [tile(f"words{s}", [P, T], U32) for s in range(PASSES)]
         scales = [tile(f"scales{s}", [P, T], U8) for s in range(PASSES)]
         w1w = tile("w1w", [P, E * PASSES, 2 * H], U8)
-        w1s = tile("w1s", [P, E * PASSES, H], U8)
+        w1s = [tile(f"w1s{a}", [P, HALF * PASSES, H], U8) for a in range(2)]
         w2w = tile("w2w", [P, E, 2 * N], U8)
         w2s = tile("w2s", [P, E, N], U8)
         gate_t = tile("gate_t", [P, T], F32)
         out_t = tile("out_t", [P, T], F32)
         ident = tile("ident", [P, P], F32)
 
-        nc.gpsimd.memset(scales[0][:], 0)
-        nc.gpsimd.memset(w1s[:].rearrange("p a b -> p (a b)").bitcast(I32), 0)
-        nc.gpsimd.memset(w2s[:].rearrange("p a b -> p (a b)").bitcast(I32), 0)
-        nc.gpsimd.memset(scales[1][:], 0)
+        nc.vector.memset(w1s[0][:].rearrange("p a b -> p (a b)").bitcast(I32), 0)
+        nc.vector.memset(w2s[:].rearrange("p a b -> p (a b)").bitcast(I32), 0)
+        nc.vector.memset(w1s[1][:].rearrange("p a b -> p (a b)").bitcast(I32), 0)
+        for s in range(PASSES):
+            nc.vector.memset(scales[s][:].bitcast(I32), 0)
         make_identity(nc, ident[:])
 
         raw, grouped = {}, {}
@@ -84,18 +90,17 @@ def tile_moe_two_mlp_relu_kernel(tc, xT, w1_words, w1_scales, w2_words, w2_scale
             load_x(0, c)
             if c == 1:
                 nc.sync.dma_start(offs_t[:], offs)
-        for c in range(len(CHUNKS[1]) + 1):
-            if c == W1_AT:
-                load_scales(w1s, w1_scales)
-                load_w1(0)
-            if c < len(CHUNKS[1]):
-                load_x(1, c)
+        for c in range(len(CHUNKS[1])):
+            load_x(1, c)
+        load_scales(w1s[0], w1_scales[:HALF])
+        load_w1(0)
         load_w1(2)
         load_scales(w2s, w2_scales)
         nc.sync.dma_start(out=w2w[:].bitcast(I32), in_=w2_words.rearrange("e s p b -> p (e s) b").bitcast(I32))
+        load_scales(w1s[1], w1_scales[HALF:])
+        load_w1(4)
         nc.sync.dma_start(dst_t[:], dst)
         nc.sync.dma_start(out=gate_t[:, : T // 2], in_=gate[:, : T // 2])
-        load_w1(4)
         load_w1(6)
         nc.sync.dma_start(out=gate_t[:, T // 2 :], in_=gate[:, T // 2 :])
 
@@ -118,80 +123,67 @@ def tile_moe_two_mlp_relu_kernel(tc, xT, w1_words, w1_scales, w2_words, w2_scale
 
         slot_words, slot_scales, hq, hqs, ys = {}, {}, {}, {}, {}
 
-        def gather(n):
+        def gather(e):
             for s in range(PASSES):
-                for g, (lo, w) in enumerate(GROUPS[s]):
-                    if lo == UNITS[n][0]:
-                        index = offs_t[:, lo // 16 : (lo + w) // 16]
-                        slot_words[s, g] = tile(f"W{s}_{g}", [P, w], U32)
-                        slot_scales[s, g] = tile(f"B{s}_{g}", [P, w], U8)
-                        nc.vector.tensor_copy(slot_words[s, g][:], words[s][:].indirect(index))
-                        nc.vector.tensor_copy(slot_scales[s, g][:], scales[s][:].indirect(index))
+                for kind, groups, tiles, window, dtype in (("W", WORDS, slot_words, words, U32), ("B", BYTES_, slot_scales, scales, U8)):
+                    for lo, w, tag in groups[s]:
+                        if lo == C * e:
+                            piece = tile(f"{kind}{s}_{lo}", [P, w], dtype, tag)
+                            nc.vector.tensor_copy(piece[:], window[s][:].indirect(offs_t[:, lo // 16 : (lo + w) // 16]))
+                            for at in range(0, w, P):
+                                tiles[s, lo + at] = piece[:, at : at + P]
 
-        def of_slots(tiles, s, lo):
-            for g, (g0, w) in enumerate(GROUPS[s]):
-                if g0 <= lo < g0 + w:
-                    return tiles[s, g][:, lo - g0 : lo - g0 + P]
-
-        def first(n):
-            lo, w = UNITS[n]
-            hs = []
-            for b in range(w // P):
-                e = (lo + P * b) // C
+        def first(e):
+            hs = tile(f"hs{e}", [P, 2, 2, P, 2], BF16)
+            for b in range(2):
                 acc = psum_a.tile([P, H], F32, name="acc")
                 for s in range(PASSES):
                     nc.tensor.matmul_mx(
                         out=acc[:],
-                        lhsT=of_slots(slot_words, s, lo + P * b).bitcast(FP8X4),
-                        lhsT_scale=of_slots(slot_scales, s, lo + P * b),
+                        lhsT=slot_words[s, C * e + P * b].bitcast(FP8X4),
+                        lhsT_scale=slot_scales[s, C * e + P * b],
                         rhs=w1w[:, 2 * e + s, :].bitcast(FP4X4),
-                        rhs_scale=w1s[:, 2 * e + s, :],
+                        rhs_scale=w1s[e // HALF][:, 2 * (e % HALF) + s, :],
                         start=(s == 0),
                         stop=(s == PASSES - 1),
                     )
-                hs.append(tile(f"hs{n}_{b}", [P, 2, P, 2], BF16))
-                nc.scalar.activation(hs[b][:], acc[:].rearrange("c (p u e) -> c u p e", u=2, e=2), RELU)
-            hg = tile(f"hg{n}", [P, w, 4], BF16)
+                nc.scalar.activation(hs[:, b], acc[:].rearrange("c (p u e) -> c u p e", u=2, e=2), RELU)
+            hg = tile(f"hg{e}", [P, C, 4], BF16)
             hg_words = hg[:].rearrange("p c t -> p (c t)").bitcast(F32).rearrange("p (c u) -> p c u", u=2)
-            for half in range(w // 256):
-                k = (lo + 256 * half) // 256
-                tp = psum_b.tile([P, 2, 256], F32, name=f"tp{k}", tag=f"bank{k % 4}")
-                for b in range(2):
-                    turned = hs[2 * half + b][:].rearrange("c u p e -> c u (p e)").bitcast(F32)
-                    for u in range(2):
-                        nc.tensor.transpose(tp[:, u, P * b : P * b + P], turned[:, u, :], ident[:])
-                nc.scalar.copy(hg_words[:, 256 * half : 256 * half + 256, :], tp[:].rearrange("p u r -> p r u"))
-            hq[n] = tile(f"hq{n}", [P, w], U32)
-            hqs[n] = tile(f"hqs{n}", [P, w], U8)
-            nc.vector.quantize_mx(out=hq[n][:].bitcast(FP8X4), scales=hqs[n][:], in_=hg[:].rearrange("p c t -> p (c t)"))
+            turned = hs[:].rearrange("c b u p e -> c b u (p e)").bitcast(F32)
+            tp = psum_b.tile([P, 2, C], F32, name=f"tp{e}", tag=f"bank{e % 4}")
+            for b in range(2):
+                for u in range(2):
+                    nc.tensor.transpose(tp[:, u, P * b : P * b + P], turned[:, b, u, :], ident[:])
+            nc.scalar.copy(hg_words, tp[:].rearrange("p u r -> p r u"))
+            hq[e] = tile(f"hq{e}", [P, C], U32)
+            hqs[e] = tile(f"hqs{e}", [P, C], U8)
+            nc.vector.quantize_mx(out=hq[e][:].bitcast(FP8X4), scales=hqs[e][:], in_=hg[:].rearrange("p c t -> p (c t)"))
 
-        def second(n):
-            lo, w = UNITS[n]
-            y = psum_b.tile([P, 512], F32, name=f"y{n}", tag=f"bank{YBANK[n]}")
-            for b in range(w // C):
-                e = lo // C + b
-                cols = slice(C * b, C * b + C)
-                nc.tensor.matmul_mx(
-                    out=y[:, cols],
-                    lhsT=w2w[:, e, :].bitcast(FP4X4),
-                    lhsT_scale=w2s[:, e, :],
-                    rhs=hq[n][:, cols].bitcast(FP8X4),
-                    rhs_scale=hqs[n][:, cols],
-                    start=True,
-                    stop=True,
-                )
-            for g, (g0, gw) in enumerate(SCATTERS):
-                if g0 <= lo < g0 + gw:
-                    if g not in ys:
-                        ys[g] = tile(f"ys{g}", [P, gw], F32)
-                    nc.scalar.copy(ys[g][:, lo - g0 : lo - g0 + w], y[:, :w])
+        def second(e):
+            y = psum_b.tile([P, C], F32, name=f"y{e}", tag=f"bank{AFTER[e] % 4}")
+            nc.tensor.matmul_mx(
+                out=y[:],
+                lhsT=w2w[:, e, :].bitcast(FP4X4),
+                lhsT_scale=w2s[:, e, :],
+                rhs=hq[e][:].bitcast(FP8X4),
+                rhs_scale=hqs[e][:],
+                start=True,
+                stop=True,
+            )
+            for lo, n in SCATTERS:
+                if lo <= e < lo + n:
+                    if e == lo:
+                        ys[lo] = tile(f"ys{lo}", [P, n * C], F32)
+                    nc.scalar.copy(ys[lo][:, (e - lo) * C : (e - lo + 1) * C], y[:])
 
-        for n in range(len(UNITS)):
-            gather(n)
-            first(n)
-            if n >= 1:
-                second(n - 1)
-        second(len(UNITS) - 1)
-        for g, (lo, w) in enumerate(SCATTERS):
-            nc.vector.tensor_tensor(out_t[:].indirect(dst_t[:, lo // 16 : (lo + w) // 16]), ys[g][:], gate_t[:, lo : lo + w], MULT)
+        for e in range(E):
+            gather(e)
+            first(e)
+            for d in range(E):
+                if AFTER[d] == e:
+                    second(d)
+        for e, n in SCATTERS:
+            lo, w = C * e, C * n
+            nc.vector.tensor_tensor(out_t[:].indirect(dst_t[:, lo // 16 : (lo + w) // 16]), ys[e][:], gate_t[:, lo : lo + w], MULT)
         nc.sync.dma_start(out=out, in_=out_t[:])

@@ -24,16 +24,16 @@ CHUNKS = (
     ((0, 256, 0), (256, 512, 0), (768, 512, 0), (1280, 512, 0), (1792, 256, 0)),
 )
 WORDS = (
-    ((0, 1536, None), (1536, 512, "grouped1_4")),
-    ((0, 256, None), (256, 256, None), (512, 256, None), (768, 256, None), (1024, 512, None), (1536, 256, None), (1792, 256, None)),
+    ((0, 1536, None), (1536, 512, "hg0")),
+    ((0, 256, None), (256, 256, None), (512, 256, None), (768, 256, None), (1024, 512, None), (1536, 512, "hg1")),
 )
 BYTES_ = (
     ((0, 1024, None), (1024, 1024, None)),
     ((0, 256, None), (256, 256, None), (512, 256, None), (768, 256, None), (1024, 512, None), (1536, 256, None), (1792, 256, None)),
 )
 HALF = E // 2
-AFTER = (3, 3, 4, 5, 6, 7, 7, 7)
-SCATTERS = ((0, 1), (1, 1), (2, 1), (3, 1), (4, 1), (5, 1), (6, 2))
+SECOND = ((0, 1, 2), (1, 2, 3), (3, 1, 4), (4, 1, 5), (5, 1, 6), (6, 1, 7), (7, 1, 4))
+NB = 4
 
 
 def tile_moe_two_mlp_relu_kernel(tc, xT, w1_words, w1_scales, w2_words, w2_scales, gate, offs, dst, out):
@@ -41,7 +41,7 @@ def tile_moe_two_mlp_relu_kernel(tc, xT, w1_words, w1_scales, w2_words, w2_scale
     with ExitStack() as ctx:
         lists = ctx.enter_context(tc.tile_pool(name="lists", bufs=1))
         keep = ctx.enter_context(tc.tile_pool(name="keep", bufs=1))
-        psum_a = ctx.enter_context(tc.psum_pool(name="psum_a", bufs=4))
+        psum_a = ctx.enter_context(tc.psum_pool(name="psum_a", bufs=8 - NB))
         psum_b = ctx.enter_context(tc.psum_pool(name="psum_b", bufs=1))
 
         offs_t = lists.tile([P, T // 16], U16, name="offs_t")
@@ -151,7 +151,7 @@ def tile_moe_two_mlp_relu_kernel(tc, xT, w1_words, w1_scales, w2_words, w2_scale
             hg = tile(f"hg{e}", [P, C, 4], BF16)
             hg_words = hg[:].rearrange("p c t -> p (c t)").bitcast(F32).rearrange("p (c u) -> p c u", u=2)
             turned = hs[:].rearrange("c b u p e -> c b u (p e)").bitcast(F32)
-            tp = psum_b.tile([P, 2, C], F32, name=f"tp{e}", tag=f"bank{e % 4}")
+            tp = psum_b.tile([P, 2, C], F32, name=f"tp{e}", tag=f"bank{e % NB}")
             for b in range(2):
                 for u in range(2):
                     nc.tensor.transpose(tp[:, u, P * b : P * b + P], turned[:, b, u, :], ident[:])
@@ -160,30 +160,29 @@ def tile_moe_two_mlp_relu_kernel(tc, xT, w1_words, w1_scales, w2_words, w2_scale
             hqs[e] = tile(f"hqs{e}", [P, C], U8)
             nc.vector.quantize_mx(out=hq[e][:].bitcast(FP8X4), scales=hqs[e][:], in_=hg[:].rearrange("p c t -> p (c t)"))
 
-        def second(e):
-            y = psum_b.tile([P, C], F32, name=f"y{e}", tag=f"bank{AFTER[e] % 4}")
-            nc.tensor.matmul_mx(
-                out=y[:],
-                lhsT=w2w[:, e, :].bitcast(FP4X4),
-                lhsT_scale=w2s[:, e, :],
-                rhs=hq[e][:].bitcast(FP8X4),
-                rhs_scale=hqs[e][:],
-                start=True,
-                stop=True,
-            )
-            for lo, n in SCATTERS:
-                if lo <= e < lo + n:
-                    if e == lo:
-                        ys[lo] = tile(f"ys{lo}", [P, n * C], F32)
-                    nc.scalar.copy(ys[lo][:, (e - lo) * C : (e - lo + 1) * C], y[:])
+        def second(lo, n, after):
+            y = psum_b.tile([P, n, C], F32, name=f"y{lo}", tag=f"bank{after % NB}")
+            for b in range(n):
+                e = lo + b
+                nc.tensor.matmul_mx(
+                    out=y[:, b, :],
+                    lhsT=w2w[:, e, :].bitcast(FP4X4),
+                    lhsT_scale=w2s[:, e, :],
+                    rhs=hq[e][:].bitcast(FP8X4),
+                    rhs_scale=hqs[e][:],
+                    start=True,
+                    stop=True,
+                )
+            ys[lo] = tile(f"ys{lo}", [P, n * C], F32)
+            nc.scalar.copy(ys[lo][:], y[:].rearrange("p b c -> p (b c)"))
 
         for e in range(E):
             gather(e)
             first(e)
-            for d in range(E):
-                if AFTER[d] == e:
-                    second(d)
-        for e, n in SCATTERS:
+            for lo, n, after in SECOND:
+                if max(after, lo + n - 1) == e:
+                    second(lo, n, after)
+        for e, n, after in SECOND:
             lo, w = C * e, C * n
             nc.vector.tensor_tensor(out_t[:].indirect(dst_t[:, lo // 16 : (lo + w) // 16]), ys[e][:], gate_t[:, lo : lo + w], MULT)
         nc.sync.dma_start(out=out, in_=out_t[:])

@@ -20,17 +20,20 @@ MULT = mybir.AluOpType.mult
 P = 128
 PASSES = K // 512
 CHUNKS = (
-    ((0, 512, 256), (512, 512, 256), (1024, 512, 256), (1536, 256, 128), (1792, 256, 128)),
-    ((0, 256, 0), (256, 512, 0), (768, 512, 0), (1280, 512, 0), (1792, 256, 0)),
+    (((512, 256), (512, 256)), ((512, 320),), ((256, 160), (256, 160))),
+    (((512, 0),), ((512, 0),), ((512, 0),), ((256, 64), (256, 128))),
 )
 WORDS = (
-    ((0, 1536, None), (1536, 512, "hg0")),
-    ((0, 256, None), (256, 256, None), (512, 256, None), (768, 256, None), (1024, 512, None), (1536, 512, "hg1")),
+    (0, 1, 0, 256, None), (1, 1, 256, 256, None), (2, 1, 512, 256, None), (3, 1, 768, 256, None),
+    (4, 1, 1024, 512, None), (6, 1, 1536, 512, "hg0"),
 )
 BYTES_ = (
-    ((0, 1024, None), (1024, 1024, None)),
-    ((0, 256, None), (256, 256, None), (512, 256, None), (768, 256, None), (1024, 512, None), (1536, 256, None), (1792, 256, None)),
+    (0, 0, 256), (1, 256, 256), (2, 512, 256), (3, 1024, 512), (3, 768, 256), (5, 1536, 512),
 )
+HOLD = {}
+W0 = ((0, 1024), (1024, 1024))
+LATE = 1024
+GATE1 = 5
 HALF = E // 2
 SECOND = ((0, 1, 2), (1, 2, 3), (3, 1, 4), (4, 1, 5), (5, 1, 6), (6, 1, 7), (7, 1, 4))
 NB = 4
@@ -51,35 +54,42 @@ def tile_moe_two_mlp_relu_kernel(tc, xT, w1_words, w1_scales, w2_words, w2_scale
             return keep.tile(shape, dtype, name=name, tag=tag or name, align_bytes=64)
 
         words = [tile(f"words{s}", [P, T], U32) for s in range(PASSES)]
-        scales = [tile(f"scales{s}", [P, T], U8) for s in range(PASSES)]
-        w1w = tile("w1w", [P, E * PASSES, 2 * H], U8)
+        scales = tile("scales", [P, T], U8)
+        w1w, gates = {}, {}
         w1s = [tile(f"w1s{a}", [P, HALF * PASSES, H], U8) for a in range(2)]
         w2w = tile("w2w", [P, E, 2 * N], U8)
         w2s = tile("w2s", [P, E, N], U8)
-        gate_t = tile("gate_t", [P, T], F32)
         out_t = tile("out_t", [P, T], F32)
         ident = tile("ident", [P, P], F32)
 
         nc.vector.memset(w1s[0][:].rearrange("p a b -> p (a b)").bitcast(I32), 0)
         nc.vector.memset(w2s[:].rearrange("p a b -> p (a b)").bitcast(I32), 0)
         nc.vector.memset(w1s[1][:].rearrange("p a b -> p (a b)").bitcast(I32), 0)
-        for s in range(PASSES):
-            nc.vector.memset(scales[s][:].bitcast(I32), 0)
+        nc.vector.memset(scales[:].bitcast(I32), 0)
+        shifted = {}
+        for lo, w in ((0, LATE),) + tuple((lo, w) for at, lo, w in BYTES_ if lo >= LATE):
+            shifted[lo] = tile(f"shifted{lo}", [P, w], U8)
+            nc.vector.memset(shifted[lo][:].bitcast(I32), 0)
         make_identity(nc, ident[:])
 
-        raw, grouped = {}, {}
+        raw = {}
 
         def load_x(s, c):
-            c0, w, v = CHUNKS[s][c]
-            raw[s, c] = tile(f"raw{s}_{c}", [P, 4, w], F32)
-            grouped[s, c] = tile(f"grouped{s}_{c}", [P, w, 4], BF16)
-            nc.sync.dma_start(out=raw[s, c][:], in_=xT[512 * s : 512 * s + 512, c0 : c0 + w].rearrange("(p j) w -> p j w", j=4))
+            c0 = sum(w for chunk in CHUNKS[s][:c] for w, v in chunk)
+            width = sum(w for w, v in CHUNKS[s][c])
+            raw[s, c] = tile(f"raw{s}_{c}", [P, 4, width], F32)
+            nc.sync.dma_start(out=raw[s, c][:], in_=xT[512 * s : 512 * s + 512, c0 : c0 + width].rearrange("(p j) w -> p j w", j=4))
 
-        def load_w1(e):
+        def load_w1(a):
+            w1w[a] = tile(f"w1w{a}", [P, 2 * PASSES, 2 * H], U8, HOLD.get(f"w1w{a}"))
             nc.sync.dma_start(
-                out=w1w[:, 2 * e : 2 * e + 4, :].bitcast(I32),
-                in_=w1_words[e : e + 2].rearrange("e s p b -> p (e s) b").bitcast(I32),
+                out=w1w[a][:].bitcast(I32),
+                in_=w1_words[2 * a : 2 * a + 2].rearrange("e s p b -> p (e s) b").bitcast(I32),
             )
+
+        def load_gate(a):
+            gates[a] = tile(f"gate{a}", [P, T // 2], F32, HOLD.get(f"gate{a}"))
+            nc.sync.dma_start(out=gates[a][:], in_=gate[:, a * T // 2 : (a + 1) * T // 2])
 
         def load_scales(plane, source):
             rows = source.rearrange("e s (q r) i -> r q (e s) i", r=4)
@@ -92,60 +102,85 @@ def tile_moe_two_mlp_relu_kernel(tc, xT, w1_words, w1_scales, w2_words, w2_scale
                 nc.sync.dma_start(offs_t[:], offs)
         for c in range(len(CHUNKS[1])):
             load_x(1, c)
-        load_scales(w1s[0], w1_scales[:HALF])
         load_w1(0)
-        load_w1(2)
-        load_scales(w2s, w2_scales)
-        nc.sync.dma_start(out=w2w[:].bitcast(I32), in_=w2_words.rearrange("e s p b -> p (e s) b").bitcast(I32))
-        load_scales(w1s[1], w1_scales[HALF:])
-        load_w1(4)
-        nc.sync.dma_start(dst_t[:], dst)
-        nc.sync.dma_start(out=gate_t[:, : T // 2], in_=gate[:, : T // 2])
-        load_w1(6)
-        nc.sync.dma_start(out=gate_t[:, T // 2 :], in_=gate[:, T // 2 :])
+        load_scales(w1s[0], w1_scales[:HALF])
 
-        def cast(engine, s, c, lo, hi):
+        def cast(engine, grouped, source, lo, hi):
             if hi > lo:
                 engine(
-                    grouped[s, c][:, lo:hi, :].rearrange("p (b i) j -> p b j i", i=4),
-                    raw[s, c][:, :, lo:hi].rearrange("p j (b i) -> p b j i", i=4),
+                    grouped[:, lo:hi, :].rearrange("p (b i) j -> p b j i", i=4),
+                    source[:, :, lo:hi].rearrange("p j (b i) -> p b j i", i=4),
                 )
 
-        for s in range(PASSES):
-            for c, (c0, w, v) in enumerate(CHUNKS[s]):
-                cast(nc.vector.tensor_copy, s, c, 0, v)
-                cast(nc.scalar.copy, s, c, v, w)
-                nc.vector.quantize_mx(
-                    out=words[s][:, c0 : c0 + w].bitcast(FP8X4),
-                    scales=scales[s][:, c0 : c0 + w],
-                    in_=grouped[s, c][:].rearrange("p w j -> p (w j)"),
-                )
+        def quantise(s):
+            c0 = 0
+            for c, chunk in enumerate(CHUNKS[s]):
+                at = 0
+                for w, v in chunk:
+                    grouped = tile(f"grouped{s}_{c0}", [P, w, 4], BF16)
+                    cast(nc.vector.tensor_copy, grouped, raw[s, c][:, :, at : at + w], 0, v)
+                    cast(nc.scalar.copy, grouped, raw[s, c][:, :, at : at + w], v, w)
+                    nc.vector.quantize_mx(
+                        out=words[s][:, c0 : c0 + w].bitcast(FP8X4),
+                        scales=scales[4 * (1 - s) : P, c0 : c0 + w],
+                        in_=grouped[:].rearrange("p w j -> p (w j)"),
+                    )
+                    at, c0 = at + w, c0 + w
 
         slot_words, slot_scales, hq, hqs, ys = {}, {}, {}, {}, {}
 
+        def gather_words(s, lo, w, tag):
+            piece = tile(f"W{s}_{lo}", [P, w], U32, tag)
+            nc.vector.tensor_copy(piece[:], words[s][:].indirect(offs_t[:, lo // 16 : (lo + w) // 16]))
+            for at in range(0, w, P):
+                slot_words[s, lo + at] = piece[:, at : at + P]
+
+        def gather_bytes(name, lo, w, direct, shift):
+            piece = tile(name, [P, w], U8)
+            nc.vector.tensor_copy(piece[:], scales[:].indirect(offs_t[:, lo // 16 : (lo + w) // 16]))
+            if shift:
+                for r in range(4):
+                    nc.sync.dma_start(out=shifted[lo][r:P:32, :].bitcast(I32), in_=piece[4 + r : P : 32, :].bitcast(I32))
+            for at in range(0, w, P):
+                if direct:
+                    slot_scales[1, lo + at] = piece[:, at : at + P]
+                if shift:
+                    slot_scales[0, lo + at] = shifted[lo][:, at : at + P]
+
+        quantise(0)
+        gather_bytes("early", 0, LATE, False, True)
+        for lo, w in W0:
+            gather_words(0, lo, w, None)
+        load_w1(1)
+        load_scales(w1s[1], w1_scales[HALF:])
+        load_w1(2)
+        nc.sync.dma_start(dst_t[:], dst)
+        load_scales(w2s, w2_scales)
+        nc.sync.dma_start(out=w2w[:].bitcast(I32), in_=w2_words.rearrange("e s p b -> p (e s) b").bitcast(I32))
+        quantise(1)
+
         def gather(e):
-            for s in range(PASSES):
-                for kind, groups, tiles, window, dtype in (("W", WORDS, slot_words, words, U32), ("B", BYTES_, slot_scales, scales, U8)):
-                    for lo, w, tag in groups[s]:
-                        if lo == C * e:
-                            piece = tile(f"{kind}{s}_{lo}", [P, w], dtype, tag)
-                            nc.vector.tensor_copy(piece[:], window[s][:].indirect(offs_t[:, lo // 16 : (lo + w) // 16]))
-                            for at in range(0, w, P):
-                                tiles[s, lo + at] = piece[:, at : at + P]
+            for at, lo, w in BYTES_:
+                if at == e:
+                    gather_bytes(f"B{lo}", lo, w, True, lo >= LATE)
+            for at, s, lo, w, tag in WORDS:
+                if at == e:
+                    gather_words(s, lo, w, tag)
 
         def first(e):
             hs = tile(f"hs{e}", [P, 2, 2, P, 2], BF16)
             for b in range(2):
                 acc = psum_a.tile([P, H], F32, name="acc")
-                for s in range(PASSES):
+                order = (0, 1) if C * e < LATE else (1, 0)
+                for s in order:
                     nc.tensor.matmul_mx(
                         out=acc[:],
                         lhsT=slot_words[s, C * e + P * b].bitcast(FP8X4),
                         lhsT_scale=slot_scales[s, C * e + P * b],
-                        rhs=w1w[:, 2 * e + s, :].bitcast(FP4X4),
+                        rhs=w1w[e // 2][:, 2 * (e % 2) + s, :].bitcast(FP4X4),
                         rhs_scale=w1s[e // HALF][:, 2 * (e % HALF) + s, :],
-                        start=(s == 0),
-                        stop=(s == PASSES - 1),
+                        start=(s == order[0]),
+                        stop=(s == order[1]),
                     )
                 nc.scalar.activation(hs[:, b], acc[:].rearrange("c (p u e) -> c u p e", u=2, e=2), RELU)
             hg = tile(f"hg{e}", [P, C, 4], BF16)
@@ -179,10 +214,16 @@ def tile_moe_two_mlp_relu_kernel(tc, xT, w1_words, w1_scales, w2_words, w2_scale
         for e in range(E):
             gather(e)
             first(e)
+            if e == 0:
+                load_gate(0)
+            if e == 1:
+                load_w1(3)
+            if e == GATE1:
+                load_gate(1)
             for lo, n, after in SECOND:
                 if max(after, lo + n - 1) == e:
                     second(lo, n, after)
         for e, n, after in SECOND:
             lo, w = C * e, C * n
-            nc.vector.tensor_tensor(out_t[:].indirect(dst_t[:, lo // 16 : (lo + w) // 16]), ys[e][:], gate_t[:, lo : lo + w], MULT)
+            nc.vector.tensor_tensor(out_t[:].indirect(dst_t[:, lo // 16 : (lo + w) // 16]), ys[e][:], gates[lo // (T // 2)][:, lo % (T // 2) : lo % (T // 2) + w], MULT)
         nc.sync.dma_start(out=out, in_=out_t[:])

@@ -105,11 +105,11 @@ def tile_moe_two_mlp_relu_kernel(tc, xT, w1_words, w1_scales, w2_words, w2_scale
         load_w1(0)
         load_scales(w1s[0], w1_scales[:HALF])
 
-        def cast(engine, grouped, source, lo, hi):
+        def cast(engine, grouped, source, lo, hi, run):
             if hi > lo:
                 engine(
-                    grouped[:, lo:hi, :].rearrange("p (b i) j -> p b j i", i=4),
-                    source[:, :, lo:hi].rearrange("p j (b i) -> p b j i", i=4),
+                    grouped[:, lo:hi, :].rearrange("p (b i) j -> p b j i", i=run),
+                    source[:, :, lo:hi].rearrange("p j (b i) -> p b j i", i=run),
                 )
 
         def quantise(s):
@@ -118,8 +118,8 @@ def tile_moe_two_mlp_relu_kernel(tc, xT, w1_words, w1_scales, w2_words, w2_scale
                 at = 0
                 for w, v in chunk:
                     grouped = tile(f"grouped{s}_{c0}", [P, w, 4], BF16)
-                    cast(nc.vector.tensor_copy, grouped, raw[s, c][:, :, at : at + w], 0, v)
-                    cast(nc.scalar.copy, grouped, raw[s, c][:, :, at : at + w], v, w)
+                    cast(nc.vector.tensor_copy, grouped, raw[s, c][:, :, at : at + w], 0, v, 4)
+                    cast(nc.scalar.copy, grouped, raw[s, c][:, :, at : at + w], v, w, 2)
                     nc.vector.quantize_mx(
                         out=words[s][:, c0 : c0 + w].bitcast(FP8X4),
                         scales=scales[4 * (1 - s) : P, c0 : c0 + w],

@@ -20,8 +20,8 @@ MULT = mybir.AluOpType.mult
 P = 128
 PASSES = K // 512
 CHUNKS = (
-    (((512, 256), (512, 256)), ((512, 320),), ((256, 160), (256, 160))),
-    (((512, 0),), ((512, 0),), ((512, 0),), ((256, 64), (256, 128))),
+    (((512, 256),), ((512, 256),), ((512, 256),), ((256, 160), (256, 160))),
+    (((512, 0),), ((512, 0),), ((512, 0),), ((256, 128), (256, 128))),
 )
 WORDS = (
     (0, 1, 0, 256, None), (1, 1, 256, 256, None), (2, 1, 512, 256, None), (3, 1, 768, 256, None),
@@ -33,10 +33,16 @@ BYTES_ = (
 HOLD = {}
 W0 = ((0, 1024), (1024, 1024))
 LATE = 1024
+ON_SCALAR = ()
 GATE1 = 5
-HALF = E // 2
-SECOND = ((0, 1, 2), (1, 2, 3), (3, 1, 4), (4, 1, 5), (5, 1, 6), (6, 1, 7), (7, 1, 4))
+SPLIT = (0, 2, 8)
+FIRST0 = 1024
+LOADS = ("x00 x01 offs x02 x03 x10 x11 x12 dst s0 x13 w0", "s1 w1 w2 t u g0 w3")
+SECOND = ((0, 1, 2), (1, 1, 2), (2, 1, 3), (3, 1, 4), (4, 1, 5), (5, 1, 6), (6, 2, 7))
 NB = 4
+HS = 2
+GS = (0, 1024, 2048)
+BEHIND = {}
 
 
 def tile_moe_two_mlp_relu_kernel(tc, xT, w1_words, w1_scales, w2_words, w2_scales, gate, offs, dst, out):
@@ -56,18 +62,17 @@ def tile_moe_two_mlp_relu_kernel(tc, xT, w1_words, w1_scales, w2_words, w2_scale
         words = [tile(f"words{s}", [P, T], U32) for s in range(PASSES)]
         scales = tile("scales", [P, T], U8)
         w1w, gates = {}, {}
-        w1s = [tile(f"w1s{a}", [P, HALF * PASSES, H], U8) for a in range(2)]
+        w1s = [tile(f"w1s{a}", [P, (SPLIT[a + 1] - SPLIT[a]) * PASSES, H], U8) for a in range(len(SPLIT) - 1)]
         w2w = tile("w2w", [P, E, 2 * N], U8)
         w2s = tile("w2s", [P, E, N], U8)
         out_t = tile("out_t", [P, T], F32)
         ident = tile("ident", [P, P], F32)
 
-        nc.vector.memset(w1s[0][:].rearrange("p a b -> p (a b)").bitcast(I32), 0)
-        nc.vector.memset(w2s[:].rearrange("p a b -> p (a b)").bitcast(I32), 0)
-        nc.vector.memset(w1s[1][:].rearrange("p a b -> p (a b)").bitcast(I32), 0)
+        for plane in w1s + [w2s]:
+            nc.vector.memset(plane[:].rearrange("p a b -> p (a b)").bitcast(I32), 0)
         nc.vector.memset(scales[:].bitcast(I32), 0)
         shifted = {}
-        for lo, w in ((0, LATE),) + tuple((lo, w) for at, lo, w in BYTES_ if lo >= LATE):
+        for lo, w in ((0, LATE),)[: min(LATE, 1)] + tuple((lo, w) for at, lo, w in BYTES_ if lo >= LATE):
             shifted[lo] = tile(f"shifted{lo}", [P, w], U8)
             nc.vector.memset(shifted[lo][:].bitcast(I32), 0)
         make_identity(nc, ident[:])
@@ -88,22 +93,36 @@ def tile_moe_two_mlp_relu_kernel(tc, xT, w1_words, w1_scales, w2_words, w2_scale
             )
 
         def load_gate(a):
-            gates[a] = tile(f"gate{a}", [P, T // 2], F32, HOLD.get(f"gate{a}"))
-            nc.sync.dma_start(out=gates[a][:], in_=gate[:, a * T // 2 : (a + 1) * T // 2])
+            lo, hi = GS[a], GS[a + 1]
+            gates[a] = tile(f"gate{a}", [P, hi - lo], F32, HOLD.get(f"gate{a}"))
+            nc.sync.dma_start(out=gates[a][:], in_=gate[:, lo:hi])
 
         def load_scales(plane, source):
             rows = source.rearrange("e s (q r) i -> r q (e s) i", r=4)
             for r in range(4):
                 nc.sync.dma_start(out=plane[r:P:32, :, :].bitcast(I32), in_=rows[r].bitcast(I32))
 
-        for c in range(len(CHUNKS[0])):
-            load_x(0, c)
-            if c == 1:
+        def load(name):
+            if name == "offs":
                 nc.sync.dma_start(offs_t[:], offs)
-        for c in range(len(CHUNKS[1])):
-            load_x(1, c)
-        load_w1(0)
-        load_scales(w1s[0], w1_scales[:HALF])
+            if name == "dst":
+                nc.sync.dma_start(dst_t[:], dst)
+            if name[0] == "x":
+                load_x(int(name[1]), int(name[2]))
+            if name[0] == "w":
+                load_w1(int(name[1]))
+            if name[0] == "s":
+                a = int(name[1])
+                load_scales(w1s[a], w1_scales[SPLIT[a] : SPLIT[a + 1]])
+            if name == "t":
+                load_scales(w2s, w2_scales)
+            if name == "u":
+                nc.sync.dma_start(out=w2w[:].bitcast(I32), in_=w2_words.rearrange("e s p b -> p (e s) b").bitcast(I32))
+            if name[0] == "g":
+                load_gate(int(name[1]))
+
+        for name in LOADS[0].split():
+            load(name)
 
         def cast(engine, grouped, source, lo, hi, run):
             if hi > lo:
@@ -118,7 +137,7 @@ def tile_moe_two_mlp_relu_kernel(tc, xT, w1_words, w1_scales, w2_words, w2_scale
                 at = 0
                 for w, v in chunk:
                     grouped = tile(f"grouped{s}_{c0}", [P, w, 4], BF16)
-                    cast(nc.vector.tensor_copy, grouped, raw[s, c][:, :, at : at + w], 0, v, 4)
+                    cast(nc.vector.tensor_copy, grouped, raw[s, c][:, :, at : at + w], 0, v, 2)
                     cast(nc.scalar.copy, grouped, raw[s, c][:, :, at : at + w], v, w, 2)
                     nc.vector.quantize_mx(
                         out=words[s][:, c0 : c0 + w].bitcast(FP8X4),
@@ -127,7 +146,7 @@ def tile_moe_two_mlp_relu_kernel(tc, xT, w1_words, w1_scales, w2_words, w2_scale
                     )
                     at, c0 = at + w, c0 + w
 
-        slot_words, slot_scales, hq, hqs, ys = {}, {}, {}, {}, {}
+        slot_words, slot_scales, hs, hq, hqs, ys = {}, {}, {}, {}, {}, {}
 
         def gather_words(s, lo, w, tag):
             piece = tile(f"W{s}_{lo}", [P, w], U32, tag)
@@ -140,7 +159,7 @@ def tile_moe_two_mlp_relu_kernel(tc, xT, w1_words, w1_scales, w2_words, w2_scale
             nc.vector.tensor_copy(piece[:], scales[:].indirect(offs_t[:, lo // 16 : (lo + w) // 16]))
             if shift:
                 for r in range(4):
-                    nc.sync.dma_start(out=shifted[lo][r:P:32, :].bitcast(I32), in_=piece[4 + r : P : 32, :].bitcast(I32))
+                    (nc.scalar if lo in ON_SCALAR else nc.sync).dma_start(out=shifted[lo][r:P:32, :].bitcast(I32), in_=piece[4 + r : P : 32, :].bitcast(I32))
             for at in range(0, w, P):
                 if direct:
                     slot_scales[1, lo + at] = piece[:, at : at + P]
@@ -148,15 +167,12 @@ def tile_moe_two_mlp_relu_kernel(tc, xT, w1_words, w1_scales, w2_words, w2_scale
                     slot_scales[0, lo + at] = shifted[lo][:, at : at + P]
 
         quantise(0)
-        gather_bytes("early", 0, LATE, False, True)
+        if LATE:
+            gather_bytes("early", 0, LATE, False, True)
         for lo, w in W0:
             gather_words(0, lo, w, None)
-        load_w1(1)
-        load_scales(w1s[1], w1_scales[HALF:])
-        load_w1(2)
-        nc.sync.dma_start(dst_t[:], dst)
-        load_scales(w2s, w2_scales)
-        nc.sync.dma_start(out=w2w[:].bitcast(I32), in_=w2_words.rearrange("e s p b -> p (e s) b").bitcast(I32))
+        for name in LOADS[1].split():
+            load(name)
         quantise(1)
 
         def gather(e):
@@ -168,30 +184,33 @@ def tile_moe_two_mlp_relu_kernel(tc, xT, w1_words, w1_scales, w2_words, w2_scale
                     gather_words(s, lo, w, tag)
 
         def first(e):
-            hs = tile(f"hs{e}", [P, 2, 2, P, 2], BF16)
+            part = sum(e >= lo for lo in SPLIT[1:])
+            hs[e] = tile(f"hs{e}", [P, 2, 2, P, 2], BF16, f"hs{e % HS}")
             for b in range(2):
                 acc = psum_a.tile([P, H], F32, name="acc")
-                order = (0, 1) if C * e < LATE else (1, 0)
+                order = (0, 1) if C * e < FIRST0 else (1, 0)
                 for s in order:
                     nc.tensor.matmul_mx(
                         out=acc[:],
                         lhsT=slot_words[s, C * e + P * b].bitcast(FP8X4),
                         lhsT_scale=slot_scales[s, C * e + P * b],
                         rhs=w1w[e // 2][:, 2 * (e % 2) + s, :].bitcast(FP4X4),
-                        rhs_scale=w1s[e // HALF][:, 2 * (e % HALF) + s, :],
+                        rhs_scale=w1s[part][:, 2 * (e - SPLIT[part]) + s, :],
                         start=(s == order[0]),
                         stop=(s == order[1]),
                     )
-                nc.scalar.activation(hs[:, b], acc[:].rearrange("c (p u e) -> c u p e", u=2, e=2), RELU)
+                nc.scalar.activation(hs[e][:, b], acc[:].rearrange("c (p u e) -> c u p e", u=2, e=2), RELU)
+
+        def turn(e):
             hg = tile(f"hg{e}", [P, C, 4], BF16)
             hg_words = hg[:].rearrange("p c t -> p (c t)").bitcast(F32).rearrange("p (c u) -> p c u", u=2)
-            turned = hs[:].rearrange("c b u p e -> c b u (p e)").bitcast(F32)
+            turned = hs[e][:].rearrange("c b u p e -> c b u (p e)").bitcast(F32)
             tp = psum_b.tile([P, 2, C], F32, name=f"tp{e}", tag=f"bank{e % NB}")
             for b in range(2):
                 for u in range(2):
                     nc.tensor.transpose(tp[:, u, P * b : P * b + P], turned[:, b, u, :], ident[:])
             nc.scalar.copy(hg_words, tp[:].rearrange("p u r -> p r u"))
-            hq[e] = tile(f"hq{e}", [P, C], U32)
+            hq[e] = tile(f"hq{e}", [P, C], U32, BEHIND.get(e))
             hqs[e] = tile(f"hqs{e}", [P, C], U8)
             nc.vector.quantize_mx(out=hq[e][:].bitcast(FP8X4), scales=hqs[e][:], in_=hg[:].rearrange("p c t -> p (c t)"))
 
@@ -210,20 +229,22 @@ def tile_moe_two_mlp_relu_kernel(tc, xT, w1_words, w1_scales, w2_words, w2_scale
                 )
             ys[lo] = tile(f"ys{lo}", [P, n * C], F32)
             nc.scalar.copy(ys[lo][:], y[:].rearrange("p b c -> p (b c)"))
+            first_slot, w = C * lo, C * n
+            half = int(first_slot >= GS[1])
+            at = first_slot - GS[half]
+            assert at + w <= GS[half + 1] - GS[half]
+            index = dst_t[:, first_slot // 16 : (first_slot + w) // 16]
+            nc.vector.tensor_tensor(out_t[:].indirect(index), ys[lo][:], gates[half][:, at : at + w], MULT)
 
-        for e in range(E):
-            gather(e)
-            first(e)
-            if e == 0:
-                load_gate(0)
-            if e == 1:
-                load_w1(3)
+        for e in range(E + 1):
+            if e < E:
+                gather(e)
+                first(e)
             if e == GATE1:
                 load_gate(1)
-            for lo, n, after in SECOND:
-                if max(after, lo + n - 1) == e:
-                    second(lo, n, after)
-        for e, n, after in SECOND:
-            lo, w = C * e, C * n
-            nc.vector.tensor_tensor(out_t[:].indirect(dst_t[:, lo // 16 : (lo + w) // 16]), ys[e][:], gates[lo // (T // 2)][:, lo % (T // 2) : lo % (T // 2) + w], MULT)
+            if e >= 1:
+                turn(e - 1)
+                for lo, n, after in SECOND:
+                    if max(after, lo + n - 1) == e - 1:
+                        second(lo, n, after)
         nc.sync.dma_start(out=out, in_=out_t[:])

@@ -20,8 +20,8 @@ MULT = mybir.AluOpType.mult
 P = 128
 PASSES = K // 512
 CHUNKS = (
-    (((512, 256),), ((512, 256),), ((512, 256),), ((256, 160), (256, 160))),
-    (((512, 0),), ((512, 0),), ((512, 0),), ((256, 128), (256, 128))),
+    (((512, 256),), ((512, 256), (256, 128)), ((512, 320),), ((256, 160),)),
+    (((512, 0),), ((512, 0),), ((512, 0),), ((256, 0), (256, 128))),
 )
 WORDS = (
     (0, 1, 0, 256, None), (1, 1, 256, 256, None), (2, 1, 512, 256, None), (3, 1, 768, 256, None),
@@ -37,7 +37,7 @@ ON_SCALAR = ()
 GATE1 = 5
 SPLIT = (0, 2, 8)
 FIRST0 = 1024
-LOADS = ("x00 x01 offs x02 x03 x10 x11 x12 dst s0 x13 w0", "s1 w1 w2 t u g0 w3")
+LOADS = ("x00 x01 offs x02 x03 x10 x11 x12 x13 s0 w0", "s1 w1 w2 dst t u g0 w3")
 SECOND = ((0, 1, 2), (1, 1, 2), (2, 1, 3), (3, 1, 4), (4, 1, 5), (5, 1, 6), (6, 2, 7))
 NB = 4
 HS = 2
@@ -155,7 +155,7 @@ def tile_moe_two_mlp_relu_kernel(tc, xT, w1_words, w1_scales, w2_words, w2_scale
                 slot_words[s, lo + at] = piece[:, at : at + P]
 
         def gather_bytes(name, lo, w, direct, shift):
-            piece = tile(name, [P, w], U8)
+            piece = tile(name, [P, w], U8, HOLD.get(name))
             nc.vector.tensor_copy(piece[:], scales[:].indirect(offs_t[:, lo // 16 : (lo + w) // 16]))
             if shift:
                 for r in range(4):

@@ -19,30 +19,22 @@ MULT = mybir.AluOpType.mult
 
 P = 128
 PASSES = K // 512
-CHUNKS = (
-    (((512, 256),), ((512, 256), (256, 128)), ((512, 320),), ((256, 160),)),
-    (((512, 0),), ((512, 0),), ((512, 0),), ((256, 0), (256, 128))),
+LIFT = 4
+WIDE, NARROW = 512, 256
+LOADS = (
+    ((WIDE,), (WIDE,), (NARROW, NARROW), (NARROW,), (NARROW,)),
+    ((WIDE,), (WIDE,), (WIDE,), (NARROW, NARROW)),
 )
-WORDS = (
-    (0, 1, 0, 256, None), (1, 1, 256, 256, None), (2, 1, 512, 256, None), (3, 1, 768, 256, None),
-    (4, 1, 1024, 512, None), (6, 1, 1536, 512, "hg0"),
-)
-BYTES_ = (
-    (0, 0, 256), (1, 256, 256), (2, 512, 256), (3, 1024, 512), (3, 768, 256), (5, 1536, 512),
-)
-HOLD = {}
-W0 = ((0, 1024), (1024, 1024))
-LATE = 1024
-ON_SCALAR = ()
-GATE1 = 5
-SPLIT = (0, 2, 8)
-FIRST0 = 1024
-LOADS = ("x00 x01 offs x02 x03 x10 x11 x12 x13 s0 w0", "s1 w1 w2 dst t u g0 w3")
-SECOND = ((0, 1, 2), (1, 1, 2), (2, 1, 3), (3, 1, 4), (4, 1, 5), (5, 1, 6), (6, 2, 7))
-NB = 4
-HS = 2
-GS = (0, 1024, 2048)
-BEHIND = {}
+EARLY = E // 2
+FIRST = 2
+PAIR = 2 * C
+TURN_BANKS = 4
+
+
+def vector_share(s, start, width):
+    if s == 0:
+        return width * 5 // 8
+    return width // 2 if start + width == T else 0
 
 
 def tile_moe_two_mlp_relu_kernel(tc, xT, w1_words, w1_scales, w2_words, w2_scales, gate, offs, dst, out):
@@ -50,8 +42,8 @@ def tile_moe_two_mlp_relu_kernel(tc, xT, w1_words, w1_scales, w2_words, w2_scale
     with ExitStack() as ctx:
         lists = ctx.enter_context(tc.tile_pool(name="lists", bufs=1))
         keep = ctx.enter_context(tc.tile_pool(name="keep", bufs=1))
-        psum_a = ctx.enter_context(tc.psum_pool(name="psum_a", bufs=8 - NB))
-        psum_b = ctx.enter_context(tc.psum_pool(name="psum_b", bufs=1))
+        psum_sums = ctx.enter_context(tc.psum_pool(name="psum_sums", bufs=8 - TURN_BANKS))
+        psum_turn = ctx.enter_context(tc.psum_pool(name="psum_turn", bufs=1))
 
         offs_t = lists.tile([P, T // 16], U16, name="offs_t")
         dst_t = lists.tile([P, T // 16], U16, name="dst_t")
@@ -60,164 +52,152 @@ def tile_moe_two_mlp_relu_kernel(tc, xT, w1_words, w1_scales, w2_words, w2_scale
             return keep.tile(shape, dtype, name=name, tag=tag or name, align_bytes=64)
 
         words = [tile(f"words{s}", [P, T], U32) for s in range(PASSES)]
-        scales = tile("scales", [P, T], U8)
-        w1w, gates = {}, {}
-        w1s = [tile(f"w1s{a}", [P, (SPLIT[a + 1] - SPLIT[a]) * PASSES, H], U8) for a in range(len(SPLIT) - 1)]
+        plane = tile("plane", [P, T], U8)
+        w1s = [tile("w1s_first", [P, FIRST * PASSES, H], U8), tile("w1s_rest", [P, (E - FIRST) * PASSES, H], U8)]
         w2w = tile("w2w", [P, E, 2 * N], U8)
         w2s = tile("w2s", [P, E, N], U8)
         out_t = tile("out_t", [P, T], F32)
         ident = tile("ident", [P, P], F32)
+        lifted = {lo: tile(f"lifted{lo}", [P, w], U8) for lo, w in [(0, C * EARLY)] + [(lo, PAIR) for lo in range(C * EARLY, T, PAIR)]}
 
-        for plane in w1s + [w2s]:
-            nc.vector.memset(plane[:].rearrange("p a b -> p (a b)").bitcast(I32), 0)
-        nc.vector.memset(scales[:].bitcast(I32), 0)
-        shifted = {}
-        for lo, w in ((0, LATE),)[: min(LATE, 1)] + tuple((lo, w) for at, lo, w in BYTES_ if lo >= LATE):
-            shifted[lo] = tile(f"shifted{lo}", [P, w], U8)
-            nc.vector.memset(shifted[lo][:].bitcast(I32), 0)
+        for weights_plane in w1s + [w2s]:
+            nc.vector.memset(weights_plane[:].rearrange("p a b -> p (a b)").bitcast(I32), 0)
+        for tokens_plane in [plane] + list(lifted.values()):
+            nc.vector.memset(tokens_plane[:].bitcast(I32), 0)
         make_identity(nc, ident[:])
 
-        raw = {}
+        raw, w1w, gates = {}, {}, {}
 
         def load_x(s, c):
-            c0 = sum(w for chunk in CHUNKS[s][:c] for w, v in chunk)
-            width = sum(w for w, v in CHUNKS[s][c])
+            start, width = sum(map(sum, LOADS[s][:c])), sum(LOADS[s][c])
             raw[s, c] = tile(f"raw{s}_{c}", [P, 4, width], F32)
-            nc.sync.dma_start(out=raw[s, c][:], in_=xT[512 * s : 512 * s + 512, c0 : c0 + width].rearrange("(p j) w -> p j w", j=4))
+            nc.sync.dma_start(out=raw[s, c][:], in_=xT[512 * s : 512 * s + 512, start : start + width].rearrange("(p j) w -> p j w", j=4))
 
-        def load_w1(a):
-            w1w[a] = tile(f"w1w{a}", [P, 2 * PASSES, 2 * H], U8, HOLD.get(f"w1w{a}"))
+        def load_w1(pair):
+            w1w[pair] = tile(f"w1w{pair}", [P, 2 * PASSES, 2 * H], U8)
             nc.sync.dma_start(
-                out=w1w[a][:].bitcast(I32),
-                in_=w1_words[2 * a : 2 * a + 2].rearrange("e s p b -> p (e s) b").bitcast(I32),
+                out=w1w[pair][:].bitcast(I32),
+                in_=w1_words[2 * pair : 2 * pair + 2].rearrange("e s p b -> p (e s) b").bitcast(I32),
             )
 
-        def load_gate(a):
-            lo, hi = GS[a], GS[a + 1]
-            gates[a] = tile(f"gate{a}", [P, hi - lo], F32, HOLD.get(f"gate{a}"))
-            nc.sync.dma_start(out=gates[a][:], in_=gate[:, lo:hi])
+        def load_gate(half):
+            gates[half] = tile(f"gate{half}", [P, T // 2], F32)
+            nc.sync.dma_start(out=gates[half][:], in_=gate[:, half * T // 2 : (half + 1) * T // 2])
 
-        def load_scales(plane, source):
+        def load_scales(weights_plane, source):
             rows = source.rearrange("e s (q r) i -> r q (e s) i", r=4)
             for r in range(4):
-                nc.sync.dma_start(out=plane[r:P:32, :, :].bitcast(I32), in_=rows[r].bitcast(I32))
+                nc.sync.dma_start(out=weights_plane[r:P:32, :, :].bitcast(I32), in_=rows[r].bitcast(I32))
 
-        def load(name):
-            if name == "offs":
+        for c in range(len(LOADS[0])):
+            load_x(0, c)
+            if c == 1:
                 nc.sync.dma_start(offs_t[:], offs)
-            if name == "dst":
-                nc.sync.dma_start(dst_t[:], dst)
-            if name[0] == "x":
-                load_x(int(name[1]), int(name[2]))
-            if name[0] == "w":
-                load_w1(int(name[1]))
-            if name[0] == "s":
-                a = int(name[1])
-                load_scales(w1s[a], w1_scales[SPLIT[a] : SPLIT[a + 1]])
-            if name == "t":
-                load_scales(w2s, w2_scales)
-            if name == "u":
-                nc.sync.dma_start(out=w2w[:].bitcast(I32), in_=w2_words.rearrange("e s p b -> p (e s) b").bitcast(I32))
-            if name[0] == "g":
-                load_gate(int(name[1]))
+        for c in range(len(LOADS[1])):
+            load_x(1, c)
+        load_scales(w1s[0], w1_scales[:FIRST])
+        load_w1(0)
 
-        for name in LOADS[0].split():
-            load(name)
-
-        def cast(engine, grouped, source, lo, hi, run):
+        def cast(engine, grouped, source, lo, hi):
             if hi > lo:
                 engine(
-                    grouped[:, lo:hi, :].rearrange("p (b i) j -> p b j i", i=run),
-                    source[:, :, lo:hi].rearrange("p j (b i) -> p b j i", i=run),
+                    grouped[:, lo:hi, :].rearrange("p (b i) j -> p b j i", i=2),
+                    source[:, :, lo:hi].rearrange("p j (b i) -> p b j i", i=2),
                 )
 
         def quantise(s):
-            c0 = 0
-            for c, chunk in enumerate(CHUNKS[s]):
+            start = 0
+            for c, pieces in enumerate(LOADS[s]):
                 at = 0
-                for w, v in chunk:
-                    grouped = tile(f"grouped{s}_{c0}", [P, w, 4], BF16)
-                    cast(nc.vector.tensor_copy, grouped, raw[s, c][:, :, at : at + w], 0, v, 2)
-                    cast(nc.scalar.copy, grouped, raw[s, c][:, :, at : at + w], v, w, 2)
+                for width in pieces:
+                    share = vector_share(s, start, width)
+                    grouped = tile(f"grouped{s}_{start}", [P, width, 4], BF16)
+                    cast(nc.vector.tensor_copy, grouped, raw[s, c][:, :, at : at + width], 0, share)
+                    cast(nc.scalar.copy, grouped, raw[s, c][:, :, at : at + width], share, width)
                     nc.vector.quantize_mx(
-                        out=words[s][:, c0 : c0 + w].bitcast(FP8X4),
-                        scales=scales[4 * (1 - s) : P, c0 : c0 + w],
+                        out=words[s][:, start : start + width].bitcast(FP8X4),
+                        scales=plane[LIFT * (1 - s) : P, start : start + width],
                         in_=grouped[:].rearrange("p w j -> p (w j)"),
                     )
-                    at, c0 = at + w, c0 + w
+                    at, start = at + width, start + width
 
-        slot_words, slot_scales, hs, hq, hqs, ys = {}, {}, {}, {}, {}, {}
+        slot_words, slot_scales, hs, hq, hqs = {}, {}, {}, {}, {}
 
-        def gather_words(s, lo, w, tag):
-            piece = tile(f"W{s}_{lo}", [P, w], U32, tag)
+        def gather_words(s, lo, w, tag=None):
+            piece = tile(f"slot_words{s}_{lo}", [P, w], U32, tag)
             nc.vector.tensor_copy(piece[:], words[s][:].indirect(offs_t[:, lo // 16 : (lo + w) // 16]))
             for at in range(0, w, P):
                 slot_words[s, lo + at] = piece[:, at : at + P]
 
-        def gather_bytes(name, lo, w, direct, shift):
-            piece = tile(name, [P, w], U8, HOLD.get(name))
-            nc.vector.tensor_copy(piece[:], scales[:].indirect(offs_t[:, lo // 16 : (lo + w) // 16]))
-            if shift:
+        def gather_bytes(passes, lo, w, tag=None):
+            piece = tile(f"slot_bytes{passes[0]}_{lo}", [P, w], U8, tag)
+            nc.vector.tensor_copy(piece[:], plane[:].indirect(offs_t[:, lo // 16 : (lo + w) // 16]))
+            if 0 in passes:
                 for r in range(4):
-                    (nc.scalar if lo in ON_SCALAR else nc.sync).dma_start(out=shifted[lo][r:P:32, :].bitcast(I32), in_=piece[4 + r : P : 32, :].bitcast(I32))
+                    nc.sync.dma_start(out=lifted[lo][r:P:32, :].bitcast(I32), in_=piece[LIFT + r : P : 32, :].bitcast(I32))
             for at in range(0, w, P):
-                if direct:
-                    slot_scales[1, lo + at] = piece[:, at : at + P]
-                if shift:
-                    slot_scales[0, lo + at] = shifted[lo][:, at : at + P]
+                for s in passes:
+                    slot_scales[s, lo + at] = (piece if s == 1 else lifted[lo])[:, at : at + P]
 
         quantise(0)
-        if LATE:
-            gather_bytes("early", 0, LATE, False, True)
-        for lo, w in W0:
-            gather_words(0, lo, w, None)
-        for name in LOADS[1].split():
-            load(name)
+        gather_bytes((0,), 0, C * EARLY)
+        for lo in range(0, T, T // 2):
+            gather_words(0, lo, T // 2)
+        load_scales(w1s[1], w1_scales[FIRST:])
+        load_w1(1)
+        load_w1(2)
+        nc.sync.dma_start(dst_t[:], dst)
+        load_scales(w2s, w2_scales)
+        nc.sync.dma_start(out=w2w[:].bitcast(I32), in_=w2_words.rearrange("e s p b -> p (e s) b").bitcast(I32))
+        load_gate(0)
+        load_w1(3)
         quantise(1)
 
         def gather(e):
-            for at, lo, w in BYTES_:
-                if at == e:
-                    gather_bytes(f"B{lo}", lo, w, True, lo >= LATE)
-            for at, s, lo, w, tag in WORDS:
-                if at == e:
-                    gather_words(s, lo, w, tag)
+            ahead = e + 1
+            if ahead >= EARLY and ahead % 2 == 0 and ahead < E:
+                gather_bytes((1, 0), C * ahead, PAIR, "hg0" if ahead == E - 2 else None)
+            if e < EARLY:
+                gather_bytes((1,), C * e, C)
+                gather_words(1, C * e, C)
+            elif e % 2 == 0:
+                gather_words(1, C * e, PAIR, "hg1" if e == E - 2 else None)
 
         def first(e):
-            part = sum(e >= lo for lo in SPLIT[1:])
-            hs[e] = tile(f"hs{e}", [P, 2, 2, P, 2], BF16, f"hs{e % HS}")
+            hs[e] = tile(f"hs{e}", [P, 2, 2, P, 2], BF16, f"hs{e % 2}")
+            scales = w1s[0][:, PASSES * e :, :] if e < FIRST else w1s[1][:, PASSES * (e - FIRST) :, :]
+            order = (0, 1) if e < EARLY else (1, 0)
             for b in range(2):
-                acc = psum_a.tile([P, H], F32, name="acc")
-                order = (0, 1) if C * e < FIRST0 else (1, 0)
+                acc = psum_sums.tile([P, H], F32, name="acc")
                 for s in order:
                     nc.tensor.matmul_mx(
                         out=acc[:],
                         lhsT=slot_words[s, C * e + P * b].bitcast(FP8X4),
                         lhsT_scale=slot_scales[s, C * e + P * b],
-                        rhs=w1w[e // 2][:, 2 * (e % 2) + s, :].bitcast(FP4X4),
-                        rhs_scale=w1s[part][:, 2 * (e - SPLIT[part]) + s, :],
+                        rhs=w1w[e // 2][:, PASSES * (e % 2) + s, :].bitcast(FP4X4),
+                        rhs_scale=scales[:, s, :],
                         start=(s == order[0]),
                         stop=(s == order[1]),
                     )
-                nc.scalar.activation(hs[e][:, b], acc[:].rearrange("c (p u e) -> c u p e", u=2, e=2), RELU)
+                nc.scalar.activation(hs[e][:, b], acc[:].rearrange("c (p u v) -> c u p v", u=2, v=2), RELU)
 
         def turn(e):
             hg = tile(f"hg{e}", [P, C, 4], BF16)
             hg_words = hg[:].rearrange("p c t -> p (c t)").bitcast(F32).rearrange("p (c u) -> p c u", u=2)
-            turned = hs[e][:].rearrange("c b u p e -> c b u (p e)").bitcast(F32)
-            tp = psum_b.tile([P, 2, C], F32, name=f"tp{e}", tag=f"bank{e % NB}")
+            hs_words = hs[e][:].rearrange("c b u p v -> c b u (p v)").bitcast(F32)
+            turned = psum_turn.tile([P, 2, C], F32, name=f"turned{e}", tag=f"bank{e % TURN_BANKS}")
             for b in range(2):
                 for u in range(2):
-                    nc.tensor.transpose(tp[:, u, P * b : P * b + P], turned[:, b, u, :], ident[:])
-            nc.scalar.copy(hg_words, tp[:].rearrange("p u r -> p r u"))
-            hq[e] = tile(f"hq{e}", [P, C], U32, BEHIND.get(e))
+                    nc.tensor.transpose(turned[:, u, P * b : P * b + P], hs_words[:, b, u, :], ident[:])
+            nc.scalar.copy(hg_words, turned[:].rearrange("p u r -> p r u"))
+            hq[e] = tile(f"hq{e}", [P, C], U32)
             hqs[e] = tile(f"hqs{e}", [P, C], U8)
             nc.vector.quantize_mx(out=hq[e][:].bitcast(FP8X4), scales=hqs[e][:], in_=hg[:].rearrange("p c t -> p (c t)"))
 
-        def second(lo, n, after):
-            y = psum_b.tile([P, n, C], F32, name=f"y{lo}", tag=f"bank{after % NB}")
-            for b in range(n):
-                e = lo + b
+        def second(experts, behind):
+            lo, w = C * experts[0], C * len(experts)
+            y = psum_turn.tile([P, len(experts), C], F32, name=f"y{lo}", tag=f"bank{behind % TURN_BANKS}")
+            for b, e in enumerate(experts):
                 nc.tensor.matmul_mx(
                     out=y[:, b, :],
                     lhsT=w2w[:, e, :].bitcast(FP4X4),
@@ -227,24 +207,19 @@ def tile_moe_two_mlp_relu_kernel(tc, xT, w1_words, w1_scales, w2_words, w2_scale
                     start=True,
                     stop=True,
                 )
-            ys[lo] = tile(f"ys{lo}", [P, n * C], F32)
-            nc.scalar.copy(ys[lo][:], y[:].rearrange("p b c -> p (b c)"))
-            first_slot, w = C * lo, C * n
-            half = int(first_slot >= GS[1])
-            at = first_slot - GS[half]
-            assert at + w <= GS[half + 1] - GS[half]
-            index = dst_t[:, first_slot // 16 : (first_slot + w) // 16]
-            nc.vector.tensor_tensor(out_t[:].indirect(index), ys[lo][:], gates[half][:, at : at + w], MULT)
+            ys = tile(f"ys{lo}", [P, w], F32)
+            nc.scalar.copy(ys[:], y[:].rearrange("p b c -> p (b c)"))
+            half, at = divmod(lo, T // 2)
+            nc.vector.tensor_tensor(out_t[:].indirect(dst_t[:, lo // 16 : (lo + w) // 16]), ys[:], gates[half][:, at : at + w], MULT)
 
         for e in range(E + 1):
             if e < E:
                 gather(e)
                 first(e)
-            if e == GATE1:
+            if e == E - 3:
                 load_gate(1)
             if e >= 1:
                 turn(e - 1)
-                for lo, n, after in SECOND:
-                    if max(after, lo + n - 1) == e - 1:
-                        second(lo, n, after)
+            if e >= 2:
+                second((e - 2, e - 1) if e == E else (e - 2,), e - 1)
         nc.sync.dma_start(out=out, in_=out_t[:])

@@ -22,7 +22,7 @@ PASSES = K // 512
 LIFT = 4
 WIDE, NARROW = 512, 256
 LOADS = (
-    ((WIDE,), (WIDE,), (NARROW, NARROW), (NARROW,), (NARROW,)),
+    ((WIDE, NARROW), (WIDE,), (NARROW, NARROW), (NARROW,)),
     ((WIDE,), (WIDE,), (WIDE,), (NARROW, NARROW)),
 )
 EARLY = E // 2
@@ -222,4 +222,5 @@ def tile_moe_two_mlp_relu_kernel(tc, xT, w1_words, w1_scales, w2_words, w2_scale
                 turn(e - 1)
             if e >= 2:
                 second((e - 2, e - 1) if e == E else (e - 2,), e - 1)
-        nc.sync.dma_start(out=out, in_=out_t[:])
+        nc.sync.dma_start(out=out[:, : T // 2], in_=out_t[:, : T // 2])
+        nc.scalar.dma_start(out=out[:, T // 2 :], in_=out_t[:, T // 2 :])

@@ -129,8 +129,8 @@ def tile_moe_two_mlp_relu_kernel(tc, xT, w1_words, w1_scales, w2_words, w2_scale
             for at in range(0, w, P):
                 slot_words[s, lo + at] = piece[:, at : at + P]
 
-        def gather_bytes(passes, lo, w, tag=None):
-            piece = tile(f"slot_bytes{passes[0]}_{lo}", [P, w], U8, tag)
+        def gather_bytes(passes, lo, w):
+            piece = tile(f"slot_bytes{passes[0]}_{lo}", [P, w], U8)
             nc.vector.tensor_copy(piece[:], plane[:].indirect(offs_t[:, lo // 16 : (lo + w) // 16]))
             if 0 in passes:
                 for r in range(4):
@@ -156,12 +156,12 @@ def tile_moe_two_mlp_relu_kernel(tc, xT, w1_words, w1_scales, w2_words, w2_scale
         def gather(e):
             ahead = e + 1
             if ahead >= EARLY and ahead % 2 == 0 and ahead < E:
-                gather_bytes((1, 0), C * ahead, PAIR, "hg0" if ahead == E - 2 else None)
+                gather_bytes((1, 0), C * ahead, PAIR)
             if e < EARLY:
                 gather_bytes((1,), C * e, C)
                 gather_words(1, C * e, C)
             elif e % 2 == 0:
-                gather_words(1, C * e, PAIR, "hg1" if e == E - 2 else None)
+                gather_words(1, C * e, PAIR, "hg0" if e == E - 2 else None)
 
         def first(e):
             hs[e] = tile(f"hs{e}", [P, 2, 2, P, 2], BF16, f"hs{e % 2}")
@@ -220,7 +220,8 @@ def tile_moe_two_mlp_relu_kernel(tc, xT, w1_words, w1_scales, w2_words, w2_scale
                 load_gate(1)
             if e >= 1:
                 turn(e - 1)
-            if e >= 2:
+            if e == 3:
+                second((0,), e - 1)
+            if e >= 3:
                 second((e - 2, e - 1) if e == E else (e - 2,), e - 1)
-        nc.sync.dma_start(out=out[:, : T // 2], in_=out_t[:, : T // 2])
-        nc.scalar.dma_start(out=out[:, T // 2 :], in_=out_t[:, T // 2 :])
+        nc.sync.dma_start(out=out, in_=out_t[:])

@@ -49,7 +49,7 @@ def tile_moe_two_mlp_relu_kernel(tc, xT, w1_words, w1_scales, w2_words, w2_scale
         dst_t = lists.tile([P, T // 16], U16, name="dst_t")
 
         def tile(name, shape, dtype, tag=None):
-            return keep.tile(shape, dtype, name=name, tag=tag or name, align_bytes=64)
+            return keep.tile(shape, dtype, name=name, tag=tag or name, align_bytes=256)
 
         words = [tile(f"words{s}", [P, T], U32) for s in range(PASSES)]
         plane = tile("plane", [P, T], U8)

@@ -45,8 +45,8 @@ def tile_moe_two_mlp_relu_kernel(tc, xT, w1_words, w1_scales, w2_words, w2_scale
         psum_sums = ctx.enter_context(tc.psum_pool(name="psum_sums", bufs=8 - TURN_BANKS))
         psum_turn = ctx.enter_context(tc.psum_pool(name="psum_turn", bufs=1))
 
-        offs_t = lists.tile([P, T // 16], U16, name="offs_t")
-        dst_t = lists.tile([P, T // 16], U16, name="dst_t")
+        offs_t = lists.tile([P, T // 16], U16, name="offs_t", align_bytes=256)
+        dst_t = lists.tile([P, T // 16], U16, name="dst_t", align_bytes=256)
 
         def tile(name, shape, dtype, tag=None):
             return keep.tile(shape, dtype, name=name, tag=tag or name, align_bytes=256)

@@ -23,18 +23,19 @@ LIFT = 4
 WIDE, NARROW = 512, 256
 LOADS = (
     ((WIDE, NARROW), (WIDE,), (NARROW, NARROW), (NARROW,)),
-    ((WIDE,), (WIDE,), (WIDE,), (NARROW, NARROW)),
+    ((WIDE,), (WIDE,), (WIDE,), (NARROW,), (NARROW,)),
 )
-EARLY = E // 2
-FIRST = 2
+EARLY = 2
+FIRST = E // 2
 PAIR = 2 * C
-TURN_BANKS = 4
+AHEAD = 3
+HELD = 2
 
 
 def vector_share(s, start, width):
-    if s == 0:
+    if s == 0 or start + width == T:
         return width * 5 // 8
-    return width // 2 if start + width == T else 0
+    return width // 2 if width == NARROW else 0
 
 
 def tile_moe_two_mlp_relu_kernel(tc, xT, w1_words, w1_scales, w2_words, w2_scales, gate, offs, dst, out):
@@ -42,8 +43,7 @@ def tile_moe_two_mlp_relu_kernel(tc, xT, w1_words, w1_scales, w2_words, w2_scale
     with ExitStack() as ctx:
         lists = ctx.enter_context(tc.tile_pool(name="lists", bufs=1))
         keep = ctx.enter_context(tc.tile_pool(name="keep", bufs=1))
-        psum_sums = ctx.enter_context(tc.psum_pool(name="psum_sums", bufs=8 - TURN_BANKS))
-        psum_turn = ctx.enter_context(tc.psum_pool(name="psum_turn", bufs=1))
+        psum = ctx.enter_context(tc.psum_pool(name="psum", bufs=1))
 
         offs_t = lists.tile([P, T // 16], U16, name="offs_t", align_bytes=256)
         dst_t = lists.tile([P, T // 16], U16, name="dst_t", align_bytes=256)
@@ -58,7 +58,7 @@ def tile_moe_two_mlp_relu_kernel(tc, xT, w1_words, w1_scales, w2_words, w2_scale
         w2s = tile("w2s", [P, E, N], U8)
         out_t = tile("out_t", [P, T], F32)
         ident = tile("ident", [P, P], F32)
-        lifted = {lo: tile(f"lifted{lo}", [P, w], U8) for lo, w in [(0, C * EARLY)] + [(lo, PAIR) for lo in range(C * EARLY, T, PAIR)]}
+        lifted = {lo: tile(f"lifted{lo}", [P, w], U8) for lo, w in [(0, PAIR), (PAIR, PAIR), (2 * PAIR, 2 * PAIR)]}
 
         for weights_plane in w1s + [w2s]:
             nc.vector.memset(weights_plane[:].rearrange("p a b -> p (a b)").bitcast(I32), 0)
@@ -93,10 +93,8 @@ def tile_moe_two_mlp_relu_kernel(tc, xT, w1_words, w1_scales, w2_words, w2_scale
             load_x(0, c)
             if c == 1:
                 nc.sync.dma_start(offs_t[:], offs)
-        for c in range(len(LOADS[1])):
+        for c in range(len(LOADS[1]) - HELD):
             load_x(1, c)
-        load_scales(w1s[0], w1_scales[:FIRST])
-        load_w1(0)
 
         def cast(engine, grouped, source, lo, hi):
             if hi > lo:
@@ -121,7 +119,7 @@ def tile_moe_two_mlp_relu_kernel(tc, xT, w1_words, w1_scales, w2_words, w2_scale
                     )
                     at, start = at + width, start + width
 
-        slot_words, slot_scales, hs, hq, hqs = {}, {}, {}, {}, {}
+        slot_words, slot_bytes, slot_scales, hs, hq, hqs = {}, {}, {}, {}, {}, {}
 
         def gather_words(s, lo, w, tag=None):
             piece = tile(f"slot_words{s}_{lo}", [P, w], U32, tag)
@@ -129,46 +127,58 @@ def tile_moe_two_mlp_relu_kernel(tc, xT, w1_words, w1_scales, w2_words, w2_scale
             for at in range(0, w, P):
                 slot_words[s, lo + at] = piece[:, at : at + P]
 
-        def gather_bytes(passes, lo, w):
-            piece = tile(f"slot_bytes{passes[0]}_{lo}", [P, w], U8)
-            nc.vector.tensor_copy(piece[:], plane[:].indirect(offs_t[:, lo // 16 : (lo + w) // 16]))
-            if 0 in passes:
-                for r in range(4):
-                    nc.sync.dma_start(out=lifted[lo][r:P:32, :].bitcast(I32), in_=piece[LIFT + r : P : 32, :].bitcast(I32))
+        def gather_bytes(name, lo, w):
+            slot_bytes[name] = tile(f"slot_bytes_{name}", [P, w], U8), lo
+            nc.vector.tensor_copy(slot_bytes[name][0][:], plane[:].indirect(offs_t[:, lo // 16 : (lo + w) // 16]))
             for at in range(0, w, P):
-                for s in passes:
-                    slot_scales[s, lo + at] = (piece if s == 1 else lifted[lo])[:, at : at + P]
+                slot_scales[1, lo + at] = slot_bytes[name][0][:, at : at + P]
+
+        def lift(name, lo):
+            piece, first_slot = slot_bytes[name]
+            w = lifted[lo].shape[1]
+            for r in range(4):
+                nc.sync.dma_start(
+                    out=lifted[lo][r:P:32, :].bitcast(I32),
+                    in_=piece[LIFT + r : P : 32, lo - first_slot : lo - first_slot + w].bitcast(I32),
+                )
+            for at in range(0, w, P):
+                slot_scales[0, lo + at] = lifted[lo][:, at : at + P]
 
         quantise(0)
-        gather_bytes((0,), 0, C * EARLY)
+        gather_bytes("early", 0, PAIR)
+        lift("early", 0)
+        for c in range(len(LOADS[1]) - HELD, len(LOADS[1])):
+            load_x(1, c)
         for lo in range(0, T, T // 2):
             gather_words(0, lo, T // 2)
-        load_scales(w1s[1], w1_scales[FIRST:])
+        load_scales(w1s[0], w1_scales[:FIRST])
+        load_w1(0)
         load_w1(1)
-        load_w1(2)
-        nc.sync.dma_start(dst_t[:], dst)
         load_scales(w2s, w2_scales)
         nc.sync.dma_start(out=w2w[:].bitcast(I32), in_=w2_words.rearrange("e s p b -> p (e s) b").bitcast(I32))
+        nc.sync.dma_start(dst_t[:], dst)
         load_gate(0)
-        load_w1(3)
         quantise(1)
 
-        def gather(e):
-            ahead = e + 1
-            if ahead >= EARLY and ahead % 2 == 0 and ahead < E:
-                gather_bytes((1, 0), C * ahead, PAIR)
-            if e < EARLY:
-                gather_bytes((1,), C * e, C)
-                gather_words(1, C * e, C)
-            elif e % 2 == 0:
-                gather_words(1, C * e, PAIR, "hg0" if e == E - 2 else None)
+        gather_bytes("first", 0, C)
+        gather_words(1, 0, C)
+        gather_bytes("middle", C, C + PAIR)
+        lift("middle", PAIR)
+        load_scales(w1s[1], w1_scales[FIRST:])
+        load_w1(2)
+        gather_words(1, C, C)
+        gather_words(1, PAIR, PAIR)
+        gather_bytes("late", 2 * PAIR, 2 * PAIR)
+        lift("late", 2 * PAIR)
+        load_w1(3)
+        load_gate(1)
 
         def first(e):
             hs[e] = tile(f"hs{e}", [P, 2, 2, P, 2], BF16, f"hs{e % 2}")
             scales = w1s[0][:, PASSES * e :, :] if e < FIRST else w1s[1][:, PASSES * (e - FIRST) :, :]
             order = (0, 1) if e < EARLY else (1, 0)
             for b in range(2):
-                acc = psum_sums.tile([P, H], F32, name="acc")
+                acc = psum.tile([P, H], F32, name=f"acc{e}_{b}", tag=f"sums{b}_{e % AHEAD}")
                 for s in order:
                     nc.tensor.matmul_mx(
                         out=acc[:],
@@ -185,7 +195,7 @@ def tile_moe_two_mlp_relu_kernel(tc, xT, w1_words, w1_scales, w2_words, w2_scale
             hg = tile(f"hg{e}", [P, C, 4], BF16)
             hg_words = hg[:].rearrange("p c t -> p (c t)").bitcast(F32).rearrange("p (c u) -> p c u", u=2)
             hs_words = hs[e][:].rearrange("c b u p v -> c b u (p v)").bitcast(F32)
-            turned = psum_turn.tile([P, 2, C], F32, name=f"turned{e}", tag=f"bank{e % TURN_BANKS}")
+            turned = psum.tile([P, 2, C], F32, name=f"turned{e}", tag=f"turn{e % 2}")
             for b in range(2):
                 for u in range(2):
                     nc.tensor.transpose(turned[:, u, P * b : P * b + P], hs_words[:, b, u, :], ident[:])
@@ -194,9 +204,9 @@ def tile_moe_two_mlp_relu_kernel(tc, xT, w1_words, w1_scales, w2_words, w2_scale
             hqs[e] = tile(f"hqs{e}", [P, C], U8)
             nc.vector.quantize_mx(out=hq[e][:].bitcast(FP8X4), scales=hqs[e][:], in_=hg[:].rearrange("p c t -> p (c t)"))
 
-        def second(experts, behind):
+        def second(experts, bank):
             lo, w = C * experts[0], C * len(experts)
-            y = psum_turn.tile([P, len(experts), C], F32, name=f"y{lo}", tag=f"bank{behind % TURN_BANKS}")
+            y = psum.tile([P, len(experts), C], F32, name=f"y{lo}", tag=bank)
             for b, e in enumerate(experts):
                 nc.tensor.matmul_mx(
                     out=y[:, b, :],
@@ -212,16 +222,15 @@ def tile_moe_two_mlp_relu_kernel(tc, xT, w1_words, w1_scales, w2_words, w2_scale
             half, at = divmod(lo, T // 2)
             nc.vector.tensor_tensor(out_t[:].indirect(dst_t[:, lo // 16 : (lo + w) // 16]), ys[:], gates[half][:, at : at + w], MULT)
 
-        for e in range(E + 1):
-            if e < E:
-                gather(e)
-                first(e)
-            if e == E - 3:
-                load_gate(1)
+        for e in range(E):
+            if e >= E // 2 and e % 2 == 0:
+                gather_words(1, C * e, PAIR, f"hg{(e - E // 2) // 2}")
+            first(e)
             if e >= 1:
                 turn(e - 1)
-            if e == 3:
-                second((0,), e - 1)
-            if e >= 3:
-                second((e - 2, e - 1) if e == E else (e - 2,), e - 1)
+            if e >= 2:
+                second((e - 2,), f"sums0_{e % AHEAD}")
+        turn(E - 1)
+        second((E - 2,), f"turn{(E - 1) % 2}")
+        second((E - 1,), f"turn{E % 2}")
         nc.sync.dma_start(out=out, in_=out_t[:])

@@ -22,7 +22,7 @@ PASSES = K // 512
 LIFT = 4
 WIDE, NARROW = 512, 256
 LOADS = (
-    ((WIDE, NARROW), (WIDE,), (NARROW, NARROW), (NARROW,)),
+    ((WIDE, WIDE), (WIDE, NARROW), (NARROW,)),
     ((WIDE,), (WIDE,), (WIDE,), (NARROW,), (NARROW,)),
 )
 EARLY = 2
@@ -176,18 +176,17 @@ def tile_moe_two_mlp_relu_kernel(tc, xT, w1_words, w1_scales, w2_words, w2_scale
         def first(e):
             hs[e] = tile(f"hs{e}", [P, 2, 2, P, 2], BF16, f"hs{e % 2}")
             scales = w1s[0][:, PASSES * e :, :] if e < FIRST else w1s[1][:, PASSES * (e - FIRST) :, :]
-            order = (0, 1) if e < EARLY else (1, 0)
             for b in range(2):
                 acc = psum.tile([P, H], F32, name=f"acc{e}_{b}", tag=f"sums{b}_{e % AHEAD}")
-                for s in order:
+                for s in range(PASSES):
                     nc.tensor.matmul_mx(
                         out=acc[:],
                         lhsT=slot_words[s, C * e + P * b].bitcast(FP8X4),
                         lhsT_scale=slot_scales[s, C * e + P * b],
                         rhs=w1w[e // 2][:, PASSES * (e % 2) + s, :].bitcast(FP4X4),
                         rhs_scale=scales[:, s, :],
-                        start=(s == order[0]),
-                        stop=(s == order[1]),
+                        start=(s == 0),
+                        stop=(s == PASSES - 1),
                     )
                 nc.scalar.activation(hs[e][:, b], acc[:].rearrange("c (p u v) -> c u p v", u=2, v=2), RELU)
 

@@ -23,19 +23,20 @@ LIFT = 4
 WIDE, NARROW = 512, 256
 LOADS = (
     ((WIDE, WIDE), (WIDE, NARROW), (NARROW,)),
-    ((WIDE,), (WIDE,), (WIDE,), (NARROW,), (NARROW,)),
+    ((NARROW,), (WIDE,), (WIDE,), (NARROW, NARROW), (NARROW,)),
 )
 EARLY = 2
-FIRST = E // 2
+WORD_LOADS = ((0, 1), (1, 2), (2, 4), (4, 6), (6, 8))
+SCALE_LOADS = ((0, 2), (2, 4), (4, 8))
 PAIR = 2 * C
 AHEAD = 3
 HELD = 2
 
 
 def vector_share(s, start, width):
-    if s == 0 or start + width == T:
-        return width * 5 // 8
-    return width // 2 if width == NARROW else 0
+    if s == 0 or start >= T - 3 * NARROW:
+        return width // 2
+    return 0
 
 
 def tile_moe_two_mlp_relu_kernel(tc, xT, w1_words, w1_scales, w2_words, w2_scales, gate, offs, dst, out):
@@ -53,7 +54,7 @@ def tile_moe_two_mlp_relu_kernel(tc, xT, w1_words, w1_scales, w2_words, w2_scale
 
         words = [tile(f"words{s}", [P, T], U32) for s in range(PASSES)]
         plane = tile("plane", [P, T], U8)
-        w1s = [tile("w1s_first", [P, FIRST * PASSES, H], U8), tile("w1s_rest", [P, (E - FIRST) * PASSES, H], U8)]
+        w1s = [tile(f"w1s{lo}", [P, (hi - lo) * PASSES, H], U8) for lo, hi in SCALE_LOADS]
         w2w = tile("w2w", [P, E, 2 * N], U8)
         w2s = tile("w2s", [P, E, N], U8)
         out_t = tile("out_t", [P, T], F32)
@@ -66,19 +67,25 @@ def tile_moe_two_mlp_relu_kernel(tc, xT, w1_words, w1_scales, w2_words, w2_scale
             nc.vector.memset(tokens_plane[:].bitcast(I32), 0)
         make_identity(nc, ident[:])
 
-        raw, w1w, gates = {}, {}, {}
+        raw, w1w, w1_planes, gates = {}, {}, {}, {}
 
         def load_x(s, c):
             start, width = sum(map(sum, LOADS[s][:c])), sum(LOADS[s][c])
             raw[s, c] = tile(f"raw{s}_{c}", [P, 4, width], F32)
             nc.sync.dma_start(out=raw[s, c][:], in_=xT[512 * s : 512 * s + 512, start : start + width].rearrange("(p j) w -> p j w", j=4))
 
-        def load_w1(pair):
-            w1w[pair] = tile(f"w1w{pair}", [P, 2 * PASSES, 2 * H], U8)
-            nc.sync.dma_start(
-                out=w1w[pair][:].bitcast(I32),
-                in_=w1_words[2 * pair : 2 * pair + 2].rearrange("e s p b -> p (e s) b").bitcast(I32),
-            )
+        def load_w1(n):
+            lo, hi = WORD_LOADS[n]
+            piece = tile(f"w1w{lo}", [P, (hi - lo) * PASSES, 2 * H], U8)
+            nc.sync.dma_start(out=piece[:].bitcast(I32), in_=w1_words[lo:hi].rearrange("e s p b -> p (e s) b").bitcast(I32))
+            for e in range(lo, hi):
+                w1w[e] = piece[:, PASSES * (e - lo) : PASSES * (e - lo + 1), :]
+
+        def load_w1_scales(n):
+            lo, hi = SCALE_LOADS[n]
+            load_scales(w1s[n], w1_scales[lo:hi])
+            for e in range(lo, hi):
+                w1_planes[e] = w1s[n][:, PASSES * (e - lo) : PASSES * (e - lo + 1), :]
 
         def load_gate(half):
             gates[half] = tile(f"gate{half}", [P, T // 2], F32)
@@ -151,31 +158,33 @@ def tile_moe_two_mlp_relu_kernel(tc, xT, w1_words, w1_scales, w2_words, w2_scale
             load_x(1, c)
         for lo in range(0, T, T // 2):
             gather_words(0, lo, T // 2)
-        load_scales(w1s[0], w1_scales[:FIRST])
+        load_w1_scales(0)
         load_w1(0)
         load_w1(1)
+        load_w1_scales(1)
+        load_w1(2)
         load_scales(w2s, w2_scales)
         nc.sync.dma_start(out=w2w[:].bitcast(I32), in_=w2_words.rearrange("e s p b -> p (e s) b").bitcast(I32))
-        nc.sync.dma_start(dst_t[:], dst)
-        load_gate(0)
         quantise(1)
 
         gather_bytes("first", 0, C)
         gather_words(1, 0, C)
         gather_bytes("middle", C, C + PAIR)
         lift("middle", PAIR)
-        load_scales(w1s[1], w1_scales[FIRST:])
-        load_w1(2)
+        nc.sync.dma_start(dst_t[:], dst)
+        load_gate(0)
+        load_w1_scales(2)
+        load_w1(3)
         gather_words(1, C, C)
         gather_words(1, PAIR, PAIR)
         gather_bytes("late", 2 * PAIR, 2 * PAIR)
         lift("late", 2 * PAIR)
-        load_w1(3)
+        gather_words(1, 2 * PAIR, PAIR)
+        load_w1(4)
         load_gate(1)
 
         def first(e):
             hs[e] = tile(f"hs{e}", [P, 2, 2, P, 2], BF16, f"hs{e % 2}")
-            scales = w1s[0][:, PASSES * e :, :] if e < FIRST else w1s[1][:, PASSES * (e - FIRST) :, :]
             for b in range(2):
                 acc = psum.tile([P, H], F32, name=f"acc{e}_{b}", tag=f"sums{b}_{e % AHEAD}")
                 for s in range(PASSES):
@@ -183,8 +192,8 @@ def tile_moe_two_mlp_relu_kernel(tc, xT, w1_words, w1_scales, w2_words, w2_scale
                         out=acc[:],
                         lhsT=slot_words[s, C * e + P * b].bitcast(FP8X4),
                         lhsT_scale=slot_scales[s, C * e + P * b],
-                        rhs=w1w[e // 2][:, PASSES * (e % 2) + s, :].bitcast(FP4X4),
-                        rhs_scale=scales[:, s, :],
+                        rhs=w1w[e][:, s, :].bitcast(FP4X4),
+                        rhs_scale=w1_planes[e][:, s, :],
                         start=(s == 0),
                         stop=(s == PASSES - 1),
                     )
@@ -222,8 +231,8 @@ def tile_moe_two_mlp_relu_kernel(tc, xT, w1_words, w1_scales, w2_words, w2_scale
             nc.vector.tensor_tensor(out_t[:].indirect(dst_t[:, lo // 16 : (lo + w) // 16]), ys[:], gates[half][:, at : at + w], MULT)
 
         for e in range(E):
-            if e >= E // 2 and e % 2 == 0:
-                gather_words(1, C * e, PAIR, f"hg{(e - E // 2) // 2}")
+            if e == E - 2:
+                gather_words(1, C * e, PAIR, "hg0")
             first(e)
             if e >= 1:
                 turn(e - 1)

@@ -22,7 +22,7 @@ PASSES = K // 512
 LIFT = 4
 WIDE, NARROW = 512, 256
 LOADS = (
-    ((WIDE, WIDE), (WIDE, NARROW), (NARROW,)),
+    ((WIDE, NARROW), (WIDE,), (NARROW, NARROW), (NARROW,)),
     ((NARROW,), (WIDE,), (WIDE,), (NARROW, NARROW), (NARROW,)),
 )
 EARLY = 2
@@ -34,9 +34,9 @@ HELD = 2
 
 
 def vector_share(s, start, width):
-    if s == 0 or start >= T - 3 * NARROW:
+    if s == 0 or start + width == T:
         return width // 2
-    return 0
+    return width // 4 if start >= T - 3 * NARROW else 0
 
 
 def tile_moe_two_mlp_relu_kernel(tc, xT, w1_words, w1_scales, w2_words, w2_scales, gate, offs, dst, out):

@@ -25,18 +25,17 @@ LOADS = (
     ((WIDE, NARROW), (WIDE,), (NARROW, NARROW), (NARROW,)),
     ((NARROW,), (WIDE,), (WIDE,), (NARROW, NARROW), (NARROW,)),
 )
-EARLY = 2
 WORD_LOADS = ((0, 1), (1, 2), (2, 4), (4, 6), (6, 8))
-SCALE_LOADS = ((0, 2), (2, 4), (4, 8))
+SCALE_LOADS = ((0, 2), (2, 8))
 PAIR = 2 * C
 AHEAD = 3
 HELD = 2
 
 
 def vector_share(s, start, width):
-    if s == 0 or start + width == T:
+    if s == 0 or start >= T - 3 * NARROW:
         return width // 2
-    return width // 4 if start >= T - 3 * NARROW else 0
+    return 0
 
 
 def tile_moe_two_mlp_relu_kernel(tc, xT, w1_words, w1_scales, w2_words, w2_scales, gate, offs, dst, out):
@@ -98,8 +97,7 @@ def tile_moe_two_mlp_relu_kernel(tc, xT, w1_words, w1_scales, w2_words, w2_scale
 
         for c in range(len(LOADS[0])):
             load_x(0, c)
-            if c == 1:
-                nc.sync.dma_start(offs_t[:], offs)
+        nc.sync.dma_start(offs_t[:], offs)
         for c in range(len(LOADS[1]) - HELD):
             load_x(1, c)
 
@@ -164,17 +162,16 @@ def tile_moe_two_mlp_relu_kernel(tc, xT, w1_words, w1_scales, w2_words, w2_scale
         load_w1_scales(1)
         load_w1(2)
         load_scales(w2s, w2_scales)
-        nc.sync.dma_start(out=w2w[:].bitcast(I32), in_=w2_words.rearrange("e s p b -> p (e s) b").bitcast(I32))
+        nc.sync.dma_start(dst_t[:], dst)
         quantise(1)
 
         gather_bytes("first", 0, C)
         gather_words(1, 0, C)
         gather_bytes("middle", C, C + PAIR)
         lift("middle", PAIR)
-        nc.sync.dma_start(dst_t[:], dst)
-        load_gate(0)
-        load_w1_scales(2)
+        nc.sync.dma_start(out=w2w[:].bitcast(I32), in_=w2_words.rearrange("e s p b -> p (e s) b").bitcast(I32))
         load_w1(3)
+        load_gate(0)
         gather_words(1, C, C)
         gather_words(1, PAIR, PAIR)
         gather_bytes("late", 2 * PAIR, 2 * PAIR)
@@ -212,23 +209,21 @@ def tile_moe_two_mlp_relu_kernel(tc, xT, w1_words, w1_scales, w2_words, w2_scale
             hqs[e] = tile(f"hqs{e}", [P, C], U8)
             nc.vector.quantize_mx(out=hq[e][:].bitcast(FP8X4), scales=hqs[e][:], in_=hg[:].rearrange("p c t -> p (c t)"))
 
-        def second(experts, bank):
-            lo, w = C * experts[0], C * len(experts)
-            y = psum.tile([P, len(experts), C], F32, name=f"y{lo}", tag=bank)
-            for b, e in enumerate(experts):
-                nc.tensor.matmul_mx(
-                    out=y[:, b, :],
-                    lhsT=w2w[:, e, :].bitcast(FP4X4),
-                    lhsT_scale=w2s[:, e, :],
-                    rhs=hq[e][:].bitcast(FP8X4),
-                    rhs_scale=hqs[e][:],
-                    start=True,
-                    stop=True,
-                )
-            ys = tile(f"ys{lo}", [P, w], F32)
-            nc.scalar.copy(ys[:], y[:].rearrange("p b c -> p (b c)"))
-            half, at = divmod(lo, T // 2)
-            nc.vector.tensor_tensor(out_t[:].indirect(dst_t[:, lo // 16 : (lo + w) // 16]), ys[:], gates[half][:, at : at + w], MULT)
+        def second(e, bank):
+            y = psum.tile([P, C], F32, name=f"y{e}", tag=bank)
+            nc.tensor.matmul_mx(
+                out=y[:],
+                lhsT=w2w[:, e, :].bitcast(FP4X4),
+                lhsT_scale=w2s[:, e, :],
+                rhs=hq[e][:].bitcast(FP8X4),
+                rhs_scale=hqs[e][:],
+                start=True,
+                stop=True,
+            )
+            ys = tile(f"ys{e}", [P, C], F32)
+            nc.scalar.copy(ys[:], y[:])
+            half, at = divmod(C * e, T // 2)
+            nc.vector.tensor_tensor(out_t[:].indirect(dst_t[:, C * e // 16 : C * (e + 1) // 16]), ys[:], gates[half][:, at : at + C], MULT)
 
         for e in range(E):
             if e == E - 2:
@@ -237,8 +232,8 @@ def tile_moe_two_mlp_relu_kernel(tc, xT, w1_words, w1_scales, w2_words, w2_scale
             if e >= 1:
                 turn(e - 1)
             if e >= 2:
-                second((e - 2,), f"sums0_{e % AHEAD}")
+                second(e - 2, f"sums0_{e % AHEAD}")
         turn(E - 1)
-        second((E - 2,), f"turn{(E - 1) % 2}")
-        second((E - 1,), f"turn{E % 2}")
+        second(E - 2, f"turn{(E - 1) % 2}")
+        second(E - 1, f"turn{E % 2}")
         nc.sync.dma_start(out=out, in_=out_t[:])

@@ -20,20 +20,17 @@ MULT = mybir.AluOpType.mult
 P = 128
 PASSES = K // 512
 LIFT = 4
-WIDE, NARROW = 512, 256
-LOADS = (
-    ((WIDE, NARROW), (WIDE,), (NARROW, NARROW), (NARROW,)),
-    ((NARROW,), (WIDE,), (WIDE,), (NARROW, NARROW), (NARROW,)),
-)
+LOADS = ((768, 512, 512, 256), (256,) * 8)
+PIECES = ((512, 256, 512, 256, 256, 256), (512, 512, 512, 256, 256))
 WORD_LOADS = ((0, 1), (1, 2), (2, 4), (4, 6), (6, 8))
 SCALE_LOADS = ((0, 2), (2, 8))
 PAIR = 2 * C
 AHEAD = 3
-HELD = 2
+HELD = 3
 
 
 def vector_share(s, start, width):
-    if s == 0 or start >= T - 3 * NARROW:
+    if s == 0 or start >= T - 256:
         return width // 2
     return 0
 
@@ -69,7 +66,7 @@ def tile_moe_two_mlp_relu_kernel(tc, xT, w1_words, w1_scales, w2_words, w2_scale
         raw, w1w, w1_planes, gates = {}, {}, {}, {}
 
         def load_x(s, c):
-            start, width = sum(map(sum, LOADS[s][:c])), sum(LOADS[s][c])
+            start, width = sum(LOADS[s][:c]), LOADS[s][c]
             raw[s, c] = tile(f"raw{s}_{c}", [P, 4, width], F32)
             nc.sync.dma_start(out=raw[s, c][:], in_=xT[512 * s : 512 * s + 512, start : start + width].rearrange("(p j) w -> p j w", j=4))
 
@@ -110,19 +107,22 @@ def tile_moe_two_mlp_relu_kernel(tc, xT, w1_words, w1_scales, w2_words, w2_scale
 
         def quantise(s):
             start = 0
-            for c, pieces in enumerate(LOADS[s]):
-                at = 0
-                for width in pieces:
-                    share = vector_share(s, start, width)
-                    grouped = tile(f"grouped{s}_{start}", [P, width, 4], BF16)
-                    cast(nc.vector.tensor_copy, grouped, raw[s, c][:, :, at : at + width], 0, share)
-                    cast(nc.scalar.copy, grouped, raw[s, c][:, :, at : at + width], share, width)
-                    nc.vector.quantize_mx(
-                        out=words[s][:, start : start + width].bitcast(FP8X4),
-                        scales=plane[LIFT * (1 - s) : P, start : start + width],
-                        in_=grouped[:].rearrange("p w j -> p (w j)"),
-                    )
-                    at, start = at + width, start + width
+            for width in PIECES[s]:
+                grouped = tile(f"grouped{s}_{start}", [P, width, 4], BF16)
+                for c, load_width in enumerate(LOADS[s]):
+                    load_start = sum(LOADS[s][:c])
+                    lo, hi = max(start, load_start), min(start + width, load_start + load_width)
+                    if lo < hi:
+                        share = vector_share(s, lo, hi - lo)
+                        part, source = grouped[:, lo - start : hi - start, :], raw[s, c][:, :, lo - load_start : hi - load_start]
+                        cast(nc.vector.tensor_copy, part, source, 0, share)
+                        cast(nc.scalar.copy, part, source, share, hi - lo)
+                nc.vector.quantize_mx(
+                    out=words[s][:, start : start + width].bitcast(FP8X4),
+                    scales=plane[LIFT * (1 - s) : P, start : start + width],
+                    in_=grouped[:].rearrange("p w j -> p (w j)"),
+                )
+                start = start + width
 
         slot_words, slot_bytes, slot_scales, hs, hq, hqs = {}, {}, {}, {}, {}, {}
 
@@ -176,7 +176,6 @@ def tile_moe_two_mlp_relu_kernel(tc, xT, w1_words, w1_scales, w2_words, w2_scale
         gather_words(1, PAIR, PAIR)
         gather_bytes("late", 2 * PAIR, 2 * PAIR)
         lift("late", 2 * PAIR)
-        gather_words(1, 2 * PAIR, PAIR)
         load_w1(4)
         load_gate(1)
 
@@ -226,8 +225,8 @@ def tile_moe_two_mlp_relu_kernel(tc, xT, w1_words, w1_scales, w2_words, w2_scale
             nc.vector.tensor_tensor(out_t[:].indirect(dst_t[:, C * e // 16 : C * (e + 1) // 16]), ys[:], gates[half][:, at : at + C], MULT)
 
         for e in range(E):
-            if e == E - 2:
-                gather_words(1, C * e, PAIR, "hg0")
+            if e in (E - 4, E - 2):
+                gather_words(1, C * e, PAIR, f"hg{(e - E + 4) // 2}")
             first(e)
             if e >= 1:
                 turn(e - 1)

@@ -20,8 +20,8 @@ MULT = mybir.AluOpType.mult
 P = 128
 PASSES = K // 512
 LIFT = 4
-LOADS = ((768, 512, 512, 256), (256,) * 8)
-PIECES = ((512, 256, 512, 256, 256, 256), (512, 512, 512, 256, 256))
+LOADS = ((768, 512, 384, 256, 128), (256,) * 8)
+PIECES = ((512, 256, 256, 256, 256, 128, 256, 128), (512, 512, 512, 256, 256))
 WORD_LOADS = ((0, 1), (1, 2), (2, 4), (4, 6), (6, 8))
 SCALE_LOADS = ((0, 2), (2, 8))
 PAIR = 2 * C
@@ -30,7 +30,7 @@ HELD = 3
 
 
 def vector_share(s, start, width):
-    if s == 0 or start >= T - 256:
+    if s == 0 or start >= T - 512:
         return width // 2
     return 0
 

@@ -20,17 +20,17 @@ MULT = mybir.AluOpType.mult
 P = 128
 PASSES = K // 512
 LIFT = 4
-LOADS = ((768, 512, 384, 256, 128), (256,) * 8)
-PIECES = ((512, 256, 256, 256, 256, 128, 256, 128), (512, 512, 512, 256, 256))
-WORD_LOADS = ((0, 1), (1, 2), (2, 4), (4, 6), (6, 8))
+LOADS = ((768, 512, 384, 256, 128), (256,) * 7 + (128, 128))
+PIECES = ((512, 256, 256, 256, 256, 128, 256, 128), (512, 512, 512, 256, 128, 128))
+WORD_LOADS = ((0, 1), (1, 2), (2, 4), (4, 8))
 SCALE_LOADS = ((0, 2), (2, 8))
 PAIR = 2 * C
 AHEAD = 3
-HELD = 3
+HELD = 4
 
 
 def vector_share(s, start, width):
-    if s == 0 or start >= T - 512:
+    if s == 0 or start in (T - 512, T - 128):
         return width // 2
     return 0
 
@@ -163,20 +163,19 @@ def tile_moe_two_mlp_relu_kernel(tc, xT, w1_words, w1_scales, w2_words, w2_scale
         load_w1(2)
         load_scales(w2s, w2_scales)
         nc.sync.dma_start(dst_t[:], dst)
+        nc.sync.dma_start(out=w2w[:].bitcast(I32), in_=w2_words.rearrange("e s p b -> p (e s) b").bitcast(I32))
         quantise(1)
 
         gather_bytes("first", 0, C)
         gather_words(1, 0, C)
         gather_bytes("middle", C, C + PAIR)
         lift("middle", PAIR)
-        nc.sync.dma_start(out=w2w[:].bitcast(I32), in_=w2_words.rearrange("e s p b -> p (e s) b").bitcast(I32))
         load_w1(3)
         load_gate(0)
         gather_words(1, C, C)
         gather_words(1, PAIR, PAIR)
         gather_bytes("late", 2 * PAIR, 2 * PAIR)
         lift("late", 2 * PAIR)
-        load_w1(4)
         load_gate(1)
 
         def first(e):

@@ -21,18 +21,20 @@ P = 128
 PASSES = K // 512
 LIFT = 4
 LOADS = ((768, 512, 384, 256, 128), (256,) * 7 + (128, 128))
-PIECES = ((512, 256, 256, 256, 256, 128, 256, 128), (512, 512, 512, 256, 128, 128))
+PIECES = ((512, 256, 256, 256, 256, 128, 256, 128), (1024, 512, 256, 128, 128))
 WORD_LOADS = ((0, 1), (1, 2), (2, 4), (4, 8))
 SCALE_LOADS = ((0, 2), (2, 8))
 PAIR = 2 * C
+HELD_PAIRS = 2
 AHEAD = 3
 HELD = 4
 
 
-def vector_share(s, start, width):
-    if s == 0 or start in (T - 512, T - 128):
+def vector_share(s, c, width):
+    if s == 0:
         return width // 2
-    return 0
+    loads_behind = len(LOADS[s]) - 1 - c
+    return {2: width // 4, 0: width // 2}.get(loads_behind, 0)
 
 
 def tile_moe_two_mlp_relu_kernel(tc, xT, w1_words, w1_scales, w2_words, w2_scales, gate, offs, dst, out):
@@ -113,8 +115,9 @@ def tile_moe_two_mlp_relu_kernel(tc, xT, w1_words, w1_scales, w2_words, w2_scale
                     load_start = sum(LOADS[s][:c])
                     lo, hi = max(start, load_start), min(start + width, load_start + load_width)
                     if lo < hi:
-                        share = vector_share(s, lo, hi - lo)
-                        part, source = grouped[:, lo - start : hi - start, :], raw[s, c][:, :, lo - load_start : hi - load_start]
+                        share = vector_share(s, c, hi - lo)
+                        part = grouped[:, lo - start : hi - start, :]
+                        source = raw[s, c][:, :, lo - load_start : hi - load_start]
                         cast(nc.vector.tensor_copy, part, source, 0, share)
                         cast(nc.scalar.copy, part, source, share, hi - lo)
                 nc.vector.quantize_mx(
@@ -122,7 +125,7 @@ def tile_moe_two_mlp_relu_kernel(tc, xT, w1_words, w1_scales, w2_words, w2_scale
                     scales=plane[LIFT * (1 - s) : P, start : start + width],
                     in_=grouped[:].rearrange("p w j -> p (w j)"),
                 )
-                start = start + width
+                start += width
 
         slot_words, slot_bytes, slot_scales, hs, hq, hqs = {}, {}, {}, {}, {}, {}
 
@@ -224,8 +227,9 @@ def tile_moe_two_mlp_relu_kernel(tc, xT, w1_words, w1_scales, w2_words, w2_scale
             nc.vector.tensor_tensor(out_t[:].indirect(dst_t[:, C * e // 16 : C * (e + 1) // 16]), ys[:], gates[half][:, at : at + C], MULT)
 
         for e in range(E):
-            if e in (E - 4, E - 2):
-                gather_words(1, C * e, PAIR, f"hg{(e - E + 4) // 2}")
+            held_pair = e // 2 - (E // 2 - HELD_PAIRS)
+            if e % 2 == 0 and held_pair >= 0:
+                gather_words(1, C * e, PAIR, f"hg{held_pair}")
             first(e)
             if e >= 1:
                 turn(e - 1)

@@ -103,8 +103,8 @@ def tile_moe_two_mlp_relu_kernel(tc, xT, w1_words, w1_scales, w2_words, w2_scale
         def cast(engine, grouped, source, lo, hi):
             if hi > lo:
                 engine(
-                    grouped[:, lo:hi, :].rearrange("p (b i) j -> p b j i", i=2),
-                    source[:, :, lo:hi].rearrange("p j (b i) -> p b j i", i=2),
+                    grouped[:, lo:hi, :].rearrange("p (b i) j -> p b j i", i=4),
+                    source[:, :, lo:hi].rearrange("p j (b i) -> p b j i", i=4),
                 )
 
         def quantise(s):

@@ -15,19 +15,22 @@ U8 = mybir.dt.uint8
 FP8X4 = mybir.dt.float8_e4m3fn_x4
 FP4X4 = mybir.dt.float4_e2m1fn_x4
 RELU = mybir.ActivationFunctionType.Relu
+COPY = mybir.ActivationFunctionType.Copy
 MULT = mybir.AluOpType.mult
+ADD = mybir.AluOpType.add
 
 P = 128
 PASSES = K // 512
 LIFT = 4
 LOADS = ((768, 512, 384, 256, 128), (256,) * 7 + (128, 128))
 PIECES = ((512, 256, 256, 256, 256, 128, 256, 128), (1024, 512, 256, 128, 128))
-WORD_LOADS = ((0, 1), (1, 2), (2, 4), (4, 8))
+WORD_LOADS = ((2, 4), (4, 8))
 SCALE_LOADS = ((0, 2), (2, 8))
 PAIR = 2 * C
-HELD_PAIRS = 2
-AHEAD = 3
 HELD = 4
+VECTOR_SCATTERS = ((0, 512), (1024, 1280), (1280, 1664))
+SCALAR_SCATTERS = ((512, 768), (768, 1024), (1664, 2048))
+STORES = (256, 512, 512, 512, 256)
 
 
 def vector_share(s, c, width):
@@ -55,14 +58,17 @@ def tile_moe_two_mlp_relu_kernel(tc, xT, w1_words, w1_scales, w2_words, w2_scale
         w1s = [tile(f"w1s{lo}", [P, (hi - lo) * PASSES, H], U8) for lo, hi in SCALE_LOADS]
         w2w = tile("w2w", [P, E, 2 * N], U8)
         w2s = tile("w2s", [P, E, N], U8)
-        out_t = tile("out_t", [P, T], F32)
         ident = tile("ident", [P, P], F32)
-        lifted = {lo: tile(f"lifted{lo}", [P, w], U8) for lo, w in [(0, PAIR), (PAIR, PAIR), (2 * PAIR, 2 * PAIR)]}
+        lifted = {lo: tile(f"lifted{lo}", [P, w], U8) for lo, w in [(0, 3 * C), (3 * C, 2 * C), (5 * C, 3 * C)]}
+        vector_window = tile("vector_window", [P, T], F32)
+        scalar_window = tile("scalar_window", [P, T], F32)
 
-        for weights_plane in w1s + [w2s]:
-            nc.vector.memset(weights_plane[:].rearrange("p a b -> p (a b)").bitcast(I32), 0)
         for tokens_plane in [plane] + list(lifted.values()):
             nc.vector.memset(tokens_plane[:].bitcast(I32), 0)
+        for weights_plane in w1s + [w2s]:
+            nc.vector.memset(weights_plane[:].rearrange("p a b -> p (a b)").bitcast(I32), 0)
+        nc.gpsimd.memset(vector_window[:], 0.0)
+        nc.scalar.copy(scalar_window[:], vector_window[:])
         make_identity(nc, ident[:])
 
         raw, w1w, w1_planes, gates = {}, {}, {}, {}
@@ -77,7 +83,19 @@ def tile_moe_two_mlp_relu_kernel(tc, xT, w1_words, w1_scales, w2_words, w2_scale
             piece = tile(f"w1w{lo}", [P, (hi - lo) * PASSES, 2 * H], U8)
             nc.sync.dma_start(out=piece[:].bitcast(I32), in_=w1_words[lo:hi].rearrange("e s p b -> p (e s) b").bitcast(I32))
             for e in range(lo, hi):
-                w1w[e] = piece[:, PASSES * (e - lo) : PASSES * (e - lo + 1), :]
+                for s in range(PASSES):
+                    w1w[e, s] = piece[:, PASSES * (e - lo) + s, :]
+
+        def load_first_pair(s):
+            piece = tile(f"w1w_first{s}", [P, 2, 2 * H], U8)
+            nc.sync.dma_start(out=piece[:].bitcast(I32), in_=w1_words[0:2, s].rearrange("e p b -> p e b").bitcast(I32))
+            for e in range(2):
+                w1w[e, s] = piece[:, e, :]
+
+        def load_scales(weights_plane, source):
+            rows = source.rearrange("e s (q r) i -> r q (e s) i", r=4)
+            for r in range(4):
+                nc.sync.dma_start(out=weights_plane[r:P:32, :, :].bitcast(I32), in_=rows[r].bitcast(I32))
 
         def load_w1_scales(n):
             lo, hi = SCALE_LOADS[n]
@@ -85,14 +103,11 @@ def tile_moe_two_mlp_relu_kernel(tc, xT, w1_words, w1_scales, w2_words, w2_scale
             for e in range(lo, hi):
                 w1_planes[e] = w1s[n][:, PASSES * (e - lo) : PASSES * (e - lo + 1), :]
 
-        def load_gate(half):
-            gates[half] = tile(f"gate{half}", [P, T // 2], F32)
-            nc.sync.dma_start(out=gates[half][:], in_=gate[:, half * T // 2 : (half + 1) * T // 2])
-
-        def load_scales(weights_plane, source):
-            rows = source.rearrange("e s (q r) i -> r q (e s) i", r=4)
-            for r in range(4):
-                nc.sync.dma_start(out=weights_plane[r:P:32, :, :].bitcast(I32), in_=rows[r].bitcast(I32))
+        def load_gate(lo, hi):
+            piece = tile(f"gate{lo}", [P, (hi - lo) * PAIR], F32)
+            nc.sync.dma_start(out=piece[:], in_=gate[:, lo * PAIR : hi * PAIR])
+            for pair in range(lo, hi):
+                gates[pair] = piece[:, (pair - lo) * PAIR : (pair - lo + 1) * PAIR]
 
         for c in range(len(LOADS[0])):
             load_x(0, c)
@@ -127,10 +142,10 @@ def tile_moe_two_mlp_relu_kernel(tc, xT, w1_words, w1_scales, w2_words, w2_scale
                 )
                 start += width
 
-        slot_words, slot_bytes, slot_scales, hs, hq, hqs = {}, {}, {}, {}, {}, {}
+        slot_words, slot_bytes, slot_scales, hs, hg, hq, hqs = {}, {}, {}, {}, {}, {}, {}
 
-        def gather_words(s, lo, w, tag=None):
-            piece = tile(f"slot_words{s}_{lo}", [P, w], U32, tag)
+        def gather_words(s, lo, w):
+            piece = tile(f"slot_words{s}_{lo}", [P, w], U32)
             nc.vector.tensor_copy(piece[:], words[s][:].indirect(offs_t[:, lo // 16 : (lo + w) // 16]))
             for at in range(0, w, P):
                 slot_words[s, lo + at] = piece[:, at : at + P]
@@ -153,89 +168,130 @@ def tile_moe_two_mlp_relu_kernel(tc, xT, w1_words, w1_scales, w2_words, w2_scale
                 slot_scales[0, lo + at] = lifted[lo][:, at : at + P]
 
         quantise(0)
-        gather_bytes("early", 0, PAIR)
+        gather_bytes("early", 0, 3 * C)
         lift("early", 0)
         for c in range(len(LOADS[1]) - HELD, len(LOADS[1])):
             load_x(1, c)
         for lo in range(0, T, T // 2):
             gather_words(0, lo, T // 2)
         load_w1_scales(0)
+        load_first_pair(0)
+        load_first_pair(1)
+        load_w1_scales(1)
         load_w1(0)
         load_w1(1)
-        load_w1_scales(1)
-        load_w1(2)
-        load_scales(w2s, w2_scales)
-        nc.sync.dma_start(dst_t[:], dst)
-        nc.sync.dma_start(out=w2w[:].bitcast(I32), in_=w2_words.rearrange("e s p b -> p (e s) b").bitcast(I32))
         quantise(1)
 
-        gather_bytes("first", 0, C)
+        gather_bytes("first", 0, PAIR)
         gather_words(1, 0, C)
-        gather_bytes("middle", C, C + PAIR)
-        lift("middle", PAIR)
-        load_w1(3)
-        load_gate(0)
         gather_words(1, C, C)
-        gather_words(1, PAIR, PAIR)
-        gather_bytes("late", 2 * PAIR, 2 * PAIR)
-        lift("late", 2 * PAIR)
-        load_gate(1)
+        gather_bytes("third", 2 * C, 3 * C)
+        lift("third", 3 * C)
+        load_scales(w2s, w2_scales)
+        nc.sync.dma_start(out=w2w[:].bitcast(I32), in_=w2_words.rearrange("e s p b -> p (e s) b").bitcast(I32))
+        nc.sync.dma_start(dst_t[:], dst)
+        load_gate(0, 1)
+        gather_words(1, 2 * C, C)
+        gather_words(1, 3 * C, C)
+        gather_bytes("fourth", 5 * C, 3 * C)
+        lift("fourth", 5 * C)
+        load_gate(1, 4)
+        gather_words(1, 2 * PAIR, PAIR)
+        gather_words(1, 3 * PAIR, PAIR)
 
-        def first(e):
-            hs[e] = tile(f"hs{e}", [P, 2, 2, P, 2], BF16, f"hs{e % 2}")
-            for b in range(2):
-                acc = psum.tile([P, H], F32, name=f"acc{e}_{b}", tag=f"sums{b}_{e % AHEAD}")
-                for s in range(PASSES):
-                    nc.tensor.matmul_mx(
-                        out=acc[:],
-                        lhsT=slot_words[s, C * e + P * b].bitcast(FP8X4),
-                        lhsT_scale=slot_scales[s, C * e + P * b],
-                        rhs=w1w[e][:, s, :].bitcast(FP4X4),
-                        rhs_scale=w1_planes[e][:, s, :],
-                        start=(s == 0),
-                        stop=(s == PASSES - 1),
-                    )
-                nc.scalar.activation(hs[e][:, b], acc[:].rearrange("c (p u v) -> c u p v", u=2, v=2), RELU)
+        gated = tile("gated", [P, T], F32, "raw0_1")
 
-        def turn(e):
-            hg = tile(f"hg{e}", [P, C, 4], BF16)
-            hg_words = hg[:].rearrange("p c t -> p (c t)").bitcast(F32).rearrange("p (c u) -> p c u", u=2)
+        sums = {}
+
+        def product(e, b, s):
+            if s == 0:
+                sums[e, b] = psum.tile([P, H], F32, name=f"acc{e}_{b}", tag=(f"lower{e % 4}", f"upper{e % 3}")[b])
+            nc.tensor.matmul_mx(
+                out=sums[e, b][:],
+                lhsT=slot_words[s, C * e + P * b].bitcast(FP8X4),
+                lhsT_scale=slot_scales[s, C * e + P * b],
+                rhs=w1w[e, s].bitcast(FP4X4),
+                rhs_scale=w1_planes[e][:, s, :],
+                start=(s == 0),
+                stop=(s == PASSES - 1),
+            )
+
+        def first(e, b):
+            if b == 0:
+                hs[e] = tile(f"hs{e}", [P, 2, 2, P, 2], BF16, f"hs{e % 3}")
+            for s in range(1 if e < 2 else 0, PASSES):
+                product(e, b, s)
+            nc.scalar.activation(hs[e][:, b], sums[e, b][:].rearrange("c (p u v) -> c u p v", u=2, v=2), RELU)
+
+        def turn(e, bank):
+            pair, side = divmod(e, 2)
+            if side == 0:
+                hg[pair] = tile(f"hg{pair}", [P, PAIR, 4], BF16)
+            part = hg[pair][:, C * side : C * side + C, :]
+            hg_words = part.rearrange("p c t -> p (c t)").bitcast(F32).rearrange("p (c u) -> p c u", u=2)
             hs_words = hs[e][:].rearrange("c b u p v -> c b u (p v)").bitcast(F32)
-            turned = psum.tile([P, 2, C], F32, name=f"turned{e}", tag=f"turn{e % 2}")
+            turned = psum.tile([P, 2, C], F32, name=f"turned{e}", tag=bank)
             for b in range(2):
                 for u in range(2):
                     nc.tensor.transpose(turned[:, u, P * b : P * b + P], hs_words[:, b, u, :], ident[:])
             nc.scalar.copy(hg_words, turned[:].rearrange("p u r -> p r u"))
-            hq[e] = tile(f"hq{e}", [P, C], U32)
-            hqs[e] = tile(f"hqs{e}", [P, C], U8)
-            nc.vector.quantize_mx(out=hq[e][:].bitcast(FP8X4), scales=hqs[e][:], in_=hg[:].rearrange("p c t -> p (c t)"))
 
-        def second(e, bank):
-            y = psum.tile([P, C], F32, name=f"y{e}", tag=bank)
-            nc.tensor.matmul_mx(
-                out=y[:],
-                lhsT=w2w[:, e, :].bitcast(FP4X4),
-                lhsT_scale=w2s[:, e, :],
-                rhs=hq[e][:].bitcast(FP8X4),
-                rhs_scale=hqs[e][:],
-                start=True,
-                stop=True,
-            )
-            ys = tile(f"ys{e}", [P, C], F32)
-            nc.scalar.copy(ys[:], y[:])
-            half, at = divmod(C * e, T // 2)
-            nc.vector.tensor_tensor(out_t[:].indirect(dst_t[:, C * e // 16 : C * (e + 1) // 16]), ys[:], gates[half][:, at : at + C], MULT)
+        def quantise_h(pair):
+            hq[pair] = tile(f"hq{pair}", [P, PAIR], U32)
+            hqs[pair] = tile(f"hqs{pair}", [P, PAIR], U8)
+            nc.vector.quantize_mx(out=hq[pair][:].bitcast(FP8X4), scales=hqs[pair][:], in_=hg[pair][:].rearrange("p c t -> p (c t)"))
 
+        def second(pair, bank):
+            y = psum.tile([P, PAIR], F32, name=f"y{pair}", tag=bank)
+            for side in range(2):
+                e, cols = 2 * pair + side, slice(C * side, C * side + C)
+                nc.tensor.matmul_mx(
+                    out=y[:, cols],
+                    lhsT=w2w[:, e, :].bitcast(FP4X4),
+                    lhsT_scale=w2s[:, e, :],
+                    rhs=hq[pair][:, cols].bitcast(FP8X4),
+                    rhs_scale=hqs[pair][:, cols],
+                    start=True,
+                    stop=True,
+                )
+            nc.vector.tensor_tensor(gated[:, PAIR * pair : PAIR * pair + PAIR], y[:], gates[pair], MULT)
+
+        def scatter_on_vector(n):
+            lo, hi = VECTOR_SCATTERS[n]
+            nc.vector.tensor_copy(vector_window[:].indirect(dst_t[:, lo // 16 : hi // 16]), gated[:, lo:hi])
+
+        def scatter_on_scalar(n):
+            lo, hi = SCALAR_SCATTERS[n]
+            nc.scalar.activation(scalar_window[:].indirect(dst_t[:, lo // 16 : hi // 16]), gated[:, lo:hi], COPY)
+
+        for e in range(2):
+            for b in range(2):
+                product(e, b, 0)
         for e in range(E):
-            held_pair = e // 2 - (E // 2 - HELD_PAIRS)
-            if e % 2 == 0 and held_pair >= 0:
-                gather_words(1, C * e, PAIR, f"hg{held_pair}")
-            first(e)
-            if e >= 1:
-                turn(e - 1)
+            first(e, 0)
             if e >= 2:
-                second(e - 2, f"sums0_{e % AHEAD}")
-        turn(E - 1)
-        second(E - 2, f"turn{(E - 1) % 2}")
-        second(E - 1, f"turn{E % 2}")
-        nc.sync.dma_start(out=out, in_=out_t[:])
+                turn(e - 2, f"lower{(e - 1) % 4}")
+            first(e, 1)
+            if e >= 3 and e % 2 == 1:
+                quantise_h(e // 2 - 1)
+            if e == 4:
+                second(0, "upper1")
+                scatter_on_vector(0)
+        turn(E - 2, "lower3")
+        turn(E - 1, "spare")
+        quantise_h(E // 2 - 1)
+        second(1, "upper1")
+        second(2, "lower3")
+        scatter_on_vector(1)
+        second(3, "upper0")
+        scatter_on_vector(2)
+        for n in range(len(SCALAR_SCATTERS)):
+            scatter_on_scalar(n)
+
+        start = 0
+        for n, width in enumerate(STORES):
+            cols = slice(start, start + width)
+            result = tile(f"result{start}", [P, width], F32, f"raw1_{n}")
+            nc.vector.tensor_tensor(result[:], vector_window[:, cols], scalar_window[:, cols], ADD)
+            nc.sync.dma_start(out=out[:, cols], in_=result[:])
+            start += width

@@ -24,13 +24,18 @@ PASSES = K // 512
 LIFT = 4
 LOADS = ((768, 512, 384, 256, 128), (256,) * 7 + (128, 128))
 PIECES = ((512, 256, 256, 256, 256, 128, 256, 128), (1024, 512, 256, 128, 128))
-WORD_LOADS = ((2, 4), (4, 8))
+WORD_LOADS = ((2, 4), (4, 6), (6, 8))
 SCALE_LOADS = ((0, 2), (2, 8))
 PAIR = 2 * C
 HELD = 4
-VECTOR_SCATTERS = ((0, 512), (1024, 1280), (1280, 1664))
-SCALAR_SCATTERS = ((512, 768), (768, 1024), (1664, 2048))
-STORES = (256, 512, 512, 512, 256)
+VECTOR_SCATTERS = ((1664, 2048),)
+SCALAR_SCATTERS = ((1024, 1344), (1344, 1664))
+GROUPS = ((0, 1), (1, 2), (2, 3), (3, 4), (4, 5), (5, 6), (6, 8))
+STORES = (256, 640, 640, 384, 128)
+
+
+def group_of(e):
+    return [group for group in GROUPS if group[0] <= e][-1]
 
 
 def vector_share(s, c, width):
@@ -63,10 +68,7 @@ def tile_moe_two_mlp_relu_kernel(tc, xT, w1_words, w1_scales, w2_words, w2_scale
         vector_window = tile("vector_window", [P, T], F32)
         scalar_window = tile("scalar_window", [P, T], F32)
 
-        for tokens_plane in [plane] + list(lifted.values()):
-            nc.vector.memset(tokens_plane[:].bitcast(I32), 0)
-        for weights_plane in w1s + [w2s]:
-            nc.vector.memset(weights_plane[:].rearrange("p a b -> p (a b)").bitcast(I32), 0)
+        nc.vector.memset(plane[:].bitcast(I32), 0)
         nc.gpsimd.memset(vector_window[:], 0.0)
         nc.scalar.copy(scalar_window[:], vector_window[:])
         make_identity(nc, ident[:])
@@ -104,10 +106,9 @@ def tile_moe_two_mlp_relu_kernel(tc, xT, w1_words, w1_scales, w2_words, w2_scale
                 w1_planes[e] = w1s[n][:, PASSES * (e - lo) : PASSES * (e - lo + 1), :]
 
         def load_gate(lo, hi):
-            piece = tile(f"gate{lo}", [P, (hi - lo) * PAIR], F32)
-            nc.sync.dma_start(out=piece[:], in_=gate[:, lo * PAIR : hi * PAIR])
-            for pair in range(lo, hi):
-                gates[pair] = piece[:, (pair - lo) * PAIR : (pair - lo + 1) * PAIR]
+            piece = tile(f"gate{lo}", [P, (hi - lo) * C], F32)
+            nc.sync.dma_start(out=piece[:], in_=gate[:, lo * C : hi * C])
+            gates[lo] = piece
 
         for c in range(len(LOADS[0])):
             load_x(0, c)
@@ -144,8 +145,8 @@ def tile_moe_two_mlp_relu_kernel(tc, xT, w1_words, w1_scales, w2_words, w2_scale
 
         slot_words, slot_bytes, slot_scales, hs, hg, hq, hqs = {}, {}, {}, {}, {}, {}, {}
 
-        def gather_words(s, lo, w):
-            piece = tile(f"slot_words{s}_{lo}", [P, w], U32)
+        def gather_words(s, lo, w, tag=None):
+            piece = tile(f"slot_words{s}_{lo}", [P, w], U32, tag)
             nc.vector.tensor_copy(piece[:], words[s][:].indirect(offs_t[:, lo // 16 : (lo + w) // 16]))
             for at in range(0, w, P):
                 slot_words[s, lo + at] = piece[:, at : at + P]
@@ -180,26 +181,30 @@ def tile_moe_two_mlp_relu_kernel(tc, xT, w1_words, w1_scales, w2_words, w2_scale
         load_w1_scales(1)
         load_w1(0)
         load_w1(1)
+        load_scales(w2s, w2_scales)
+        nc.sync.dma_start(out=w2w[:].bitcast(I32), in_=w2_words.rearrange("e s p b -> p (e s) b").bitcast(I32))
+        nc.sync.dma_start(dst_t[:], dst)
+        load_gate(0, 2)
         quantise(1)
 
         gather_bytes("first", 0, PAIR)
         gather_words(1, 0, C)
         gather_words(1, C, C)
-        gather_bytes("third", 2 * C, 3 * C)
-        lift("third", 3 * C)
-        load_scales(w2s, w2_scales)
-        nc.sync.dma_start(out=w2w[:].bitcast(I32), in_=w2_words.rearrange("e s p b -> p (e s) b").bitcast(I32))
-        nc.sync.dma_start(dst_t[:], dst)
-        load_gate(0, 1)
+        gather_bytes("second", 2 * C, 3 * C)
+        lift("second", 3 * C)
         gather_words(1, 2 * C, C)
         gather_words(1, 3 * C, C)
-        gather_bytes("fourth", 5 * C, 3 * C)
-        lift("fourth", 5 * C)
-        load_gate(1, 4)
+        gather_bytes("third", 5 * C, 3 * C)
+        lift("third", 5 * C)
+        load_w1(2)
+        load_gate(2, E)
         gather_words(1, 2 * PAIR, PAIR)
-        gather_words(1, 3 * PAIR, PAIR)
 
-        gated = tile("gated", [P, T], F32, "raw0_1")
+        gated_tiles, ys = {}, {}
+
+        def gated(lo, hi):
+            first_slot = max(at for at in gated_tiles if at <= lo)
+            return gated_tiles[first_slot][:, lo - first_slot : hi - first_slot]
 
         sums = {}
 
@@ -224,10 +229,10 @@ def tile_moe_two_mlp_relu_kernel(tc, xT, w1_words, w1_scales, w2_words, w2_scale
             nc.scalar.activation(hs[e][:, b], sums[e, b][:].rearrange("c (p u v) -> c u p v", u=2, v=2), RELU)
 
         def turn(e, bank):
-            pair, side = divmod(e, 2)
-            if side == 0:
-                hg[pair] = tile(f"hg{pair}", [P, PAIR, 4], BF16)
-            part = hg[pair][:, C * side : C * side + C, :]
+            lo, hi = group_of(e)
+            if e == lo:
+                hg[lo] = tile(f"hg{lo}", [P, (hi - lo) * C, 4], BF16)
+            part = hg[lo][:, C * (e - lo) : C * (e - lo + 1), :]
             hg_words = part.rearrange("p c t -> p (c t)").bitcast(F32).rearrange("p (c u) -> p c u", u=2)
             hs_words = hs[e][:].rearrange("c b u p v -> c b u (p v)").bitcast(F32)
             turned = psum.tile([P, 2, C], F32, name=f"turned{e}", tag=bank)
@@ -236,62 +241,95 @@ def tile_moe_two_mlp_relu_kernel(tc, xT, w1_words, w1_scales, w2_words, w2_scale
                     nc.tensor.transpose(turned[:, u, P * b : P * b + P], hs_words[:, b, u, :], ident[:])
             nc.scalar.copy(hg_words, turned[:].rearrange("p u r -> p r u"))
 
-        def quantise_h(pair):
-            hq[pair] = tile(f"hq{pair}", [P, PAIR], U32)
-            hqs[pair] = tile(f"hqs{pair}", [P, PAIR], U8)
-            nc.vector.quantize_mx(out=hq[pair][:].bitcast(FP8X4), scales=hqs[pair][:], in_=hg[pair][:].rearrange("p c t -> p (c t)"))
+        def quantise_h(lo):
+            hi = group_of(lo)[1]
+            codes = tile(f"hq{lo}", [P, (hi - lo) * C], U32)
+            scales = tile(f"hqs{lo}", [P, (hi - lo) * C], U8)
+            nc.vector.quantize_mx(out=codes[:].bitcast(FP8X4), scales=scales[:], in_=hg[lo][:].rearrange("p c t -> p (c t)"))
+            for e in range(lo, hi):
+                hq[e] = codes[:, C * (e - lo) : C * (e - lo + 1)]
+                hqs[e] = scales[:, C * (e - lo) : C * (e - lo + 1)]
 
-        def second(pair, bank):
-            y = psum.tile([P, PAIR], F32, name=f"y{pair}", tag=bank)
-            for side in range(2):
-                e, cols = 2 * pair + side, slice(C * side, C * side + C)
+        def second(lo, hi, bank):
+            y = psum.tile([P, (hi - lo) * C], F32, name=f"y{lo}", tag=bank)
+            for e in range(lo, hi):
                 nc.tensor.matmul_mx(
-                    out=y[:, cols],
+                    out=y[:, C * (e - lo) : C * (e - lo + 1)],
                     lhsT=w2w[:, e, :].bitcast(FP4X4),
                     lhsT_scale=w2s[:, e, :],
-                    rhs=hq[pair][:, cols].bitcast(FP8X4),
-                    rhs_scale=hqs[pair][:, cols],
+                    rhs=hq[e].bitcast(FP8X4),
+                    rhs_scale=hqs[e],
                     start=True,
                     stop=True,
                 )
-            nc.vector.tensor_tensor(gated[:, PAIR * pair : PAIR * pair + PAIR], y[:], gates[pair], MULT)
+                ys[e] = y, lo
+
+        def times_gate(lo, hi):
+            y, first_expert = ys[lo]
+            gate_lo = max(at for at in gates if at <= lo)
+            nc.vector.tensor_tensor(
+                gated(C * lo, C * hi),
+                y[:, C * (lo - first_expert) : C * (hi - first_expert)],
+                gates[gate_lo][:, C * (lo - gate_lo) : C * (hi - gate_lo)],
+                MULT,
+            )
+
+        def copy_out(lo, hi):
+            y, first_expert = ys[lo]
+            nc.scalar.copy(gated(C * lo, C * hi), y[:, C * (lo - first_expert) : C * (hi - first_expert)])
+
+        def scatter_times_gate(e):
+            gate_lo = max(at for at in gates if at <= e)
+            nc.vector.tensor_tensor(
+                vector_window[:].indirect(dst_t[:, C * e // 16 : C * (e + 1) // 16]),
+                gated(C * e, C * (e + 1)),
+                gates[gate_lo][:, C * (e - gate_lo) : C * (e + 1 - gate_lo)],
+                MULT,
+            )
 
         def scatter_on_vector(n):
             lo, hi = VECTOR_SCATTERS[n]
-            nc.vector.tensor_copy(vector_window[:].indirect(dst_t[:, lo // 16 : hi // 16]), gated[:, lo:hi])
+            nc.vector.tensor_copy(vector_window[:].indirect(dst_t[:, lo // 16 : hi // 16]), gated(lo, hi))
 
         def scatter_on_scalar(n):
             lo, hi = SCALAR_SCATTERS[n]
-            nc.scalar.activation(scalar_window[:].indirect(dst_t[:, lo // 16 : hi // 16]), gated[:, lo:hi], COPY)
+            nc.scalar.activation(scalar_window[:].indirect(dst_t[:, lo // 16 : hi // 16]), gated(lo, hi), COPY)
 
         for e in range(2):
             for b in range(2):
                 product(e, b, 0)
+        gated_tiles[0] = tile("gated0", [P, 4 * C], F32)
         for e in range(E):
+            if e == 6:
+                gather_words(1, 3 * PAIR, PAIR, "hg1")
             first(e, 0)
             if e >= 2:
                 turn(e - 2, f"lower{(e - 1) % 4}")
+                if group_of(e - 2)[1] == e - 1:
+                    quantise_h(group_of(e - 2)[0])
             first(e, 1)
-            if e >= 3 and e % 2 == 1:
-                quantise_h(e // 2 - 1)
-            if e == 4:
-                second(0, "upper1")
-                scatter_on_vector(0)
+            if 3 <= e < E - 1:
+                second(e - 3, e - 2, f"upper{e % 3}")
+                copy_out(e - 3, e - 2)
+                scatter_times_gate(e - 3)
         turn(E - 2, "lower3")
         turn(E - 1, "spare")
-        quantise_h(E // 2 - 1)
-        second(1, "upper1")
-        second(2, "lower3")
-        scatter_on_vector(1)
-        second(3, "upper0")
-        scatter_on_vector(2)
+        gated_tiles[4 * C] = tile("gated4", [P, 4 * C], F32, "raw1_0")
+        second(4, 5, "upper1")
+        times_gate(4, 5)
+        second(5, 6, "lower3")
+        times_gate(5, 6)
+        quantise_h(E - 2)
+        second(6, 8, "lower0")
+        times_gate(6, 8)
+        scatter_on_vector(0)
         for n in range(len(SCALAR_SCATTERS)):
             scatter_on_scalar(n)
 
         start = 0
         for n, width in enumerate(STORES):
             cols = slice(start, start + width)
-            result = tile(f"result{start}", [P, width], F32, f"raw1_{n}")
+            result = tile(f"result{start}", [P, width], F32, f"raw0_{n}")
             nc.vector.tensor_tensor(result[:], vector_window[:, cols], scalar_window[:, cols], ADD)
             nc.sync.dma_start(out=out[:, cols], in_=result[:])
             start += width

@@ -31,7 +31,7 @@ HELD = 4
 VECTOR_SCATTERS = ((1664, 2048),)
 SCALAR_SCATTERS = ((1024, 1344), (1344, 1664))
 GROUPS = ((0, 1), (1, 2), (2, 3), (3, 4), (4, 5), (5, 6), (6, 8))
-STORES = (256, 640, 640, 384, 128)
+STORES = (512, 416, 384, 320, 224, 192)
 
 
 def group_of(e):
@@ -42,7 +42,7 @@ def vector_share(s, c, width):
     if s == 0:
         return width // 2
     loads_behind = len(LOADS[s]) - 1 - c
-    return {2: width // 4, 0: width // 2}.get(loads_behind, 0)
+    return {0: width // 2}.get(loads_behind, 0)
 
 
 def tile_moe_two_mlp_relu_kernel(tc, xT, w1_words, w1_scales, w2_words, w2_scales, gate, offs, dst, out):
@@ -69,8 +69,8 @@ def tile_moe_two_mlp_relu_kernel(tc, xT, w1_words, w1_scales, w2_words, w2_scale
         scalar_window = tile("scalar_window", [P, T], F32)
 
         nc.vector.memset(plane[:].bitcast(I32), 0)
-        nc.gpsimd.memset(vector_window[:], 0.0)
-        nc.scalar.copy(scalar_window[:], vector_window[:])
+        nc.vector.memset(vector_window[:], 0.0)
+        nc.gpsimd.memset(scalar_window[:], 0.0)
         make_identity(nc, ident[:])
 
         raw, w1w, w1_planes, gates = {}, {}, {}, {}
@@ -226,7 +226,7 @@ def tile_moe_two_mlp_relu_kernel(tc, xT, w1_words, w1_scales, w2_words, w2_scale
                 hs[e] = tile(f"hs{e}", [P, 2, 2, P, 2], BF16, f"hs{e % 3}")
             for s in range(1 if e < 2 else 0, PASSES):
                 product(e, b, s)
-            nc.scalar.activation(hs[e][:, b], sums[e, b][:].rearrange("c (p u v) -> c u p v", u=2, v=2), RELU)
+            nc.scalar.activation(hs[e][:, b], sums[e, b][:].rearrange("c (p u v) -> c u p v", u=2, v=2), RELU, bias=scalar_window[:, 0:1])
 
         def turn(e, bank):
             lo, hi = group_of(e)
@@ -329,7 +329,7 @@ def tile_moe_two_mlp_relu_kernel(tc, xT, w1_words, w1_scales, w2_words, w2_scale
         start = 0
         for n, width in enumerate(STORES):
             cols = slice(start, start + width)
-            result = tile(f"result{start}", [P, width], F32, f"raw0_{n}")
+            result = tile(f"result{start}", [P, width], F32, f"raw1_{n + 1}")
             nc.vector.tensor_tensor(result[:], vector_window[:, cols], scalar_window[:, cols], ADD)
             nc.sync.dma_start(out=out[:, cols], in_=result[:])
             start += width

@@ -28,8 +28,8 @@ WORD_LOADS = ((2, 4), (4, 6), (6, 8))
 SCALE_LOADS = ((0, 2), (2, 8))
 PAIR = 2 * C
 HELD = 4
-VECTOR_SCATTERS = ((1664, 2048),)
-SCALAR_SCATTERS = ((1024, 1344), (1344, 1664))
+VECTOR_SCATTERS = ((0, 256), (256, 512), (512, 768), (1568, 2048))
+SCALAR_SCATTERS = ((768, 1024), (1024, 1280), (1280, 1568))
 GROUPS = ((0, 1), (1, 2), (2, 3), (3, 4), (4, 5), (5, 6), (6, 8))
 STORES = (512, 416, 384, 320, 224, 192)
 
@@ -42,7 +42,7 @@ def vector_share(s, c, width):
     if s == 0:
         return width // 2
     loads_behind = len(LOADS[s]) - 1 - c
-    return {0: width // 2}.get(loads_behind, 0)
+    return {2: width // 4, 0: width // 2}.get(loads_behind, 0)
 
 
 def tile_moe_two_mlp_relu_kernel(tc, xT, w1_words, w1_scales, w2_words, w2_scales, gate, offs, dst, out):
@@ -210,7 +210,7 @@ def tile_moe_two_mlp_relu_kernel(tc, xT, w1_words, w1_scales, w2_words, w2_scale
 
         def product(e, b, s):
             if s == 0:
-                sums[e, b] = psum.tile([P, H], F32, name=f"acc{e}_{b}", tag=(f"lower{e % 4}", f"upper{e % 3}")[b])
+                sums[e, b] = psum.tile([P, H], F32, name=f"acc{e}_{b}", tag=(f"lower{e % 3}", f"upper{e % 3}")[b])
             nc.tensor.matmul_mx(
                 out=sums[e, b][:],
                 lhsT=slot_words[s, C * e + P * b].bitcast(FP8X4),
@@ -226,7 +226,7 @@ def tile_moe_two_mlp_relu_kernel(tc, xT, w1_words, w1_scales, w2_words, w2_scale
                 hs[e] = tile(f"hs{e}", [P, 2, 2, P, 2], BF16, f"hs{e % 3}")
             for s in range(1 if e < 2 else 0, PASSES):
                 product(e, b, s)
-            nc.scalar.activation(hs[e][:, b], sums[e, b][:].rearrange("c (p u v) -> c u p v", u=2, v=2), RELU, bias=scalar_window[:, 0:1])
+            nc.scalar.activation(hs[e][:, b], sums[e, b][:].rearrange("c (p u v) -> c u p v", u=2, v=2), RELU)
 
         def turn(e, bank):
             lo, hi = group_of(e)
@@ -274,19 +274,6 @@ def tile_moe_two_mlp_relu_kernel(tc, xT, w1_words, w1_scales, w2_words, w2_scale
                 MULT,
             )
 
-        def copy_out(lo, hi):
-            y, first_expert = ys[lo]
-            nc.scalar.copy(gated(C * lo, C * hi), y[:, C * (lo - first_expert) : C * (hi - first_expert)])
-
-        def scatter_times_gate(e):
-            gate_lo = max(at for at in gates if at <= e)
-            nc.vector.tensor_tensor(
-                vector_window[:].indirect(dst_t[:, C * e // 16 : C * (e + 1) // 16]),
-                gated(C * e, C * (e + 1)),
-                gates[gate_lo][:, C * (e - gate_lo) : C * (e + 1 - gate_lo)],
-                MULT,
-            )
-
         def scatter_on_vector(n):
             lo, hi = VECTOR_SCATTERS[n]
             nc.vector.tensor_copy(vector_window[:].indirect(dst_t[:, lo // 16 : hi // 16]), gated(lo, hi))
@@ -298,31 +285,34 @@ def tile_moe_two_mlp_relu_kernel(tc, xT, w1_words, w1_scales, w2_words, w2_scale
         for e in range(2):
             for b in range(2):
                 product(e, b, 0)
-        gated_tiles[0] = tile("gated0", [P, 4 * C], F32)
+        gated_tiles[0] = tile("gated0", [P, 3 * C], F32)
         for e in range(E):
             if e == 6:
                 gather_words(1, 3 * PAIR, PAIR, "hg1")
             first(e, 0)
+            if e >= 4:
+                second(e - 4, e - 3, f"lower{e % 3}")
+            if 4 <= e < E - 1:
+                times_gate(e - 4, e - 3)
             if e >= 2:
-                turn(e - 2, f"lower{(e - 1) % 4}")
-                if group_of(e - 2)[1] == e - 1:
-                    quantise_h(group_of(e - 2)[0])
+                turn(e - 2, f"lower{(e - 1) % 3}" if e in (3, 4) else f"turn{e % 2}")
+                quantise_h(e - 2)
+            if 4 <= e < E - 1:
+                scatter_on_vector(e - 4)
             first(e, 1)
-            if 3 <= e < E - 1:
-                second(e - 3, e - 2, f"upper{e % 3}")
-                copy_out(e - 3, e - 2)
-                scatter_times_gate(e - 3)
-        turn(E - 2, "lower3")
-        turn(E - 1, "spare")
+        turn(E - 2, "turn0")
+        turn(E - 1, "turn1")
+        gated_tiles[3 * C] = tile("gated3", [P, C], F32, "hs1")
         gated_tiles[4 * C] = tile("gated4", [P, 4 * C], F32, "raw1_0")
+        times_gate(3, 4)
         second(4, 5, "upper1")
         times_gate(4, 5)
-        second(5, 6, "lower3")
-        times_gate(5, 6)
         quantise_h(E - 2)
-        second(6, 8, "lower0")
+        second(5, 6, "turn0")
+        times_gate(5, 6)
+        second(6, 8, "upper0")
         times_gate(6, 8)
-        scatter_on_vector(0)
+        scatter_on_vector(3)
         for n in range(len(SCALAR_SCATTERS)):
             scatter_on_scalar(n)
 

@@ -31,7 +31,7 @@ HELD = 4
 VECTOR_SCATTERS = ((0, 256), (256, 512), (512, 768), (1568, 2048))
 SCALAR_SCATTERS = ((768, 1024), (1024, 1280), (1280, 1568))
 GROUPS = ((0, 1), (1, 2), (2, 3), (3, 4), (4, 5), (5, 6), (6, 8))
-STORES = (512, 416, 384, 320, 224, 192)
+STORES = (512, 448, 384, 320, 256, 128)
 
 
 def group_of(e):

@@ -28,8 +28,8 @@ WORD_LOADS = ((2, 4), (4, 6), (6, 8))
 SCALE_LOADS = ((0, 2), (2, 8))
 PAIR = 2 * C
 HELD = 4
-VECTOR_SCATTERS = ((0, 256), (256, 512), (512, 768), (1568, 2048))
-SCALAR_SCATTERS = ((768, 1024), (1024, 1280), (1280, 1568))
+VECTOR_SCATTERS = ((0, 256), (256, 512), (1024, 1280), (1664, 2048))
+SCALAR_SCATTERS = ((512, 768), (768, 1024), (1280, 1664))
 GROUPS = ((0, 1), (1, 2), (2, 3), (3, 4), (4, 5), (5, 6), (6, 8))
 STORES = (512, 448, 384, 320, 256, 128)
 
@@ -285,31 +285,31 @@ def tile_moe_two_mlp_relu_kernel(tc, xT, w1_words, w1_scales, w2_words, w2_scale
         for e in range(2):
             for b in range(2):
                 product(e, b, 0)
-        gated_tiles[0] = tile("gated0", [P, 3 * C], F32)
+        gated_tiles[0] = tile("gated0", [P, 2 * C], F32)
         for e in range(E):
             if e == 6:
                 gather_words(1, 3 * PAIR, PAIR, "hg1")
             first(e, 0)
-            if e >= 4:
+            if e in (4, 5):
                 second(e - 4, e - 3, f"lower{e % 3}")
-            if 4 <= e < E - 1:
                 times_gate(e - 4, e - 3)
+            if e == E - 1:
+                second(2, 4, f"lower{e % 3}")
             if e >= 2:
                 turn(e - 2, f"lower{(e - 1) % 3}" if e in (3, 4) else f"turn{e % 2}")
                 quantise_h(e - 2)
-            if 4 <= e < E - 1:
+            if e in (4, 5):
                 scatter_on_vector(e - 4)
             first(e, 1)
         turn(E - 2, "turn0")
         turn(E - 1, "turn1")
-        gated_tiles[3 * C] = tile("gated3", [P, C], F32, "hs1")
+        gated_tiles[2 * C] = tile("gated2", [P, 2 * C], F32, "hs1")
         gated_tiles[4 * C] = tile("gated4", [P, 4 * C], F32, "raw1_0")
-        times_gate(3, 4)
-        second(4, 5, "upper1")
-        times_gate(4, 5)
+        times_gate(2, 4)
+        second(4, 6, "upper1")
+        times_gate(4, 6)
         quantise_h(E - 2)
-        second(5, 6, "turn0")
-        times_gate(5, 6)
+        scatter_on_vector(2)
         second(6, 8, "upper0")
         times_gate(6, 8)
         scatter_on_vector(3)

@@ -184,7 +184,6 @@ def tile_moe_two_mlp_relu_kernel(tc, xT, w1_words, w1_scales, w2_words, w2_scale
         load_scales(w2s, w2_scales)
         nc.sync.dma_start(out=w2w[:].bitcast(I32), in_=w2_words.rearrange("e s p b -> p (e s) b").bitcast(I32))
         nc.sync.dma_start(dst_t[:], dst)
-        load_gate(0, 2)
         quantise(1)
 
         gather_bytes("first", 0, PAIR)
@@ -192,11 +191,12 @@ def tile_moe_two_mlp_relu_kernel(tc, xT, w1_words, w1_scales, w2_words, w2_scale
         gather_words(1, C, C)
         gather_bytes("second", 2 * C, 3 * C)
         lift("second", 3 * C)
+        load_w1(2)
         gather_words(1, 2 * C, C)
         gather_words(1, 3 * C, C)
         gather_bytes("third", 5 * C, 3 * C)
         lift("third", 5 * C)
-        load_w1(2)
+        load_gate(0, 2)
         load_gate(2, E)
         gather_words(1, 2 * PAIR, PAIR)
 
@@ -296,7 +296,7 @@ def tile_moe_two_mlp_relu_kernel(tc, xT, w1_words, w1_scales, w2_words, w2_scale
             if e == E - 1:
                 second(2, 4, f"lower{e % 3}")
             if e >= 2:
-                turn(e - 2, f"lower{(e - 1) % 3}" if e in (3, 4) else f"turn{e % 2}")
+                turn(e - 2, f"lower{(e - 1) % 3}" if e == 3 else f"turn{e % 2}")
                 quantise_h(e - 2)
             if e in (4, 5):
                 scatter_on_vector(e - 4)

@@ -28,6 +28,7 @@ WORD_LOADS = ((2, 4), (4, 6), (6, 8))
 SCALE_LOADS = ((0, 2), (2, 8))
 PAIR = 2 * C
 HELD = 4
+GPSIMD_LOADS = 4
 VECTOR_SCATTERS = ((0, 256), (256, 512), (1024, 1280), (1664, 2048))
 SCALAR_SCATTERS = ((512, 768), (768, 1024), (1280, 1664))
 GROUPS = ((0, 1), (1, 2), (2, 3), (3, 4), (4, 5), (5, 6), (6, 8))
@@ -38,11 +39,10 @@ def group_of(e):
     return [group for group in GROUPS if group[0] <= e][-1]
 
 
-def vector_share(s, c, width):
-    if s == 0:
+def helper_share(s, c, width):
+    if s == 0 or c < GPSIMD_LOADS or c == len(LOADS[s]) - 1:
         return width // 2
-    loads_behind = len(LOADS[s]) - 1 - c
-    return {2: width // 4, 0: width // 2}.get(loads_behind, 0)
+    return 0
 
 
 def tile_moe_two_mlp_relu_kernel(tc, xT, w1_words, w1_scales, w2_words, w2_scales, gate, offs, dst, out):
@@ -131,10 +131,13 @@ def tile_moe_two_mlp_relu_kernel(tc, xT, w1_words, w1_scales, w2_words, w2_scale
                     load_start = sum(LOADS[s][:c])
                     lo, hi = max(start, load_start), min(start + width, load_start + load_width)
                     if lo < hi:
-                        share = vector_share(s, c, hi - lo)
+                        share = helper_share(s, c, hi - lo)
                         part = grouped[:, lo - start : hi - start, :]
                         source = raw[s, c][:, :, lo - load_start : hi - load_start]
-                        cast(nc.vector.tensor_copy, part, source, 0, share)
+                        if s == 1 and c < GPSIMD_LOADS:
+                            nc.gpsimd.tensor_copy(part[:, :share, :], source[:, :, :share].rearrange("p j w -> p w j"))
+                        else:
+                            cast(nc.vector.tensor_copy, part, source, 0, share)
                         cast(nc.scalar.copy, part, source, share, hi - lo)
                 nc.vector.quantize_mx(
                     out=words[s][:, start : start + width].bitcast(FP8X4),

@@ -28,6 +28,7 @@ WORD_LOADS = ((2, 4), (4, 6), (6, 8))
 SCALE_LOADS = ((0, 2), (2, 8))
 PAIR = 2 * C
 HELD = 4
+TURNED = 6
 GPSIMD_LOADS = 4
 VECTOR_SCATTERS = ((0, 256), (256, 512), (1024, 1280), (1664, 2048))
 SCALAR_SCATTERS = ((512, 768), (768, 1024), (1280, 1664))
@@ -72,6 +73,7 @@ def tile_moe_two_mlp_relu_kernel(tc, xT, w1_words, w1_scales, w2_words, w2_scale
         nc.vector.memset(vector_window[:], 0.0)
         nc.gpsimd.memset(scalar_window[:], 0.0)
         make_identity(nc, ident[:])
+        nc.gpsimd.memset(w1s[1][:, PASSES * (TURNED - 2) :, :].bitcast(I32), 0)
 
         raw, w1w, w1_planes, gates = {}, {}, {}, {}
 
@@ -183,6 +185,7 @@ def tile_moe_two_mlp_relu_kernel(tc, xT, w1_words, w1_scales, w2_words, w2_scale
         load_first_pair(1)
         load_w1_scales(1)
         load_w1(0)
+        load_w1(2)
         load_w1(1)
         load_scales(w2s, w2_scales)
         nc.sync.dma_start(out=w2w[:].bitcast(I32), in_=w2_words.rearrange("e s p b -> p (e s) b").bitcast(I32))
@@ -194,7 +197,6 @@ def tile_moe_two_mlp_relu_kernel(tc, xT, w1_words, w1_scales, w2_words, w2_scale
         gather_words(1, C, C)
         gather_bytes("second", 2 * C, 3 * C)
         lift("second", 3 * C)
-        load_w1(2)
         gather_words(1, 2 * C, C)
         gather_words(1, 3 * C, C)
         gather_bytes("third", 5 * C, 3 * C)
@@ -202,6 +204,15 @@ def tile_moe_two_mlp_relu_kernel(tc, xT, w1_words, w1_scales, w2_words, w2_scale
         load_gate(0, 2)
         load_gate(2, E)
         gather_words(1, 2 * PAIR, PAIR)
+
+        dealt_words, dealt_scales = {}, {}
+        for e in range(TURNED, E):
+            dealt_scales[e] = tile(f"dealt_scales{e}", [P, PASSES, 4, P], U8, f"raw0_{e - 3}")
+            nc.gpsimd.tensor_copy(dealt_scales[e][:], w1_planes[e].rearrange("p s (m t) -> p s t m", t=4))
+        for e in range(TURNED, E):
+            dealt_words[e] = tile(f"dealt_words{e}", [P, PASSES, 4, P], U16, f"raw0_{e - 6}")
+            for s in range(PASSES):
+                nc.gpsimd.tensor_copy(dealt_words[e][:, s], w1w[e, s].bitcast(U16).rearrange("p (m t) -> p t m", t=4))
 
         gated_tiles, ys = {}, {}
 
@@ -224,7 +235,27 @@ def tile_moe_two_mlp_relu_kernel(tc, xT, w1_words, w1_scales, w2_words, w2_scale
                 stop=(s == PASSES - 1),
             )
 
+        def first_dealt(e, b):
+            if (e, b) == (TURNED, 0):
+                hg[TURNED] = tile(f"hg{TURNED}", [P, (E - TURNED) * C, 4], BF16)
+            at = C * e + P * b
+            acc = psum.tile([P, 4, P], F32, name=f"acc{e}_{b}", tag=(f"lower{e % 3}", f"upper{e % 3}")[b])
+            for t in range(4):
+                for s in range(PASSES):
+                    nc.tensor.matmul_mx(
+                        out=acc[:, t, :],
+                        lhsT=dealt_words[e][:, s, t, :].bitcast(U8).bitcast(FP4X4),
+                        lhsT_scale=dealt_scales[e][:, s, t, :],
+                        rhs=slot_words[s, at].bitcast(FP8X4),
+                        rhs_scale=slot_scales[s, at],
+                        start=(s == 0),
+                        stop=(s == PASSES - 1),
+                    )
+            nc.scalar.activation(hg[TURNED][:, at - C * TURNED : at - C * TURNED + P, :], acc[:].rearrange("p t c -> p c t"), RELU)
+
         def first(e, b):
+            if e >= TURNED:
+                return first_dealt(e, b)
             if b == 0:
                 hs[e] = tile(f"hs{e}", [P, 2, 2, P, 2], BF16, f"hs{e % 3}")
             for s in range(1 if e < 2 else 0, PASSES):
@@ -304,9 +335,7 @@ def tile_moe_two_mlp_relu_kernel(tc, xT, w1_words, w1_scales, w2_words, w2_scale
             if e in (4, 5):
                 scatter_on_vector(e - 4)
             first(e, 1)
-        turn(E - 2, "turn0")
-        turn(E - 1, "turn1")
-        gated_tiles[2 * C] = tile("gated2", [P, 2 * C], F32, "hs1")
+        gated_tiles[2 * C] = tile("gated2", [P, 2 * C], F32, "raw0_1")
         gated_tiles[4 * C] = tile("gated4", [P, 4 * C], F32, "raw1_0")
         times_gate(2, 4)
         second(4, 6, "upper1")

@@ -30,8 +30,8 @@ PAIR = 2 * C
 HELD = 4
 TURNED = 6
 GPSIMD_LOADS = 4
-VECTOR_SCATTERS = ((0, 256), (256, 512), (1024, 1280), (1664, 2048))
-SCALAR_SCATTERS = ((512, 768), (768, 1024), (1280, 1664))
+VECTOR_SCATTERS = ((0, 256), (256, 512), (1472, 2048))
+SCALAR_SCATTERS = ((512, 768), (768, 1120), (1120, 1472))
 GROUPS = ((0, 1), (1, 2), (2, 3), (3, 4), (4, 5), (5, 6), (6, 8))
 STORES = (512, 448, 384, 320, 256, 128)
 
@@ -201,8 +201,8 @@ def tile_moe_two_mlp_relu_kernel(tc, xT, w1_words, w1_scales, w2_words, w2_scale
         gather_words(1, 3 * C, C)
         gather_bytes("third", 5 * C, 3 * C)
         lift("third", 5 * C)
-        load_gate(0, 2)
-        load_gate(2, E)
+        load_gate(0, 3)
+        load_gate(3, E)
         gather_words(1, 2 * PAIR, PAIR)
 
         dealt_words, dealt_scales = {}, {}
@@ -251,7 +251,8 @@ def tile_moe_two_mlp_relu_kernel(tc, xT, w1_words, w1_scales, w2_words, w2_scale
                         start=(s == 0),
                         stop=(s == PASSES - 1),
                     )
-            nc.scalar.activation(hg[TURNED][:, at - C * TURNED : at - C * TURNED + P, :], acc[:].rearrange("p t c -> p c t"), RELU)
+            bias = scalar_window[:, 0:1] if (e, b) == (E - 1, 1) else 0.0
+            nc.scalar.activation(hg[TURNED][:, at - C * TURNED : at - C * TURNED + P, :], acc[:].rearrange("p t c -> p c t"), RELU, bias=bias)
 
         def first(e, b):
             if e >= TURNED:
@@ -319,32 +320,31 @@ def tile_moe_two_mlp_relu_kernel(tc, xT, w1_words, w1_scales, w2_words, w2_scale
         for e in range(2):
             for b in range(2):
                 product(e, b, 0)
-        gated_tiles[0] = tile("gated0", [P, 2 * C], F32)
+        gated_tiles[0] = tile("gated0", [P, T], F32, "raw1_0")
         for e in range(E):
             if e == 6:
                 gather_words(1, 3 * PAIR, PAIR, "hg1")
             first(e, 0)
-            if e in (4, 5):
-                second(e - 4, e - 3, f"lower{e % 3}")
-                times_gate(e - 4, e - 3)
-            if e == E - 1:
-                second(2, 4, f"lower{e % 3}")
+            if e == 4:
+                second(0, 1, "lower1")
+                times_gate(0, 1)
+            if e == 5:
+                second(1, 3, "lower2")
+                times_gate(1, 3)
             if e >= 2:
                 turn(e - 2, f"lower{(e - 1) % 3}" if e == 3 else f"turn{e % 2}")
                 quantise_h(e - 2)
             if e in (4, 5):
                 scatter_on_vector(e - 4)
             first(e, 1)
-        gated_tiles[2 * C] = tile("gated2", [P, 2 * C], F32, "raw0_1")
-        gated_tiles[4 * C] = tile("gated4", [P, 4 * C], F32, "raw1_0")
-        times_gate(2, 4)
-        second(4, 6, "upper1")
-        times_gate(4, 6)
+        second(3, 5, "upper2")
+        times_gate(3, 5)
         quantise_h(E - 2)
-        scatter_on_vector(2)
+        second(5, 6, "lower0")
+        times_gate(5, 6)
         second(6, 8, "upper0")
         times_gate(6, 8)
-        scatter_on_vector(3)
+        scatter_on_vector(2)
         for n in range(len(SCALAR_SCATTERS)):
             scatter_on_scalar(n)
 

@@ -33,7 +33,7 @@ GPSIMD_LOADS = 4
 VECTOR_SCATTERS = ((0, 256), (256, 512), (1472, 2048))
 SCALAR_SCATTERS = ((512, 768), (768, 1120), (1120, 1472))
 GROUPS = ((0, 1), (1, 2), (2, 3), (3, 4), (4, 5), (5, 6), (6, 8))
-STORES = (512, 448, 384, 320, 256, 128)
+STORES = (256, 384, 384, 384, 384, 256)
 
 
 def group_of(e):
@@ -252,7 +252,8 @@ def tile_moe_two_mlp_relu_kernel(tc, xT, w1_words, w1_scales, w2_words, w2_scale
                         stop=(s == PASSES - 1),
                     )
             bias = scalar_window[:, 0:1] if (e, b) == (E - 1, 1) else 0.0
-            nc.scalar.activation(hg[TURNED][:, at - C * TURNED : at - C * TURNED + P, :], acc[:].rearrange("p t c -> p c t"), RELU, bias=bias)
+            part = hg[TURNED][:, at - C * TURNED : at - C * TURNED + P, :]
+            nc.scalar.activation(part.rearrange("p (c i) t -> p c t i", i=2), acc[:].rearrange("p t (c i) -> p c t i", i=2), RELU, bias=bias)
 
         def first(e, b):
             if e >= TURNED:
@@ -328,14 +329,14 @@ def tile_moe_two_mlp_relu_kernel(tc, xT, w1_words, w1_scales, w2_words, w2_scale
             if e == 4:
                 second(0, 1, "lower1")
                 times_gate(0, 1)
-            if e == 5:
+            if e == 6:
                 second(1, 3, "lower2")
                 times_gate(1, 3)
             if e >= 2:
                 turn(e - 2, f"lower{(e - 1) % 3}" if e == 3 else f"turn{e % 2}")
                 quantise_h(e - 2)
-            if e in (4, 5):
-                scatter_on_vector(e - 4)
+            if e in (4, 6):
+                scatter_on_vector(e // 2 - 2)
             first(e, 1)
         second(3, 5, "upper2")
         times_gate(3, 5)

@@ -204,6 +204,7 @@ def tile_moe_two_mlp_relu_kernel(tc, xT, w1_words, w1_scales, w2_words, w2_scale
         load_gate(0, 3)
         load_gate(3, E)
         gather_words(1, 2 * PAIR, PAIR)
+        gather_words(1, 3 * PAIR, PAIR, "raw0_2")
 
         dealt_words, dealt_scales = {}, {}
         for e in range(TURNED, E):
@@ -323,8 +324,6 @@ def tile_moe_two_mlp_relu_kernel(tc, xT, w1_words, w1_scales, w2_words, w2_scale
                 product(e, b, 0)
         gated_tiles[0] = tile("gated0", [P, T], F32, "raw1_0")
         for e in range(E):
-            if e == 6:
-                gather_words(1, 3 * PAIR, PAIR, "hg1")
             first(e, 0)
             if e == 4:
                 second(0, 1, "lower1")

@@ -30,8 +30,8 @@ PAIR = 2 * C
 HELD = 4
 TURNED = 6
 GPSIMD_LOADS = 4
-VECTOR_SCATTERS = ((0, 256), (256, 512), (1472, 2048))
-SCALAR_SCATTERS = ((512, 768), (768, 1120), (1120, 1472))
+VECTOR_SCATTERS = ((0, 256), (256, 512), (1536, 2048))
+SCALAR_SCATTERS = ((512, 768), (768, 1152), (1152, 1536))
 GROUPS = ((0, 1), (1, 2), (2, 3), (3, 4), (4, 5), (5, 6), (6, 8))
 STORES = (256, 384, 384, 384, 384, 256)
 

@@ -22,14 +22,14 @@ ADD = mybir.AluOpType.add
 P = 128
 PASSES = K // 512
 LIFT = 4
-LOADS = ((768, 512, 384, 256, 128), (256,) * 7 + (128, 128))
+LOADS = ((768, 512, 384, 256, 128), (512, 512, 256, 256, 256, 128, 128))
 PIECES = ((512, 256, 256, 256, 256, 128, 256, 128), (1024, 512, 256, 128, 128))
-WORD_LOADS = ((2, 4), (4, 6), (6, 8))
+WORD_LOADS = ((2, 4), (6, 7), (4, 5), (7, 8), (5, 6))
 SCALE_LOADS = ((0, 2), (2, 8))
 PAIR = 2 * C
 HELD = 4
 TURNED = 6
-GPSIMD_LOADS = 4
+GPSIMD_LOADS = 3
 VECTOR_SCATTERS = ((0, 256), (256, 512), (1536, 2048))
 SCALAR_SCATTERS = ((512, 768), (768, 1152), (1152, 1536))
 GROUPS = ((0, 1), (1, 2), (2, 3), (3, 4), (4, 5), (5, 6), (6, 8))
@@ -184,9 +184,8 @@ def tile_moe_two_mlp_relu_kernel(tc, xT, w1_words, w1_scales, w2_words, w2_scale
         load_first_pair(0)
         load_first_pair(1)
         load_w1_scales(1)
-        load_w1(0)
-        load_w1(2)
-        load_w1(1)
+        for n in range(3):
+            load_w1(n)
         load_scales(w2s, w2_scales)
         nc.sync.dma_start(out=w2w[:].bitcast(I32), in_=w2_words.rearrange("e s p b -> p (e s) b").bitcast(I32))
         nc.sync.dma_start(dst_t[:], dst)
@@ -197,12 +196,14 @@ def tile_moe_two_mlp_relu_kernel(tc, xT, w1_words, w1_scales, w2_words, w2_scale
         gather_words(1, C, C)
         gather_bytes("second", 2 * C, 3 * C)
         lift("second", 3 * C)
+        load_w1(3)
+        load_w1(4)
+        load_gate(0, 1)
         gather_words(1, 2 * C, C)
         gather_words(1, 3 * C, C)
         gather_bytes("third", 5 * C, 3 * C)
         lift("third", 5 * C)
-        load_gate(0, 3)
-        load_gate(3, E)
+        load_gate(1, E)
         gather_words(1, 2 * PAIR, PAIR)
         gather_words(1, 3 * PAIR, PAIR, "raw0_2")
 

@@ -30,8 +30,8 @@ PAIR = 2 * C
 HELD = 4
 TURNED = 6
 GPSIMD_LOADS = 3
-VECTOR_SCATTERS = ((0, 256), (256, 512), (1536, 2048))
-SCALAR_SCATTERS = ((512, 768), (768, 1152), (1152, 1536))
+VECTOR_SCATTERS = ((0, 256), (256, 512), (1472, 2048))
+SCALAR_SCATTERS = ((512, 768), (768, 1120), (1120, 1472))
 GROUPS = ((0, 1), (1, 2), (2, 3), (3, 4), (4, 5), (5, 6), (6, 8))
 STORES = (256, 384, 384, 384, 384, 256)
 

from contextlib import ExitStack

import concourse.mybir as mybir
from concourse.masks import make_identity

K, T, E, C, H, N = 1024, 2048, 8, 256, 512, 128
FLOPS = 2 * E * C * (K * H + H * N)

F32 = mybir.dt.float32
BF16 = mybir.dt.bfloat16
I32 = mybir.dt.int32
U32 = mybir.dt.uint32
U16 = mybir.dt.uint16
U8 = mybir.dt.uint8
FP8X4 = mybir.dt.float8_e4m3fn_x4
FP4X4 = mybir.dt.float4_e2m1fn_x4
RELU = mybir.ActivationFunctionType.Relu
COPY = mybir.ActivationFunctionType.Copy
MULT = mybir.AluOpType.mult
ADD = mybir.AluOpType.add

P = 128
PASSES = K // 512
LIFT = 4
LOADS = ((768, 512, 384, 256, 128), (512, 512, 256, 256, 256, 128, 128))
PIECES = ((512, 256, 256, 256, 256, 128, 256, 128), (1024, 512, 256, 128, 128))
WORD_LOADS = ((2, 4), (6, 7), (4, 5), (7, 8), (5, 6))
SCALE_LOADS = ((0, 2), (2, 8))
PAIR = 2 * C
HELD = 4
TURNED = 6
GPSIMD_LOADS = 3
VECTOR_SCATTERS = ((0, 256), (256, 512), (1472, 2048))
SCALAR_SCATTERS = ((512, 768), (768, 1120), (1120, 1472))
GROUPS = ((0, 1), (1, 2), (2, 3), (3, 4), (4, 5), (5, 6), (6, 8))
STORES = (256, 384, 384, 384, 384, 256)


def group_of(e):
    return [group for group in GROUPS if group[0] <= e][-1]


def helper_share(s, c, width):
    if s == 0 or c < GPSIMD_LOADS or c == len(LOADS[s]) - 1:
        return width // 2
    return 0


def tile_moe_two_mlp_relu_kernel(tc, xT, w1_words, w1_scales, w2_words, w2_scales, gate, offs, dst, out):
    nc = tc.nc
    with ExitStack() as ctx:
        lists = ctx.enter_context(tc.tile_pool(name="lists", bufs=1))
        keep = ctx.enter_context(tc.tile_pool(name="keep", bufs=1))
        psum = ctx.enter_context(tc.psum_pool(name="psum", bufs=1))

        offs_t = lists.tile([P, T // 16], U16, name="offs_t", align_bytes=256)
        dst_t = lists.tile([P, T // 16], U16, name="dst_t", align_bytes=256)

        def tile(name, shape, dtype, tag=None):
            return keep.tile(shape, dtype, name=name, tag=tag or name, align_bytes=256)

        words = [tile(f"words{s}", [P, T], U32) for s in range(PASSES)]
        plane = tile("plane", [P, T], U8)
        w1s = [tile(f"w1s{lo}", [P, (hi - lo) * PASSES, H], U8) for lo, hi in SCALE_LOADS]
        w2w = tile("w2w", [P, E, 2 * N], U8)
        w2s = tile("w2s", [P, E, N], U8)
        ident = tile("ident", [P, P], F32)
        lifted = {lo: tile(f"lifted{lo}", [P, w], U8) for lo, w in [(0, 3 * C), (3 * C, 2 * C), (5 * C, 3 * C)]}
        vector_window = tile("vector_window", [P, T], F32)
        scalar_window = tile("scalar_window", [P, T], F32)

        nc.vector.memset(plane[:].bitcast(I32), 0)
        nc.vector.memset(vector_window[:], 0.0)
        nc.gpsimd.memset(scalar_window[:], 0.0)
        make_identity(nc, ident[:])
        nc.gpsimd.memset(w1s[1][:, PASSES * (TURNED - 2) :, :].bitcast(I32), 0)

        raw, w1w, w1_planes, gates = {}, {}, {}, {}

        def load_x(s, c):
            start, width = sum(LOADS[s][:c]), LOADS[s][c]
            raw[s, c] = tile(f"raw{s}_{c}", [P, 4, width], F32)
            nc.sync.dma_start(out=raw[s, c][:], in_=xT[512 * s : 512 * s + 512, start : start + width].rearrange("(p j) w -> p j w", j=4))

        def load_w1(n):
            lo, hi = WORD_LOADS[n]
            piece = tile(f"w1w{lo}", [P, (hi - lo) * PASSES, 2 * H], U8)
            nc.sync.dma_start(out=piece[:].bitcast(I32), in_=w1_words[lo:hi].rearrange("e s p b -> p (e s) b").bitcast(I32))
            for e in range(lo, hi):
                for s in range(PASSES):
                    w1w[e, s] = piece[:, PASSES * (e - lo) + s, :]

        def load_first_pair(s):
            piece = tile(f"w1w_first{s}", [P, 2, 2 * H], U8)
            nc.sync.dma_start(out=piece[:].bitcast(I32), in_=w1_words[0:2, s].rearrange("e p b -> p e b").bitcast(I32))
            for e in range(2):
                w1w[e, s] = piece[:, e, :]

        def load_scales(weights_plane, source):
            rows = source.rearrange("e s (q r) i -> r q (e s) i", r=4)
            for r in range(4):
                nc.sync.dma_start(out=weights_plane[r:P:32, :, :].bitcast(I32), in_=rows[r].bitcast(I32))

        def load_w1_scales(n):
            lo, hi = SCALE_LOADS[n]
            load_scales(w1s[n], w1_scales[lo:hi])
            for e in range(lo, hi):
                w1_planes[e] = w1s[n][:, PASSES * (e - lo) : PASSES * (e - lo + 1), :]

        def load_gate(lo, hi):
            piece = tile(f"gate{lo}", [P, (hi - lo) * C], F32)
            nc.sync.dma_start(out=piece[:], in_=gate[:, lo * C : hi * C])
            gates[lo] = piece

        for c in range(len(LOADS[0])):
            load_x(0, c)
        nc.sync.dma_start(offs_t[:], offs)
        for c in range(len(LOADS[1]) - HELD):
            load_x(1, c)

        def cast(engine, grouped, source, lo, hi):
            if hi > lo:
                engine(
                    grouped[:, lo:hi, :].rearrange("p (b i) j -> p b j i", i=4),
                    source[:, :, lo:hi].rearrange("p j (b i) -> p b j i", i=4),
                )

        def quantise(s):
            start = 0
            for width in PIECES[s]:
                grouped = tile(f"grouped{s}_{start}", [P, width, 4], BF16)
                for c, load_width in enumerate(LOADS[s]):
                    load_start = sum(LOADS[s][:c])
                    lo, hi = max(start, load_start), min(start + width, load_start + load_width)
                    if lo < hi:
                        share = helper_share(s, c, hi - lo)
                        part = grouped[:, lo - start : hi - start, :]
                        source = raw[s, c][:, :, lo - load_start : hi - load_start]
                        if s == 1 and c < GPSIMD_LOADS:
                            nc.gpsimd.tensor_copy(part[:, :share, :], source[:, :, :share].rearrange("p j w -> p w j"))
                        else:
                            cast(nc.vector.tensor_copy, part, source, 0, share)
                        cast(nc.scalar.copy, part, source, share, hi - lo)
                nc.vector.quantize_mx(
                    out=words[s][:, start : start + width].bitcast(FP8X4),
                    scales=plane[LIFT * (1 - s) : P, start : start + width],
                    in_=grouped[:].rearrange("p w j -> p (w j)"),
                )
                start += width

        slot_words, slot_bytes, slot_scales, hs, hg, hq, hqs = {}, {}, {}, {}, {}, {}, {}

        def gather_words(s, lo, w, tag=None):
            piece = tile(f"slot_words{s}_{lo}", [P, w], U32, tag)
            nc.vector.tensor_copy(piece[:], words[s][:].indirect(offs_t[:, lo // 16 : (lo + w) // 16]))
            for at in range(0, w, P):
                slot_words[s, lo + at] = piece[:, at : at + P]

        def gather_bytes(name, lo, w):
            slot_bytes[name] = tile(f"slot_bytes_{name}", [P, w], U8), lo
            nc.vector.tensor_copy(slot_bytes[name][0][:], plane[:].indirect(offs_t[:, lo // 16 : (lo + w) // 16]))
            for at in range(0, w, P):
                slot_scales[1, lo + at] = slot_bytes[name][0][:, at : at + P]

        def lift(name, lo):
            piece, first_slot = slot_bytes[name]
            w = lifted[lo].shape[1]
            for r in range(4):
                nc.sync.dma_start(
                    out=lifted[lo][r:P:32, :].bitcast(I32),
                    in_=piece[LIFT + r : P : 32, lo - first_slot : lo - first_slot + w].bitcast(I32),
                )
            for at in range(0, w, P):
                slot_scales[0, lo + at] = lifted[lo][:, at : at + P]

        quantise(0)
        gather_bytes("early", 0, 3 * C)
        lift("early", 0)
        for c in range(len(LOADS[1]) - HELD, len(LOADS[1])):
            load_x(1, c)
        for lo in range(0, T, T // 2):
            gather_words(0, lo, T // 2)
        load_w1_scales(0)
        load_first_pair(0)
        load_first_pair(1)
        load_w1_scales(1)
        for n in range(3):
            load_w1(n)
        load_scales(w2s, w2_scales)
        nc.sync.dma_start(out=w2w[:].bitcast(I32), in_=w2_words.rearrange("e s p b -> p (e s) b").bitcast(I32))
        nc.sync.dma_start(dst_t[:], dst)
        quantise(1)

        gather_bytes("first", 0, PAIR)
        gather_words(1, 0, C)
        gather_words(1, C, C)
        gather_bytes("second", 2 * C, 3 * C)
        lift("second", 3 * C)
        load_w1(3)
        load_w1(4)
        load_gate(0, 1)
        gather_words(1, 2 * C, C)
        gather_words(1, 3 * C, C)
        gather_bytes("third", 5 * C, 3 * C)
        lift("third", 5 * C)
        load_gate(1, E)
        gather_words(1, 2 * PAIR, PAIR)
        gather_words(1, 3 * PAIR, PAIR, "raw0_2")

        dealt_words, dealt_scales = {}, {}
        for e in range(TURNED, E):
            dealt_scales[e] = tile(f"dealt_scales{e}", [P, PASSES, 4, P], U8, f"raw0_{e - 3}")
            nc.gpsimd.tensor_copy(dealt_scales[e][:], w1_planes[e].rearrange("p s (m t) -> p s t m", t=4))
        for e in range(TURNED, E):
            dealt_words[e] = tile(f"dealt_words{e}", [P, PASSES, 4, P], U16, f"raw0_{e - 6}")
            for s in range(PASSES):
                nc.gpsimd.tensor_copy(dealt_words[e][:, s], w1w[e, s].bitcast(U16).rearrange("p (m t) -> p t m", t=4))

        gated_tiles, ys = {}, {}

        def gated(lo, hi):
            first_slot = max(at for at in gated_tiles if at <= lo)
            return gated_tiles[first_slot][:, lo - first_slot : hi - first_slot]

        sums = {}

        def product(e, b, s):
            if s == 0:
                sums[e, b] = psum.tile([P, H], F32, name=f"acc{e}_{b}", tag=(f"lower{e % 3}", f"upper{e % 3}")[b])
            nc.tensor.matmul_mx(
                out=sums[e, b][:],
                lhsT=slot_words[s, C * e + P * b].bitcast(FP8X4),
                lhsT_scale=slot_scales[s, C * e + P * b],
                rhs=w1w[e, s].bitcast(FP4X4),
                rhs_scale=w1_planes[e][:, s, :],
                start=(s == 0),
                stop=(s == PASSES - 1),
            )

        def first_dealt(e, b):
            if (e, b) == (TURNED, 0):
                hg[TURNED] = tile(f"hg{TURNED}", [P, (E - TURNED) * C, 4], BF16)
            at = C * e + P * b
            acc = psum.tile([P, 4, P], F32, name=f"acc{e}_{b}", tag=(f"lower{e % 3}", f"upper{e % 3}")[b])
            for t in range(4):
                for s in range(PASSES):
                    nc.tensor.matmul_mx(
                        out=acc[:, t, :],
                        lhsT=dealt_words[e][:, s, t, :].bitcast(U8).bitcast(FP4X4),
                        lhsT_scale=dealt_scales[e][:, s, t, :],
                        rhs=slot_words[s, at].bitcast(FP8X4),
                        rhs_scale=slot_scales[s, at],
                        start=(s == 0),
                        stop=(s == PASSES - 1),
                    )
            bias = scalar_window[:, 0:1] if (e, b) == (E - 1, 1) else 0.0
            part = hg[TURNED][:, at - C * TURNED : at - C * TURNED + P, :]
            nc.scalar.activation(part.rearrange("p (c i) t -> p c t i", i=2), acc[:].rearrange("p t (c i) -> p c t i", i=2), RELU, bias=bias)

        def first(e, b):
            if e >= TURNED:
                return first_dealt(e, b)
            if b == 0:
                hs[e] = tile(f"hs{e}", [P, 2, 2, P, 2], BF16, f"hs{e % 3}")
            for s in range(1 if e < 2 else 0, PASSES):
                product(e, b, s)
            nc.scalar.activation(hs[e][:, b], sums[e, b][:].rearrange("c (p u v) -> c u p v", u=2, v=2), RELU)

        def turn(e, bank):
            lo, hi = group_of(e)
            if e == lo:
                hg[lo] = tile(f"hg{lo}", [P, (hi - lo) * C, 4], BF16)
            part = hg[lo][:, C * (e - lo) : C * (e - lo + 1), :]
            hg_words = part.rearrange("p c t -> p (c t)").bitcast(F32).rearrange("p (c u) -> p c u", u=2)
            hs_words = hs[e][:].rearrange("c b u p v -> c b u (p v)").bitcast(F32)
            turned = psum.tile([P, 2, C], F32, name=f"turned{e}", tag=bank)
            for b in range(2):
                for u in range(2):
                    nc.tensor.transpose(turned[:, u, P * b : P * b + P], hs_words[:, b, u, :], ident[:])
            nc.scalar.copy(hg_words, turned[:].rearrange("p u r -> p r u"))

        def quantise_h(lo):
            hi = group_of(lo)[1]
            codes = tile(f"hq{lo}", [P, (hi - lo) * C], U32)
            scales = tile(f"hqs{lo}", [P, (hi - lo) * C], U8)
            nc.vector.quantize_mx(out=codes[:].bitcast(FP8X4), scales=scales[:], in_=hg[lo][:].rearrange("p c t -> p (c t)"))
            for e in range(lo, hi):
                hq[e] = codes[:, C * (e - lo) : C * (e - lo + 1)]
                hqs[e] = scales[:, C * (e - lo) : C * (e - lo + 1)]

        def second(lo, hi, bank):
            y = psum.tile([P, (hi - lo) * C], F32, name=f"y{lo}", tag=bank)
            for e in range(lo, hi):
                nc.tensor.matmul_mx(
                    out=y[:, C * (e - lo) : C * (e - lo + 1)],
                    lhsT=w2w[:, e, :].bitcast(FP4X4),
                    lhsT_scale=w2s[:, e, :],
                    rhs=hq[e].bitcast(FP8X4),
                    rhs_scale=hqs[e],
                    start=True,
                    stop=True,
                )
                ys[e] = y, lo

        def times_gate(lo, hi):
            y, first_expert = ys[lo]
            gate_lo = max(at for at in gates if at <= lo)
            nc.vector.tensor_tensor(
                gated(C * lo, C * hi),
                y[:, C * (lo - first_expert) : C * (hi - first_expert)],
                gates[gate_lo][:, C * (lo - gate_lo) : C * (hi - gate_lo)],
                MULT,
            )

        def scatter_on_vector(n):
            lo, hi = VECTOR_SCATTERS[n]
            nc.vector.tensor_copy(vector_window[:].indirect(dst_t[:, lo // 16 : hi // 16]), gated(lo, hi))

        def scatter_on_scalar(n):
            lo, hi = SCALAR_SCATTERS[n]
            nc.scalar.activation(scalar_window[:].indirect(dst_t[:, lo // 16 : hi // 16]), gated(lo, hi), COPY)

        for e in range(2):
            for b in range(2):
                product(e, b, 0)
        gated_tiles[0] = tile("gated0", [P, T], F32, "raw1_0")
        for e in range(E):
            first(e, 0)
            if e == 4:
                second(0, 1, "lower1")
                times_gate(0, 1)
            if e == 6:
                second(1, 3, "lower2")
                times_gate(1, 3)
            if e >= 2:
                turn(e - 2, f"lower{(e - 1) % 3}" if e == 3 else f"turn{e % 2}")
                quantise_h(e - 2)
            if e in (4, 6):
                scatter_on_vector(e // 2 - 2)
            first(e, 1)
        second(3, 5, "upper2")
        times_gate(3, 5)
        quantise_h(E - 2)
        second(5, 6, "lower0")
        times_gate(5, 6)
        second(6, 8, "upper0")
        times_gate(6, 8)
        scatter_on_vector(2)
        for n in range(len(SCALAR_SCATTERS)):
            scatter_on_scalar(n)

        start = 0
        for n, width in enumerate(STORES):
            cols = slice(start, start + width)
            result = tile(f"result{start}", [P, width], F32, f"raw1_{n + 1}")
            nc.vector.tensor_tensor(result[:], vector_window[:, cols], scalar_window[:, cols], ADD)
            nc.sync.dma_start(out=out[:, cols], in_=result[:])
            start += width
